import numpy as np, ml_dtypes
CORES = [40,41,42,43,44,45,46,47]
N = 8
BF = ml_dtypes.bfloat16
W, K, E, TH, ST, RO = 8192, 512, 16, 8, 3, 3
def subset(rng, cnt):
    a = 2 * rng.integers(0, 8, cnt.shape) + 1; o = rng.integers(0, 16, cnt.shape)
    return (((a * np.arange(16)[:, None] + o) & 15) < cnt).astype(np.int16)
def parts(rng):
    x = rng.integers(0, 256, (N, 8, 1, W), dtype=np.int16) + rng.integers(-12, 13, (N, 8, 16, W), dtype=np.int16)
    x = np.where(rng.random((N, 8, 1, W)) < 0.125, rng.integers(0, 256, (N, 8, 16, W), dtype=np.int16), np.clip(x, 0, 255))
    stk = rng.integers(0, W, (N, 8, 16, K)); bas = rng.integers(0, W, (N, 8, 16, K)); con = rng.integers(0, W, (N, 8, 16, K)); ln = rng.integers(1, 16, (N, 8, K))
    lv = (255.0 * (1.0 - rng.random((N, 8, 1, K)) ** 2)).astype(np.int64)
    z = np.clip(lv + rng.integers(-12, 13, (N, 8, 16, K)), 0, 255); w = rng.integers(1, 258, (N, 8, 16, 1))
    return x, stk, bas, con, ln, z, w
def pack(x, stk, bas, con, ln, z, w):
    def t(a, n): return np.ascontiguousarray(np.reshape(a, (N, 128, n)))
    return {"xt": t(x, W).astype(np.float32).astype(BF), "stk": t(stk, K).astype(np.int32), "bas": t(bas, K).astype(np.int32), "con": t(con, K).astype(np.int32),
            "ln": np.ascontiguousarray(ln).astype(np.int32), "z": t(z, K).astype(np.float32).astype(BF), "w": t(w, 1).astype(np.int32)}
def setup_inputs(rng):
    return pack(*parts(rng))
def setup_inputs_spread(rng):
    x, stk, bas, con, ln, z, w = parts(rng)
    x = (np.exp2(8.0 * rng.random((N, 8, 1, W), dtype=np.float32)) * rng.random((N, 8, 16, W), dtype=np.float32)).astype(np.int16)
    x = np.minimum(x, 255) * (rng.random((N, 8, 1, W)) > 0.0625)
    z = np.minimum((np.exp2(8.0 * rng.random((N, 8, 1, K))) * rng.random((N, 8, 16, K))).astype(np.int64), 255)
    def skew(lo, n, shape):
        e = rng.choice(np.array([0.25, 1.0, 4.0]), (N, 8) + (1,) * (len(shape) - 2))
        return np.minimum(lo + (n * rng.random(shape) ** e).astype(np.int64), lo + n - 1)
    stk = skew(0, W, (N, 8, 16, K)); bas = skew(0, W, (N, 8, 16, K)); con = skew(0, W, (N, 8, 16, K)); ln = skew(1, 15, (N, 8, K))
    w = np.minimum(np.exp2(8.01 * rng.random((N, 8, 16, 1))).astype(np.int64), 257)
    return pack(x, stk, bas, con, ln, z, w)
def endnames(rng):
    a = (W - 1) * rng.integers(0, 2, (N, 8, 16, K))
    s = (W - 1) * ((np.arange(16)[:, None] >= rng.integers(0, 17, (N, 8, 1, K))).astype(np.int64) ^ rng.integers(0, 2, (N, 8, 1, K)))
    ty = rng.random((N, 8, 1, K))
    return np.where(ty < 0.4, a, np.where(ty < 0.75, s, rng.integers(0, W, (N, 8, 16, K))))
def setup_inputs_ends(rng):
    cnt = rng.choice(np.array([0, 1, TH - 2, TH - 1, TH, 12, 16]), (N, 8, 1, W)); cnt[1] = np.minimum(cnt[1], TH - 2)
    x = 255 * subset(rng, cnt)
    zc = rng.choice(np.array([0, 1, 3, TH - 1, TH, 12]), (N, 8, 1, K)); zc[0] = rng.choice(np.array([TH, 12, 15]), (8, 1, K)); zc[1] = 1
    z = 255 * (1 - subset(rng, zc)); stk = endnames(rng); bas = endnames(rng); con = endnames(rng)
    for k in (0, K // 2, K - 1): z[1, 0, :, k] = 0
    ln = 1 + 14 * rng.integers(0, 2, (N, 8, K)); w = 1 + 256 * rng.integers(0, 2, (N, 8, 16, 1)); q = N - 1
    w[q, 7] = 257; w[q, 0] = 1; w[q, 6, 0] = 257; x[q, 6:8, :, 0] = 0; x[q, 7, :, W - 1] = 255; x[q, 6, :, W - 1] = 0; x[q, 6, 0, W - 1] = 255
    for k in (0, K - 1): stk[q, 7, :, k] = 0; stk[q, 7, 15, k] = W - 1
    for k in (1, K - 2): stk[q, 7, :, k] = W - 1
    for k in (2, K - 3): stk[q, 7, :, k] = 0; stk[q, 7, 0, k] = W - 1
    for k in (0, 1, 2, K - 3, K - 2, K - 1): z[q, 7, :, k] = 255
    for k in (2, K - 1): stk[q, 6, :, k] = W - 1; z[q, 6, :12, k] = 0; z[q, 6, 12:, k] = 255
    return pack(x, stk, bas, con, ln, z, w)
def setup_inputs_corners(rng):
    x, stk, bas, con, ln, z, w = parts(rng)
    cnt = rng.choice(np.array([0, TH - 1, TH, 16]), (N, 8, 1, W))
    over = rng.integers(0, 2, (N, 8, 1, W), dtype=np.int16) * rng.integers(0, 56, (N, 8, 16, W), dtype=np.int16)
    x = np.where(subset(rng, cnt) > 0, 200 + over, rng.integers(0, 200, (N, 8, 16, W), dtype=np.int16))
    z[:] = np.where(rng.random((N, 8, 1, K)) < 0.125, 201, 200); i = np.arange(16)[:, None]
    for q in range(N):
        for g in range(8):
            hot = np.flatnonzero(cnt[q, g, 0] >= TH); cold = np.flatnonzero(cnt[q, g, 0] < TH)
            row = rng.integers(1, 17, K); row[0] = 1; row[1] = 16; row[2] = 14; row[K - 1] = 15; row[K - 2] = 16
            hn = hot[rng.integers(0, len(hot), (16, K))]; cn = cold[rng.integers(0, len(cold), (16, K))]
            stk[q, g] = np.where(i == row, hn, np.where(i > row, stk[q, g], np.where((i == 0) & (rng.random((1, K)) < 0.5), hn, cn)))
    ln = rng.choice(np.array([1, 2, 14, 15]), (N, 8, K))
    for q in range(N): ln[q, q % 8] = 15; ln[q, (q + 1) % 8] = 1
    four = np.arange(K) % 4; stk[:, 3] = stk[:, 3][..., four]; z[:, 3] = z[:, 3][..., four]
    bas[:, 4] = (W - 1) * rng.integers(0, 2, (N, 16, K)); con[:, 2] = (W - 1) * rng.integers(0, 2, (N, 16, K))
    stk[:, 5] = stk[:, 5, :1].copy(); stk[:, 6] = E * np.arange(K) + rng.integers(0, E, (N, 16, K)); bas[:, 6] = E * np.arange(K) + rng.integers(0, E, (N, 16, K))
    w[0] = 1; w[N - 1] = 257
    return pack(x, stk, bas, con, ln, z, w)
def setup_inputs_long(rng):
    x, stk, bas, con, ln, z, w = parts(rng)
    x = np.where(rng.random((N, 8, 1, W)) < 0.06, rng.integers(250, 254, (N, 8, 16, W), dtype=np.int16), np.minimum(x, 249))
    ty = rng.random((N, 8, 1, K)); z = np.where(ty < 0.4, 250, np.where(ty < 0.8, 254, z)); ln = np.maximum(ln, rng.integers(1, 16, (N, 8, K)))
    return pack(x, stk, bas, con, ln, z, w)
def setup_inputs_alike(rng):
    x, stk, bas, con, ln, z, w = parts(rng); ga, gb, gc = [int(g) for g in rng.permutation(8)[:3]]; o = int(rng.integers(0, N))
    for a in (stk, bas, con):
        a[:, gb] = np.where(rng.random((N, 16, K)) < 0.5, E * rng.integers(K - 16, K, (N, 16, K)) + E - 1, a[:, gb])
    w[:, gb] = E * rng.integers(1, 256 // E + 1, (N, 16, 1)); w[:, gb, 0] = 1 + 256 * rng.integers(0, 2, (N, 1))
    for i in range(N):
        q = (o + i * ST) % N; lo, hi = ((32, 63), (96, 127), (192, 254), (96, 127), (0, 255))[min(i, 4)]
        if i < 4:
            x[q] = rng.integers(lo, hi + 1, (8, 16, W)); z[q] = 255 if i == 1 else 0
        if i == 2:
            m = np.zeros(8 * K, dtype=bool); m[rng.permutation(8 * K)[:K * int(rng.integers(0, 8)) + int(rng.integers(1, K))]] = True
            z[q] = np.where(m.reshape(8, 1, K), 255, 0)
        for g, v in ((ga, int(rng.integers(1, 4))), (gc, 0)):
            one = rng.integers(lo, hi - 2, 16); one[15] += (v - int(np.sum(one))) % 4
            x[q, g] = one[:, None]
        x[q, gb, 0] = (hi + 1) // E * E - 1
    return pack(x, stk, bas, con, ln, z, w)
def check_inputs(d):
    bad = []
    for k, lo, hi in (("xt", 0, 255), ("stk", 0, W - 1), ("bas", 0, W - 1), ("con", 0, W - 1), ("ln", 1, 15), ("z", 0, 255), ("w", 1, 257)):
        v = np.asarray(d[k]).astype(np.float32)
        if not (np.min(v) >= lo and np.max(v) <= hi and np.all(v == np.floor(v))): bad.append("range of " + k)
    return bad
def reference(xt, stk, bas, con, ln, z, w):
    X = xt.astype(np.float32).astype(np.int32).reshape(N, 8, 16, W); Z = z.astype(np.float32).astype(np.int64).reshape(N, 8, 16, K); wt = w.astype(np.int64).reshape(N, 8, 16, 1)
    S = stk.astype(np.int64).reshape(N, 8, 16, K); B = bas.astype(np.int64).reshape(N, 8, 16, K); C = con.astype(np.int64).reshape(N, 8, 16, K); n = ln.astype(np.int64).reshape(N, 8, K)
    A = [0] * N; p = np.arange(16)[None, :, None]
    for t in range(RO):
        for q in range(N):
            b = (q - t * ST) % N
            s, zz = S[b].copy(), Z[b].copy()
            R = np.take_along_axis(X[q], s.reshape(8, 1, 16 * K), 2).reshape(8, 16, 16, K).astype(np.int64)
            votes = np.add.reduce((R >= zz[:, :, None, :]).astype(np.int64), axis=1)
            hit = votes >= TH; hit[:, 0] = False
            found = np.maximum.accumulate(hit.astype(np.int64), axis=1)
            handled = found[:, 15] == 1; h = 16 - np.add.reduce(found, axis=1)
            M = np.max(np.where(found[:, None] == 1, 0, R), axis=2)
            u = np.add.reduce(wt[q] * M, axis=1) & 4095
            xh = np.take_along_axis(R, np.minimum(h, 15)[:, None, None, :], 2)[:, :, 0]
            v = np.add.reduce(xh, axis=1) & 3
            j = (((u * u) >> 5) + u + A[q]) & (K - 1)
            paste = handled & (v > 0)
            m = np.where(paste, np.take_along_axis(n[q], j, 1), 0)
            src = p + (np.where(paste, h + 1, h) - m)[:, None, :]
            low = np.take_along_axis(s, np.clip(src, 0, 15), 1); piece = np.take_along_axis(C[q], j[:, None, :], 2)
            new = np.where(p < m[:, None, :], piece, np.where(src <= 15, low, B[b]))
            S[b] = np.where(handled[:, None, :], new, s)
            Z[b] = np.where(handled[:, None, :], np.abs(xh - zz), M)
            C[q] = np.where(paste[:, None, :] & (p < h[:, None, :]), s, C[q])
            n[q] = np.where(paste, h, n[q])
            A[q] = int(np.sum(np.where(handled, 0, 1)))
            if t < RO - 1:
                col = (E * np.arange(K) + (u & (E - 1)))[:, None, :]
                np.put_along_axis(X[q], col, ((np.take_along_axis(X[q], col, 2) + M) >> 1).astype(np.int32), 2)
    last = [(q - (RO - 1) * ST) % N for q in range(N)]
    return {"ys": S[last].reshape(N, 128, K).astype(np.float32), "yc": C.reshape(N, 128, K).astype(np.float32), "yn": n.astype(np.float32), "yz": Z[last].reshape(N, 128, K).astype(np.float32).astype(BF)}

@@ -1,0 +1,446 @@
+from concourse.mybir import AluOpType, AxisListType, ActivationFunctionType
+
+ROUNDS, STEP, K, NREC = 3, 3, 512, 8192
+EDGES = [0, 64, 192, 320, 448, 512]
+CHUNKS = list(zip(EDGES[:-1], EDGES[1:]))
+HALVES = [(0, 256), (256, 512)]
+LATER = 2
+NP = 1 << 20
+TOP = 1 << 22
+WHOLE = 12582912.0
+
+SCRATCH = {
+    "X": ("sbuf", [128, NREC], "bfloat16"),
+    "RB": ("sbuf", [128, NREC + 32], "bfloat16"),
+    "PM": ("sbuf", [128, NREC], "bfloat16"),
+    "GE": ("sbuf", [128, 32, 256], "bfloat16"),
+    "Y": ("sbuf", [128, 16 * K], "int32"),
+    "D": ("dram", [8, 32, K], "int32"),
+    "STK": ("sbuf", [128, K], "int32"), "CON": ("sbuf", [128, K], "int32"),
+    "LN8": ("sbuf", [128, K], "int32"), "LNB": ("sbuf", [128, K], "bfloat16"), "LX": ("sbuf", [128, K], "float32"),
+    "WI": ("sbuf", [128, 1], "int32"), "WF": ("sbuf", [128, 1], "float32"),
+    "CM0": ("sbuf", [128, 1040], "float32"), "CM1": ("sbuf", [128, 1040], "float32"),
+    "LW0": ("sbuf", [128, 560], "bfloat16"), "LW1": ("sbuf", [128, 560], "bfloat16"),
+    "CF0": ("sbuf", [128, K], "float32"), "CF1": ("sbuf", [128, K], "float32"), "CFI": ("sbuf", [128, K], "int32"),
+    "ZM": ("sbuf", [128, 2 * K], "bfloat16"), "AG": ("sbuf", [128, K], "bfloat16"),
+    "OX": ("sbuf", [128, K], "bfloat16"), "NF": ("sbuf", [128, K], "float32"), "NB": ("sbuf", [128, K], "bfloat16"),
+    "T1": ("sbuf", [128, K], "bfloat16"), "OA": ("sbuf", [128, K], "float32"),
+    "LG": ("sbuf", [128, K], "bfloat16"),
+    "BE": ("sbuf", [128, K], "float32"), "PB": ("sbuf", [128, K], "float32"), "TY": ("sbuf", [128, K], "int32"),
+    "SN": ("sbuf", [128, K], "int32"), "FO": ("sbuf", [128, K], "float32"), "FC": ("sbuf", [128, K], "float32"),
+    "FI": ("sbuf", [128, K], "int32"), "FN": ("sbuf", [128, K], "float32"),
+    "E": ("sbuf", [128, 128], "float32"), "ONE": ("sbuf", [128, 128], "float32"),
+    "KC": ("sbuf", [128, 1], "float32"),
+    "RC": ("sbuf", [128, 1], "float32"), "IC": ("sbuf", [128, 1], "float32"),
+    "TA": ("sbuf", [128, 128], "float32"), "TB": ("sbuf", [128, 32], "float32"),
+    "TC": ("sbuf", [128, 128], "float32"), "TD": ("sbuf", [128, 128], "float32"),
+    "ID": ("sbuf", [128, 128], "bfloat16"), "ND": ("sbuf", [128, 128], "bfloat16"), "HI": ("sbuf", [128, 128], "bfloat16"),
+    "HQ": ("sbuf", [128, 128], "bfloat16"), "ONB": ("sbuf", [128, K], "bfloat16"),
+    "BQ": ("sbuf", [128, 144], "bfloat16"), "BW": ("sbuf", [128, 144], "float16"),
+    "GA": ("sbuf", [128, 128], "bfloat16"), "MK": ("sbuf", [128, 2048], "bfloat16"),
+    "D1A": ("sbuf", [128, K], "float32"),
+    "KW": ("sbuf", [128, 32], "float32"), "K16": ("sbuf", [128, 32], "float32"), "KH": ("sbuf", [128, 32], "float32"),
+    "K5": ("sbuf", [128, 32], "float32"), "KI": ("sbuf", [128, 32], "float32"),
+    "LB": ("sbuf", [128, 64], "float32"), "L2": ("sbuf", [128, 192], "float32"), "L2S": ("sbuf", [128, 192], "float32"),
+    "L2T": ("sbuf", [128, 192], "float32"),
+    "ACOL": ("sbuf", [128, 1], "float32"), "RED": ("sbuf", [128, 1], "float32"),
+}
+BANKS = ["ZP", "UU", "VV", "PX", "VT0", "VT1", "DF0", "DF1"]
+for _n in BANKS:
+    SCRATCH[_n] = ("psum", [128, K], "float32")
+for _t in range(3):
+    SCRATCH["SU%d" % _t] = ("sbuf", [128, K], "uint16")
+    SCRATCH["SE%d" % _t] = ("sbuf", [128, K], "int32")
+    SCRATCH["Z%d" % _t] = ("sbuf", [128, K], "bfloat16")
+    SCRATCH["BA%d" % _t] = ("sbuf", [128, K], "int32")
+    SCRATCH["ZO%d" % _t] = ("sbuf", [128, K], "bfloat16")
+    if _t < 2:
+        SCRATCH["UO%d" % _t] = ("sbuf", [128, K], "uint16")
+        SCRATCH["EO%d" % _t] = ("sbuf", [128, K], "int32")
+WF32 = ["h", "un", "u20", "zq", "zl", "h5", "h1k", "np0", "np", "w0", "w1", "n32", "hl", "p5", "cl", "pz", "h528", "lp", "ll"]
+WI32 = ["vi", "v", "ui", "u", "u2", "q", "j0", "j", "d", "dd", "x15", "xk"]
+WU16 = ["MLu", "zlu", "jlu", "hlu", "ylu", "xlu", "clu", "llu", "huu"]
+SCRATCH["FW"] = ("sbuf", [128, 32 * len(WF32)], "float32")
+SCRATCH["IW"] = ("sbuf", [128, 32 * len(WI32)], "int32")
+SCRATCH["LU"] = ("sbuf", [128, 32 * len(WU16)], "uint16")
+TILE = {}
+for _i, _n in enumerate(WF32): TILE["f_" + _n] = ("FW", 32 * _i)
+for _i, _n in enumerate(WI32): TILE["i_" + _n] = ("IW", 32 * _i)
+for _i, _n in enumerate(WU16): TILE[_n] = ("LU", 32 * _i)
+
+LOADS = ["STK", "X", "Z0", "WI", "LN8", "BA0", "CON"]
+ARR = ["SU1a", "SU1b", "SU2a", "SU2b", "SE1", "SE2", "Z1", "Z2", "BA1", "BA2"]
+SEMAPHORES = (["sV", "sA", "sP", "sG", "local", "dD", "dY", "oS", "oZ", "oC", "oN"]
+              + ["ld" + n for n in LOADS] + ["ar" + n for n in ARR])
+
+
+def rank_program(g, core, T, topo):
+    rank = T.rank_of(core)
+    if rank is None:
+        return
+    op = AluOpType
+    act = ActivationFunctionType
+    queue = {"V": g.vector, "A": g.scalar, "P": g.tensor, "G": g, "S": g.sync}
+    total = {s: 0 for s in SEMAPHORES}
+    seen = {q: {} for q in queue}
+    snap = {}
+    hist = {}
+
+    def learn(q, sem, cnt):
+        if seen[q].get(sem, 0) < cnt: seen[q][sem] = cnt
+        for s, n in snap.get((sem, cnt), {}).items():
+            if seen[q].get(s, 0) < n: seen[q][s] = n
+
+    def await_deps(q, reads, writes, own_waw):
+        need = {}
+        for lst, isw in ((reads, False), (writes, True)):
+            for name, lo, hi in lst:
+                ps = name in BANKS
+                for l, h, w, oq, sem, cnt in hist.get(name, []):
+                    if not ps and (h <= lo or hi <= l): continue
+                    if oq == q:
+                        if not (w and (not isw or own_waw)): continue
+                    elif not (isw or w or ps): continue
+                    if seen[q].get(sem, 0) >= cnt: continue
+                    if sem[0] in "ldo": cnt = total[sem]
+                    if need.get(sem, 0) < cnt: need[sem] = cnt
+        for sem in sorted(need, key=lambda s: -need[s]):
+            if seen[q].get(sem, 0) < need[sem]:
+                queue[q].wait_ge(T.sem[sem], need[sem])
+                learn(q, sem, need[sem])
+
+    def note(oq, q, reads, writes, sem, cnt):
+        snap[(sem, cnt)] = dict(seen[q]) if q else {}
+        for name, lo, hi in writes:
+            old = [e for e in hist.get(name, []) if not (lo <= e[0] and e[1] <= hi)]
+            hist[name] = old + [(lo, hi, True, oq, sem, cnt)]
+        for name, lo, hi in reads:
+            old = [e for e in hist.get(name, []) if not (not e[2] and e[3] == oq and lo <= e[0] and e[1] <= hi)]
+            hist[name] = old + [(lo, hi, False, oq, sem, cnt)]
+
+    def run(q, fn, out, ins, own_waw=False):
+        reads = [x for i in ins for x in i[1]]
+        writes = list(out[1])
+        for x in out[2:]: reads += x
+        await_deps(q, reads, writes, own_waw)
+        sem = "s" + q
+        total[sem] += 1
+        fn().then_inc(T.sem[sem], 1)
+        note(q, q, reads, writes, sem, total[sem])
+
+    def dma(q, out, in_, sem, last=True):
+        await_deps(q, in_[1], out[1], True)
+        total[sem] += 16
+        queue[q].dma_start(out[0], in_[0]).then_inc(T.sem[sem], 16)
+        note("dma" + sem, q, in_[1], out[1], sem, total[sem])
+
+    def b(name, lo=0, hi=None, step=1, p0=0, p1=128):
+        if name in TILE:
+            name, o = TILE[name]
+            lo, hi = o + lo, o + (32 if hi is None else hi)
+        hi = SCRATCH[name][1][-1] if hi is None else hi
+        ap = T[name][p0:p1, lo:hi] if step == 1 else T[name][p0:p1, lo:hi:step]
+        return (ap, [(name, lo, hi)])
+
+    def ind(name, lo, hi, lst, c0=0, c1=32):
+        lst, o = TILE.get(lst, (lst, 0))
+        return (T[name][:, lo:hi].indirect(T[lst][:, o + c0:o + c1]), [(name, lo, hi), (lst, o + c0, o + c1)])
+
+    def tt(out, a, c, o):
+        run("V", lambda: g.vector.tensor_tensor(out[0], a[0], c[0], o), out, [a, c])
+
+    def ts(out, a, s1, o1, s2=None, o2=None, waw=False):
+        ins = [a] + ([s1] if isinstance(s1, tuple) else [])
+        v1 = s1[0] if isinstance(s1, tuple) else s1
+        if o2 is None:
+            run("V", lambda: g.vector.tensor_scalar(out[0], a[0], v1, None, o1), out, ins, waw)
+        else:
+            run("V", lambda: g.vector.tensor_scalar(out[0], a[0], v1, s2, o1, o2), out, ins, waw)
+
+    def cp(out, a, waw=False):
+        run("V", lambda: g.vector.tensor_copy(out[0], a[0]), out, [a], waw)
+
+    def scan(out, a, c, o1, o2):
+        run("V", lambda: g.vector.tensor_tensor_scan(out[0], a[0], c[0], 0.0, o1, o2), out, [a, c])
+
+    def fill(out, v, waw=False):
+        run("V", lambda: g.vector.memset(out[0], v), out, [], waw)
+
+    def ac(out, a, func=act.Copy, **kw):
+        run("A", lambda: g.scalar.activation(out[0], a[0], func, **kw), out, [a])
+
+    def mm(out, l, r, start, stop):
+        run("P", lambda: g.tensor.matmul(out[0], l[0], r[0], start, stop), out, [l, r])
+
+    def iota(out, pattern, base, cm):
+        run("G", lambda: g.iota(out[0], pattern, base, cm, allow_small_or_imprecise_dtypes=True), out, [])
+
+    def select(out, a, pattern, cmp, fillv, base, cm):
+        run("G", lambda: g.affine_select(out[0], a[0], pattern, cmp, fillv, base, cm), out, [a])
+
+    def send(src, dst_name, lo, hi, dst, part=""):
+        await_deps("G", src[1], [], False)
+        rid, pid, _se = topo.addr(dst)
+        m = topo.mask(core, dst)
+        n = len(topo.engines(core, dst))
+        g.remote_dma(T[dst_name][:, lo:hi], src[0], T.sem["ar" + dst_name + part], T.sem["local"], pid, rid, m)
+        total["local"] += n
+
+    def arrives(name, lo, hi, src, part=""):
+        n = len(topo.engines(src, core))
+        total["ar" + name + part] += n
+        note("remote", None, [], [(name, lo, hi)], "ar" + name + part, n)
+
+    nxt = T.cores[(rank + STEP) % len(T.cores)]
+    nxt2 = T.cores[(rank + 2 * STEP) % len(T.cores)]
+    prv = T.cores[(rank - STEP) % len(T.cores)]
+    prv2 = T.cores[(rank - 2 * STEP) % len(T.cores)]
+    for t in (1, 2):
+        for part, (l0, l1) in zip("ab", HALVES): arrives("SU%d" % t, l0, l1, prv, part)
+        arrives("SE%d" % t, 0, K, prv)
+        arrives("Z%d" % t, 0, K, prv)
+    arrives("BA1", 0, K, prv)
+    arrives("BA2", 0, K, prv2)
+
+    dma("S", b("STK"), (T.stk[:, :], []), "ldSTK")
+    dma("S", b("X"), (T.xt[:, :], []), "ldX")
+    dma("A", b("LN8", p1=8), (T.ln[:, :], []), "ldLN8")
+    dma("A", b("WI"), (T.w[:, :], []), "ldWI")
+    dma("A", b("Z0", 0, K), (T.z[:, :], []), "ldZ0")
+    dma("A", b("CON"), (T.con[:, :], []), "ldCON")
+    dma("A", b("BA0"), (T.bas[:, :], []), "ldBA0")
+
+    fill(b("ONE"), 1.0)
+    iota(b("KC", p1=16), [[0, 1]], 0, 1)
+    select(b("E", p1=16), b("ONE", p1=16), [[0, 8], [-1, 16]], op.is_equal, 0.0, 0, 1)
+    mm(b("UU", 0, 1), b("E", p1=16), b("KC", p1=16), True, True)
+    for t in range(3): fill(b("L2S", 64 * t, 64 * t + 64, p1=16), float(TOP + (t + 1) * NP))
+    iota(b("KI"), [[16, 32]], 0, 0)
+    select(b("TA"), b("ONE"), [[-1, 128]], op.is_equal, 0.0, 0, 1)
+    select(b("TB", 0, 9), b("ONE", 0, 9), [[-16, 9]], op.is_ge, 0.0, 0, 1)
+    select(b("TB", 16, 25), b("TB", 0, 9), [[16, 9]], op.is_ge, 0.0, 15, -1)
+    select(b("TC", p1=8), b("ONE", p1=8), [[1, 128]], op.is_ge, 0.0, 0, -16)
+    select(b("TD", p1=8), b("TC", p1=8), [[-1, 128]], op.is_ge, 0.0, 15, 16)
+    for t in range(3):
+        select(b("L2T", 64 * t, 64 * t + 64, p1=16), b("L2S", 64 * t, 64 * t + 64, p1=16), [[1, 64]], op.is_ge, -float(TOP), -1, -1)
+    iota(b("LB", 0, 32), [[16384, 32]], 8192, 0)
+    iota(b("LB", 32, 64), [[16384, 32]], -8192, 0)
+    for n in ("LW0", "LW1"): iota(b(n, 528, 560), [[32, 32]], 0, 0)
+    fill(b("BQ"), 0.0)
+    fill(b("D1A"), -1.0)
+    cp(b("RC"), b("UU", 0, 1))
+    fill(b("RB", 8192, 8224), 0.0)
+    ts(b("IC"), b("RC"), 16384.0, op.mult)
+    ts(b("SE0"), b("STK"), b("IC"), op.add)
+    cp(b("SU0"), b("STK"))
+    cp(b("ID"), b("TA"))
+    fill((T.GE[:, :, 0:256:16], [("GE0", 0, K)]), 1.0)
+
+    def rotations(t):
+        se = b("SE%d" % t)
+        for half in (0, 1):
+            dma("S", (T.D[:, 16 * half:16 * half + 16, :], [("D", 16 * half, 16 * half + 16)]), se, "dD")
+        for q in range(16):
+            dma("S", (T.Y[q::16, :], [("Y", q * 100000, q * 100000 + 1)]), (T.D[:, q:q + 16, :], [("D", q, q + 16)]), "dY")
+
+    yall = [("Y", 0, 1600000)]
+    rotations(0)
+
+    ts(b("ND"), b("TA"), -1.0, op.mult)
+    ts(b("HI"), b("TA"), 0.5, op.mult)
+    ts(b("KW"), b("KI"), b("RC"), op.add)
+    cp(b("BQ", 15, 144, 16), b("TB", 16, 25), True)
+    ts(b("K16"), b("KW"), 16.0, op.mult)
+    ts(b("K5"), b("KW"), 512.0, op.add)
+    fill(b("D1A", 0, K, 16), 15.0, True)
+    for l0, l1 in CHUNKS:
+        c0, c1 = l0 // 16, l1 // 16
+        ts(b("KH", c0, c1), b("K16", c0, c1), float(-1 - 16 * l0), op.add)
+        ts(b("D1A", l0 + 15, l1, 16), b("K16", c0, c1), float(14 - 16 * l0), op.add, waw=True)
+    fill(b("MK"), 1.0)
+    fill(b("MK", 0, 2048, 16), 0.0, True)
+    for n in ("LW0", "LW1"): fill(b(n, 512, 528), 32.0)
+    for n in ("CM0", "CM1"): fill(b(n, 512, 528), -1.0)
+    fill(b("LB", 48, 64), -1048576.0, True)
+    fill(b("HQ"), -1.0 / 512.0)
+    fill(b("ONB"), 1.0)
+    cp(b("GA", p1=8), b("TD", p1=8))
+    cp(b("LNB", p1=8), b("LN8", p1=8))
+    mm(b("PX"), b("GA", p1=8), b("LNB", p1=8), True, True)
+    mm(b("VV", 0, 192), b("E", p1=16), b("L2T", p1=16), True, True)
+    mm(b("ZP"), b("ID"), b("Z0", 0, K), True, True)
+    cp(b("WF"), b("WI"))
+    ts(b("BW"), b("BQ"), b("WF"), op.mult)
+    cp(b("L2"), b("VV", 0, 192))
+    ts(b("LX"), b("PX"), b("RC"), op.is_gt, float(TOP), op.mult)
+
+    send(b("BA0"), "BA1", 0, K, nxt)
+    send(b("BA0"), "BA2", 0, K, nxt2)
+
+    NC = len(CHUNKS)
+    w = lambda n: b("f_" + n)
+    x = lambda n: b("i_" + n)
+    later = [lambda: ac(b("LW0", 0, K), b("PX"), scale=32.0),
+             lambda: tt(b("CM0", 0, K), b("LX"), b("CON"), op.add)]
+    for t in range(ROUNDS):
+        last = t == ROUNDS - 1
+        SU, SE, Z, BA = "SU%d" % t, "SE%d" % t, "Z%d" % t, "BA%d" % t
+        CMc, CMn = "CM%d" % (t % 2), "CM%d" % ((t + 1) % 2)
+        LWc, LWn = "LW%d" % (t % 2), "LW%d" % ((t + 1) % 2)
+        if t: rotations(t)
+        if t: mm(b("ZP"), b("ID"), b(Z, 0, K), True, True)
+
+        def records(ci):
+            l0, l1 = CHUNKS[ci]
+            ac(b("RB", 16 * l0 + 15, 16 * l1 + 15), ind("X", 0, NREC, SU, l0, l1))
+
+        def ge(l0, l1, i):
+            return (T.GE[:, l0 // 16:l1 // 16, i:256:16], [("GE%d" % i, l0, l1)])
+
+        def row(l0, l1, i):
+            a0, a1 = 16 * l0 + 15, 16 * l1 + 15
+            return (T.RB[:, a0 + i:a1:16], [("RB", a0, a1)])
+
+        def compare(ci):
+            l0, l1 = CHUNKS[ci]
+            for i in range(1, 16):
+                tt(ge(l0, l1, i), row(l0, l1, i), b("ZP", l0, l1), op.is_ge)
+            scan(b("PM", 16 * l0, 16 * l1), b("MK", 0, 16 * (l1 - l0)), b("RB", 16 * l0 + 15, 16 * l1 + 15), op.mult, op.max)
+
+        def votes(ci):
+            l0, l1 = CHUNKS[ci]
+            for r in range(16):
+                mm(b("VT%d" % (ci % 2), 0, l1 - l0), b("BQ", 15 - r, 143 - r),
+                   (T.GE[:, l0 // 16:l1 // 16, 16 * r:16 * r + 16], [("GE%d" % i, l0, l1) for i in range(16)]), r == 0, r == 15)
+
+        def handler(ci):
+            l0, l1 = CHUNKS[ci]
+            c0, c1 = l0 // 16, l1 // 16
+            ts(b("T1", l0, l1), b("VT%d" % (ci % 2), 0, l1 - l0), 7.5, op.is_lt, 32768.0, op.mult)
+            scan(b("OA", l0, l1), b("T1", l0, l1), b("D1A", l0, l1), op.min, op.add)
+            cp(b("MLu", c0, c1), b("OA", l0 + 15, l1, 16))
+
+        def taken(ci):
+            l0, l1 = CHUNKS[ci]
+            ac(b("ZM", K + l0, K + l1), ind("PM", 16 * l0, 16 * l1, "MLu", l0 // 16, l1 // 16))
+            ac(b("AG", l0, l1), ind("RB", 16 * l0 + 16, 16 * l1 + 16, "MLu", l0 // 16, l1 // 16))
+
+        def changes(ci):
+            l0, l1 = CHUNKS[ci]
+            mm(b("DF0", l0, l1), b("ID"), b("AG", l0, l1), True, False)
+            mm(b("DF0", l0, l1), b("ND"), b(Z, l0, l1), False, True)
+
+        records(0)
+        records(1)
+        for ci in range(NC):
+            compare(ci)
+            votes(ci)
+            if ci >= 2: changes(ci - 2)
+            if ci + 2 < NC: records(ci + 2)
+            if ci == 0 and t: cp(b("ACOL"), b("VV", 0, 1))
+            if ci == LATER:
+                for f in later: f()
+                later = []
+            if ci:
+                handler(ci - 1)
+                taken(ci - 1)
+        handler(NC - 1)
+        taken(NC - 1)
+        for r in range(16): mm(b("UU", 0, 32), b("BW", 15 - r, 143 - r), b("ZM", K + r, 2 * K, 16), r == 0, r == 15)
+        changes(NC - 2)
+        changes(NC - 1)
+        for r in range(16): mm(b("VV", 0, 32), b("BQ", 15 - r, 143 - r), b("AG", r, K, 16), r == 0, r == 15)
+
+        tt(w("h"), b("OA", 15, K, 16), b("KH"), op.subtract)
+        ts(w("zq"), w("h"), 16.0, op.is_ge, 512.0, op.mult)
+        ts(w("u20"), w("h"), 16.0, op.is_ge, float(NP), op.mult)
+        tt(w("zl"), w("zq"), b("KW"), op.add)
+        ts(w("h5"), w("h"), 512.0, op.mult)
+        cp(b("zlu"), w("zl"))
+        tt(w("h1k"), w("h5"), b("K5"), op.add)
+        ts(w("h528"), w("h"), 528.0, op.add)
+        cp(b("huu"), w("h"))
+        tt(b(CMc, 528, 1040), ind("L2", 64 * t, 64 * t + 64, "huu"), b(SE), op.add)
+        cp(x("ui"), b("UU", 0, 32))
+        ts(x("u"), x("ui"), 4095, op.bitwise_and)
+        tt(x("u2"), x("u"), x("u"), op.mult)
+        cp(x("vi"), b("VV", 0, 32))
+        ts(x("q"), x("u2"), 5, op.arith_shift_right)
+        ts(x("v"), x("vi"), 3, op.bitwise_and)
+        if t: ts(w("w0"), x("u"), b("ACOL"), op.add)
+        ts(w("np0"), x("v"), 0.0, op.is_equal, float(NP), op.mult)
+        if not last: ts(x("x15"), x("u"), 15, op.bitwise_and)
+        tt(w("np"), w("np0"), w("u20"), op.max)
+        if not last: tt(x("xk"), x("x15"), b("K16"), op.add)
+        tt(w("w1"), w("w0") if t else x("u"), w("np"), op.add)
+        ts(w("n32"), w("np"), 1.0 / 32768.0, op.mult)
+        tt(x("j0"), x("q"), w("w1"), op.add)
+        tt(w("hl"), w("n32"), w("h"), op.add)
+        ts(x("j"), x("j0"), NP + 511, op.bitwise_and)
+        cp(b("hlu"), w("hl"))
+        ts(b("jlu"), x("j"), 512.0, op.min)
+        if not last: cp(b("xlu"), x("xk"))
+        ac(b("ZM", 0, K), b("DF0"), act.Abs)
+        ac(b("ZO%d" % t), ind("ZM", 0, 2 * K, "zlu"))
+        ac(b("LG"), ind(LWc, 0, 528, "jlu"))
+        if not last:
+            mm(b("DF1"), b("HQ"), b("ONB"), True, False)
+            mm(b("DF1"), b("HI"), b("ZM", K, 2 * K), False, False)
+        for r in range(16): mm(b("PX", 0, 32), b("BQ", 15 - r, 143 - r), b("LG", r, K, 16), r == 0, r == 15)
+        if not last:
+            ac(b("OX"), ind("X", 0, NREC, "xlu"))
+            mm(b("DF1"), b("HI"), b("OX"), False, True)
+        tt(b("BE"), ind("LB", 0, 64, "hlu"), b(BA), op.add)
+        tt(b("PB"), ind(CMc, 0, 528, "jlu"), b("BE"), op.max)
+
+        def pieces():
+            ts(w("p5"), w("np"), 1.0, op.is_lt, 528.0, op.mult)
+            ts(w("pz"), w("np"), 1.0, op.is_lt)
+            tt(w("cl"), w("p5"), b("KW"), op.add)
+            tt(w("lp"), w("h528"), w("pz"), op.mult)
+            cp(b("clu"), w("cl"))
+            tt(w("ll"), w("lp"), b("KW"), op.max)
+            cp(b("llu"), w("ll"))
+            cf_old = b("CON") if t == 0 else b("CF%d" % ((t + 1) % 2))
+            tt(b("CFI") if last else b("CF%d" % (t % 2)), ind(CMc, 0, 1040, "clu"), cf_old, op.max)
+
+        if last: pieces()
+        tt(x("d"), w("h1k"), b("PX", 0, 32), op.subtract)
+        ts(x("dd"), x("d"), 8191, op.bitwise_and)
+        cp(b("ylu"), x("dd"))
+        if not last: send(b("ZO%d" % t), "Z%d" % (t + 1), 0, K, nxt)
+        if not last:
+            ac(b("NF"), b("DF1"), act.Identity, bias=WHOLE)
+            ac(b("NB"), b("NF"), act.Identity, bias=-WHOLE)
+        for half, (l0, l1) in enumerate(HALVES):
+            yi = ind("Y", 0, 16 * K, "ylu", l0 // 16, l1 // 16)
+            tt(b("TY", l0, l1), (yi[0], yall + yi[1][1:]), b("PB", l0, l1), op.max)
+            ts(b("SN", l0, l1), b("TY", l0, l1), 8191, op.bitwise_and)
+            if not last:
+                cp(b("UO%d" % t, l0, l1), b("SN", l0, l1))
+                send(b("UO%d" % t, l0, l1), "SU%d" % (t + 1), l0, l1, nxt, "ab"[half])
+                if half == 0:
+                    si = ind("X", 0, NREC, "xlu")
+                    cp((si[0], si[1][:1], si[1][1:]), b("NB"))
+        if not last:
+            ts(b("EO%d" % t), b("SN"), b("IC"), op.add)
+            send(b("EO%d" % t), "SE%d" % (t + 1), 0, K, nxt)
+            pieces()
+            later.append(lambda a=LWn, c=LWc: ac(b(a, 0, K), ind(c, 0, 560, "llu")))
+            later.append(lambda a=CMn, c=CMc: ac(b(a, 0, K), ind(c, 0, 1040, "clu")))
+            ts(w("un"), w("h"), 16.0, op.is_ge)
+            run("V", lambda: g.vector.tensor_reduce(T.RED[:, :], w("un")[0], AxisListType.X, op.add), b("RED"), [w("un")])
+            mm(b("VV", 0, 1), b("ONE"), b("RED"), True, True)
+        else:
+            cp(b("FO"), b("SN"))
+            dma("S", (T.ys[:, :], []), b("FO"), "oS")
+            dma("S", (T.yz[:, :], []), b("ZO%d" % t), "oZ")
+            ts(b("FI"), b("CFI"), 8191, op.bitwise_and)
+            cp(b("FC"), b("FI"))
+            dma("S", (T.yc[:, :], []), b("FC"), "oC")
+            ac(b(LWn, 0, K), ind(LWc, 0, 560, "llu"))
+            ac(b("FN"), b(LWn, 0, K), scale=1.0 / 32.0)
+            dma("S", (T.yn[:, :], []), (T.FN[0:128:16, :], [("FN", 0, K)]), "oN")
+
+    for s in SEMAPHORES:
+        if total[s]: g.wait_ge(T.sem[s], total[s])

@@ -1,76 +1,77 @@
 from concourse.mybir import AluOpType, AxisListType, ActivationFunctionType
 
 ROUNDS, STEP, K, NREC = 3, 3, 512, 8192
-EDGES = [0, 64, 192, 320, 448, 512]
+H = 256
+PARTS = [(0, H), (H, K)]
+EDGES = [0, 64, 160, 256, 352, 448, 512]
 CHUNKS = list(zip(EDGES[:-1], EDGES[1:]))
-HALVES = [(0, 256), (256, 512)]
-LATER = 2
-NP = 1 << 20
-TOP = 1 << 22
+SIGNS = [0, 0, 0, 0, 4, 4]
+VOTE = 4096.0
+FAR = 1 << 20
+DEAD = 16384
+BASE = 8192
+NOP = 1 << 26
+TOFF = 528
 WHOLE = 12582912.0
+YV = 3072
 
 SCRATCH = {
     "X": ("sbuf", [128, NREC], "bfloat16"),
     "RB": ("sbuf", [128, NREC + 32], "bfloat16"),
     "PM": ("sbuf", [128, NREC], "bfloat16"),
-    "GE": ("sbuf", [128, 32, 256], "bfloat16"),
-    "Y": ("sbuf", [128, 16 * K], "int32"),
-    "D": ("dram", [8, 32, K], "int32"),
-    "STK": ("sbuf", [128, K], "int32"), "CON": ("sbuf", [128, K], "int32"),
+    "GE": ("sbuf", [128, 32, 16, 16], "bfloat16"),
+    "Y0": ("sbuf", [128, 31 * H], "int32"), "Y1": ("sbuf", [128, 31 * H], "int32"),
+    "STK": ("sbuf", [128, K], "int32"), "CON": ("sbuf", [128, K], "int32"), "BAS": ("sbuf", [128, K], "int32"),
     "LN8": ("sbuf", [128, K], "int32"), "LNB": ("sbuf", [128, K], "bfloat16"), "LX": ("sbuf", [128, K], "float32"),
     "WI": ("sbuf", [128, 1], "int32"), "WF": ("sbuf", [128, 1], "float32"),
-    "CM0": ("sbuf", [128, 1040], "float32"), "CM1": ("sbuf", [128, 1040], "float32"),
-    "LW0": ("sbuf", [128, 560], "bfloat16"), "LW1": ("sbuf", [128, 560], "bfloat16"),
-    "CF0": ("sbuf", [128, K], "float32"), "CF1": ("sbuf", [128, K], "float32"), "CFI": ("sbuf", [128, K], "int32"),
-    "ZM": ("sbuf", [128, 2 * K], "bfloat16"), "AG": ("sbuf", [128, K], "bfloat16"),
-    "OX": ("sbuf", [128, K], "bfloat16"), "NF": ("sbuf", [128, K], "float32"), "NB": ("sbuf", [128, K], "bfloat16"),
-    "T1": ("sbuf", [128, K], "bfloat16"), "OA": ("sbuf", [128, K], "float32"),
-    "LG": ("sbuf", [128, K], "bfloat16"),
-    "BE": ("sbuf", [128, K], "float32"), "PB": ("sbuf", [128, K], "float32"), "TY": ("sbuf", [128, K], "int32"),
-    "SN": ("sbuf", [128, K], "int32"), "FO": ("sbuf", [128, K], "float32"), "FC": ("sbuf", [128, K], "float32"),
-    "FI": ("sbuf", [128, K], "int32"), "FN": ("sbuf", [128, K], "float32"),
+    "PW0": ("sbuf", [128, TOFF + K], "float32"), "PW1": ("sbuf", [128, TOFF + K], "float32"),
+    "ZM0": ("sbuf", [128, 2 * H], "bfloat16"), "ZM1": ("sbuf", [128, 2 * H], "bfloat16"),
+    "AG": ("sbuf", [128, K], "bfloat16"), "OA": ("sbuf", [128, K], "float32"),
+    "OX": ("sbuf", [128, H], "bfloat16"), "NF": ("sbuf", [128, H], "float32"), "NB": ("sbuf", [128, H], "bfloat16"),
+    "XS": ("sbuf", [128, H], "int32"), "XH": ("sbuf", [128, H], "int32"),
+    "PB": ("sbuf", [128, K], "float32"), "SG": ("sbuf", [128, K], "bfloat16"), "TY": ("sbuf", [128, K], "int32"),
+    "CI32": ("sbuf", [128, K], "int32"), "CN": ("sbuf", [128, K], "int32"), "SF": ("sbuf", [128, K], "bfloat16"),
+    "FO": ("sbuf", [128, K], "float32"), "FC": ("sbuf", [128, K], "float32"), "FN": ("sbuf", [128, K], "float32"),
     "E": ("sbuf", [128, 128], "float32"), "ONE": ("sbuf", [128, 128], "float32"),
-    "KC": ("sbuf", [128, 1], "float32"),
-    "RC": ("sbuf", [128, 1], "float32"), "IC": ("sbuf", [128, 1], "float32"),
-    "TA": ("sbuf", [128, 128], "float32"), "TB": ("sbuf", [128, 32], "float32"),
+    "KC": ("sbuf", [128, 1], "float32"), "RC": ("sbuf", [128, 1], "float32"), "R16": ("sbuf", [128, 1], "float32"),
+    "TA": ("sbuf", [128, 128], "float32"), "TB": ("sbuf", [128, 32], "float32"), "GB": ("sbuf", [128, 8], "bfloat16"),
     "TC": ("sbuf", [128, 128], "float32"), "TD": ("sbuf", [128, 128], "float32"),
-    "ID": ("sbuf", [128, 128], "bfloat16"), "ND": ("sbuf", [128, 128], "bfloat16"), "HI": ("sbuf", [128, 128], "bfloat16"),
-    "HQ": ("sbuf", [128, 128], "bfloat16"), "ONB": ("sbuf", [128, K], "bfloat16"),
-    "BQ": ("sbuf", [128, 144], "bfloat16"), "BW": ("sbuf", [128, 144], "float16"),
-    "GA": ("sbuf", [128, 128], "bfloat16"), "MK": ("sbuf", [128, 2048], "bfloat16"),
-    "D1A": ("sbuf", [128, K], "float32"),
-    "KW": ("sbuf", [128, 32], "float32"), "K16": ("sbuf", [128, 32], "float32"), "KH": ("sbuf", [128, 32], "float32"),
-    "K5": ("sbuf", [128, 32], "float32"), "KI": ("sbuf", [128, 32], "float32"),
-    "LB": ("sbuf", [128, 64], "float32"), "L2": ("sbuf", [128, 192], "float32"), "L2S": ("sbuf", [128, 192], "float32"),
-    "L2T": ("sbuf", [128, 192], "float32"),
-    "ACOL": ("sbuf", [128, 1], "float32"), "RED": ("sbuf", [128, 1], "float32"),
+    "ID": ("sbuf", [128, 128], "bfloat16"), "ND": ("sbuf", [128, 128], "bfloat16"), "I16": ("sbuf", [128, 128], "bfloat16"),
+    "I32": ("sbuf", [128, 128], "bfloat16"), "I256": ("sbuf", [128, 128], "bfloat16"), "IT": ("sbuf", [128, 128], "bfloat16"),
+    "ONB": ("sbuf", [128, 128], "bfloat16"), "CS": ("sbuf", [128, 128], "bfloat16"),
+    "BQ": ("sbuf", [128, 144], "bfloat16"), "BN": ("sbuf", [128, 144], "bfloat16"), "BV": ("sbuf", [128, 144], "bfloat16"),
+    "BM": ("sbuf", [128, 144], "bfloat16"), "BW": ("sbuf", [128, 144], "float16"),
+    "GA": ("sbuf", [128, 128], "bfloat16"), "MK": ("sbuf", [128, 16 * 96], "bfloat16"),
+    "CI": ("sbuf", [128, H], "float32"), "CAP": ("sbuf", [128, H], "float32"),
+    "LI": ("sbuf", [128, 32], "float32"), "LJ": ("sbuf", [128, 32], "float32"), "LT": ("sbuf", [128, 128], "float32"),
+    "KI": ("sbuf", [128, 32], "float32"), "K16": ("sbuf", [128, 32], "float32"), "KH": ("sbuf", [128, 16], "float32"),
+    "KF": ("sbuf", [128, 32], "float16"), "KY": ("sbuf", [128, 16], "float16"),
+    "ACOL": ("sbuf", [128, 1], "float32"), "AJ": ("sbuf", [128, 32], "float32"),
 }
-BANKS = ["ZP", "UU", "VV", "PX", "VT0", "VT1", "DF0", "DF1"]
+BANKS = ["VT0", "VT1", "UU", "VV", "LS", "SA", "CC", "DD"]
 for _n in BANKS:
     SCRATCH[_n] = ("psum", [128, K], "float32")
 for _t in range(3):
     SCRATCH["SU%d" % _t] = ("sbuf", [128, K], "uint16")
-    SCRATCH["SE%d" % _t] = ("sbuf", [128, K], "int32")
     SCRATCH["Z%d" % _t] = ("sbuf", [128, K], "bfloat16")
     SCRATCH["BA%d" % _t] = ("sbuf", [128, K], "int32")
     SCRATCH["ZO%d" % _t] = ("sbuf", [128, K], "bfloat16")
-    if _t < 2:
-        SCRATCH["UO%d" % _t] = ("sbuf", [128, K], "uint16")
-        SCRATCH["EO%d" % _t] = ("sbuf", [128, K], "int32")
-WF32 = ["h", "un", "u20", "zq", "zl", "h5", "h1k", "np0", "np", "w0", "w1", "n32", "hl", "p5", "cl", "pz", "h528", "lp", "ll"]
-WI32 = ["vi", "v", "ui", "u", "u2", "q", "j0", "j", "d", "dd", "x15", "xk"]
-WU16 = ["MLu", "zlu", "jlu", "hlu", "ylu", "xlu", "clu", "llu", "huu"]
-SCRATCH["FW"] = ("sbuf", [128, 32 * len(WF32)], "float32")
-SCRATCH["IW"] = ("sbuf", [128, 32 * len(WI32)], "int32")
-SCRATCH["LU"] = ("sbuf", [128, 32 * len(WU16)], "uint16")
+    SCRATCH["SN%d" % _t] = ("sbuf", [128, K], "int32")
+    if _t < 2: SCRATCH["UO%d" % _t] = ("sbuf", [128, K], "uint16")
+    for _p in range(2): SCRATCH["D%d%d" % (_t, _p)] = ("dram", [128, H], "int32")
+TILES = {"FW": ("float32", ["xk", "a", "w"]), "IW": ("int32", ["x15", "n", "n2", "j"]), "BT": ("bfloat16", ["h", "un", "pst"]),
+         "LU": ("uint16", ["ml", "xl", "jl", "yl"])}
 TILE = {}
-for _i, _n in enumerate(WF32): TILE["f_" + _n] = ("FW", 32 * _i)
-for _i, _n in enumerate(WI32): TILE["i_" + _n] = ("IW", 32 * _i)
-for _i, _n in enumerate(WU16): TILE[_n] = ("LU", 32 * _i)
+for _b, (_d, _names) in TILES.items():
+    SCRATCH[_b] = ("sbuf", [128, 32 * len(_names)], _d)
+    for _i, _n in enumerate(_names): TILE[_n] = (_b, 32 * _i)
+SCRATCH["UI"] = ("sbuf", [128, 64], "int32")
+SCRATCH["UM"] = ("sbuf", [128, 64], "int32")
+SCRATCH["L3"] = ("sbuf", [128, 96], "uint16")
 
-LOADS = ["STK", "X", "Z0", "WI", "LN8", "BA0", "CON"]
-ARR = ["SU1a", "SU1b", "SU2a", "SU2b", "SE1", "SE2", "Z1", "Z2", "BA1", "BA2"]
-SEMAPHORES = (["sV", "sA", "sP", "sG", "local", "dD", "dY", "oS", "oZ", "oC", "oN"]
+LOADS = ["STKa", "STKb", "X", "Z0", "WI", "LN8", "BAS", "CON", "D00", "D01"]
+ARR = ["%s%d%d" % (n, t, p) for n in ("SU", "D", "Z") for t in (1, 2) for p in (0, 1)] + ["BA1", "BA2"]
+SEMAPHORES = (["sV", "sA", "sP", "sG", "local", "dY0", "dY1", "out"]
               + ["ld" + n for n in LOADS] + ["ar" + n for n in ARR])
 
 
@@ -97,7 +98,7 @@ def rank_program(g, core, T, topo):
             for name, lo, hi in lst:
                 ps = name in BANKS
                 for l, h, w, oq, sem, cnt in hist.get(name, []):
-                    if not ps and (h <= lo or hi <= l): continue
+                    if (oq == q or not ps) and (h <= lo or hi <= l): continue
                     if oq == q:
                         if not (w and (not isw or own_waw)): continue
                     elif not (isw or w or ps): continue
@@ -128,34 +129,38 @@ def rank_program(g, core, T, topo):
         fn().then_inc(T.sem[sem], 1)
         note(q, q, reads, writes, sem, total[sem])
 
-    def dma(q, out, in_, sem, last=True):
+    def dma(q, out, in_, sem):
         await_deps(q, in_[1], out[1], True)
         total[sem] += 16
         queue[q].dma_start(out[0], in_[0]).then_inc(T.sem[sem], 16)
         note("dma" + sem, q, in_[1], out[1], sem, total[sem])
 
     def b(name, lo=0, hi=None, step=1, p0=0, p1=128):
-        if name in TILE:
-            name, o = TILE[name]
-            lo, hi = o + lo, o + (32 if hi is None else hi)
         hi = SCRATCH[name][1][-1] if hi is None else hi
         ap = T[name][p0:p1, lo:hi] if step == 1 else T[name][p0:p1, lo:hi:step]
         return (ap, [(name, lo, hi)])
 
-    def ind(name, lo, hi, lst, c0=0, c1=32):
-        lst, o = TILE.get(lst, (lst, 0))
-        return (T[name][:, lo:hi].indirect(T[lst][:, o + c0:o + c1]), [(name, lo, hi), (lst, o + c0, o + c1)])
+    def w(name, p=None):
+        buf, o = TILE[name]
+        return b(buf, o, o + 32) if p is None else b(buf, o + 16 * p, o + 16 * p + 16)
+
+    def ind(win, lst):
+        return (win[0].indirect(lst[0]), win[1] + lst[1])
+
+    def scattered(win, lst):
+        return (win[0].indirect(lst[0]), win[1], lst[1])
 
     def tt(out, a, c, o):
         run("V", lambda: g.vector.tensor_tensor(out[0], a[0], c[0], o), out, [a, c])
 
     def ts(out, a, s1, o1, s2=None, o2=None, waw=False):
-        ins = [a] + ([s1] if isinstance(s1, tuple) else [])
+        ins = [a] + [s for s in (s1, s2) if isinstance(s, tuple)]
         v1 = s1[0] if isinstance(s1, tuple) else s1
+        v2 = s2[0] if isinstance(s2, tuple) else s2
         if o2 is None:
             run("V", lambda: g.vector.tensor_scalar(out[0], a[0], v1, None, o1), out, ins, waw)
         else:
-            run("V", lambda: g.vector.tensor_scalar(out[0], a[0], v1, s2, o1, o2), out, ins, waw)
+            run("V", lambda: g.vector.tensor_scalar(out[0], a[0], v1, v2, o1, o2), out, ins, waw)
 
     def cp(out, a, waw=False):
         run("V", lambda: g.vector.tensor_copy(out[0], a[0]), out, [a], waw)
@@ -166,281 +171,350 @@ def rank_program(g, core, T, topo):
     def fill(out, v, waw=False):
         run("V", lambda: g.vector.memset(out[0], v), out, [], waw)
 
-    def ac(out, a, func=act.Copy, **kw):
+    def ac(out, a, func=act.Copy, total_in=None, **kw):
+        if total_in:
+            kw["accum_out"] = total_in[0]
+            out = (out[0], out[1] + total_in[1])
         run("A", lambda: g.scalar.activation(out[0], a[0], func, **kw), out, [a])
 
     def mm(out, l, r, start, stop):
         run("P", lambda: g.tensor.matmul(out[0], l[0], r[0], start, stop), out, [l, r])
 
-    def iota(out, pattern, base, cm):
-        run("G", lambda: g.iota(out[0], pattern, base, cm, allow_small_or_imprecise_dtypes=True), out, [])
+    def mms(out, terms):
+        for i, (l, r) in enumerate(terms): mm(out, l, r, i == 0, i == len(terms) - 1)
+
+    def wrap(sel, name, lo, hi):
+        return [(b(sel, 15 - r, 143 - r), b(name, lo + r, hi, 16)) for r in range(16)]
+
+    def iota(out, pattern, base, cm, small=True):
+        if small: run("G", lambda: g.iota(out[0], pattern, base, cm, allow_small_or_imprecise_dtypes=True), out, [])
+        else: run("G", lambda: g.iota(out[0], pattern, base, cm), out, [])
 
     def select(out, a, pattern, cmp, fillv, base, cm):
         run("G", lambda: g.affine_select(out[0], a[0], pattern, cmp, fillv, base, cm), out, [a])
 
-    def send(src, dst_name, lo, hi, dst, part=""):
+    def send(src, dst_ap, sem, dst):
         await_deps("G", src[1], [], False)
         rid, pid, _se = topo.addr(dst)
-        m = topo.mask(core, dst)
-        n = len(topo.engines(core, dst))
-        g.remote_dma(T[dst_name][:, lo:hi], src[0], T.sem["ar" + dst_name + part], T.sem["local"], pid, rid, m)
-        total["local"] += n
+        g.remote_dma(dst_ap, src[0], T.sem["ar" + sem], T.sem["local"], pid, rid, topo.mask(core, dst))
+        total["local"] += len(topo.engines(core, dst))
 
-    def arrives(name, lo, hi, src, part=""):
+    def arrives(name, lo, hi, src, sem):
         n = len(topo.engines(src, core))
-        total["ar" + name + part] += n
-        note("remote", None, [], [(name, lo, hi)], "ar" + name + part, n)
+        total["ar" + sem] += n
+        note("remote", None, [], [(name, lo, hi)], "ar" + sem, n)
 
-    nxt = T.cores[(rank + STEP) % len(T.cores)]
-    nxt2 = T.cores[(rank + 2 * STEP) % len(T.cores)]
-    prv = T.cores[(rank - STEP) % len(T.cores)]
-    prv2 = T.cores[(rank - 2 * STEP) % len(T.cores)]
+    def weave(*steps):
+        steps = list(steps)
+        while steps:
+            steps = [s for s in steps if next(s, None) is not None]
+
+    ring = lambda n: T.cores[(rank + n * STEP) % len(T.cores)]
     for t in (1, 2):
-        for part, (l0, l1) in zip("ab", HALVES): arrives("SU%d" % t, l0, l1, prv, part)
-        arrives("SE%d" % t, 0, K, prv)
-        arrives("Z%d" % t, 0, K, prv)
-    arrives("BA1", 0, K, prv)
-    arrives("BA2", 0, K, prv2)
+        for p, (l0, l1) in enumerate(PARTS):
+            arrives("SU%d" % t, l0, l1, ring(-1), "SU%d%d" % (t, p))
+            arrives("Z%d" % t, l0, l1, ring(-1), "Z%d%d" % (t, p))
+            arrives("D%d%d" % (t, p), 0, H, ring(-1), "D%d%d" % (t, p))
+        arrives("BA%d" % t, 0, K, ring(-t), "BA%d" % t)
 
-    dma("S", b("STK"), (T.stk[:, :], []), "ldSTK")
+    first = EDGES[2]
+    dma("S", b("STK", 0, first), (T.stk[:, 0:first], []), "ldSTKa")
     dma("S", b("X"), (T.xt[:, :], []), "ldX")
+    dma("S", b("STK", first, K), (T.stk[:, first:K], []), "ldSTKb")
+    dma("S", b("Z0", 0, K), (T.z[:, :], []), "ldZ0")
     dma("A", b("LN8", p1=8), (T.ln[:, :], []), "ldLN8")
     dma("A", b("WI"), (T.w[:, :], []), "ldWI")
-    dma("A", b("Z0", 0, K), (T.z[:, :], []), "ldZ0")
-    dma("A", b("CON"), (T.con[:, :], []), "ldCON")
-    dma("A", b("BA0"), (T.bas[:, :], []), "ldBA0")
+    dma("S", b("CON"), (T.con[:, :], []), "ldCON")
+    dma("S", b("BAS"), (T.bas[:, :], []), "ldBAS")
+    for p, (l0, l1) in enumerate(PARTS): dma("S", (T["D0%d" % p][:, :], [("D0%d" % p, 0, H)]), (T.stk[:, l0:l1], []), "ldD0%d" % p)
+
+    def yall(p, lo, hi):
+        return (T["Y%d" % p][:, lo:hi], [("Y%d" % p, 0, 64)])
+
+    def shifts(t, p):
+        Y, D = "Y%d" % p, "D%d%d" % (t, p)
+        if t: await_deps("S", [("D%d1" % t, 0, H)], [], False)
+        for q in range(16):
+            dma("S", (T[Y][q::16, (15 - q) * H:(31 - q) * H], [(Y, 4 * q, 4 * q + 1)]), (T[D][:, :], [(D, 0, H), (Y + "f", 0, 2)]), "d" + Y)
+        if t == 0:
+            for q in range(13):
+                dma("S", (T[Y][q::16, 2 * H:(15 - q) * H], [(Y, 4 * q + 2, 4 * q + 3)]), (T[D][0:8 * (13 - q), :], [(D, 0, H)]), "d" + Y)
 
     fill(b("ONE"), 1.0)
     iota(b("KC", p1=16), [[0, 1]], 0, 1)
     select(b("E", p1=16), b("ONE", p1=16), [[0, 8], [-1, 16]], op.is_equal, 0.0, 0, 1)
     mm(b("UU", 0, 1), b("E", p1=16), b("KC", p1=16), True, True)
-    for t in range(3): fill(b("L2S", 64 * t, 64 * t + 64, p1=16), float(TOP + (t + 1) * NP))
-    iota(b("KI"), [[16, 32]], 0, 0)
     select(b("TA"), b("ONE"), [[-1, 128]], op.is_equal, 0.0, 0, 1)
     select(b("TB", 0, 9), b("ONE", 0, 9), [[-16, 9]], op.is_ge, 0.0, 0, 1)
     select(b("TB", 16, 25), b("TB", 0, 9), [[16, 9]], op.is_ge, 0.0, 15, -1)
+    iota(b("KI"), [[16, 32]], 0, 0)
+    iota(b("LI"), [[1, 32]], 0, 0)
+    iota(b("CI"), [[256, 16], [-1, 16]], 15 - 8 * int(VOTE), 0)
     select(b("TC", p1=8), b("ONE", p1=8), [[1, 128]], op.is_ge, 0.0, 0, -16)
     select(b("TD", p1=8), b("TC", p1=8), [[-1, 128]], op.is_ge, 0.0, 15, 16)
-    for t in range(3):
-        select(b("L2T", 64 * t, 64 * t + 64, p1=16), b("L2S", 64 * t, 64 * t + 64, p1=16), [[1, 64]], op.is_ge, -float(TOP), -1, -1)
-    iota(b("LB", 0, 32), [[16384, 32]], 8192, 0)
-    iota(b("LB", 32, 64), [[16384, 32]], -8192, 0)
-    for n in ("LW0", "LW1"): iota(b(n, 528, 560), [[32, 32]], 0, 0)
+    iota((T.Y0[:, 16 * H + YV:31 * H], [("Y0f", 0, 1)]), [[0, 15 * H - YV]], FAR, 0, False)
+    iota((T.Y1[:, 16 * H:31 * H], [("Y1f", 0, 1)]), [[0, 15 * H]], FAR, 0, False)
     fill(b("BQ"), 0.0)
-    fill(b("D1A"), -1.0)
-    cp(b("RC"), b("UU", 0, 1))
-    fill(b("RB", 8192, 8224), 0.0)
-    ts(b("IC"), b("RC"), 16384.0, op.mult)
-    ts(b("SE0"), b("STK"), b("IC"), op.add)
-    cp(b("SU0"), b("STK"))
-    cp(b("ID"), b("TA"))
-    fill((T.GE[:, :, 0:256:16], [("GE0", 0, K)]), 1.0)
-
-    def rotations(t):
-        se = b("SE%d" % t)
-        for half in (0, 1):
-            dma("S", (T.D[:, 16 * half:16 * half + 16, :], [("D", 16 * half, 16 * half + 16)]), se, "dD")
-        for q in range(16):
-            dma("S", (T.Y[q::16, :], [("Y", q * 100000, q * 100000 + 1)]), (T.D[:, q:q + 16, :], [("D", q, q + 16)]), "dY")
-
-    yall = [("Y", 0, 1600000)]
-    rotations(0)
-
-    ts(b("ND"), b("TA"), -1.0, op.mult)
-    ts(b("HI"), b("TA"), 0.5, op.mult)
-    ts(b("KW"), b("KI"), b("RC"), op.add)
-    cp(b("BQ", 15, 144, 16), b("TB", 16, 25), True)
-    ts(b("K16"), b("KW"), 16.0, op.mult)
-    ts(b("K5"), b("KW"), 512.0, op.add)
-    fill(b("D1A", 0, K, 16), 15.0, True)
-    for l0, l1 in CHUNKS:
-        c0, c1 = l0 // 16, l1 // 16
-        ts(b("KH", c0, c1), b("K16", c0, c1), float(-1 - 16 * l0), op.add)
-        ts(b("D1A", l0 + 15, l1, 16), b("K16", c0, c1), float(14 - 16 * l0), op.add, waw=True)
     fill(b("MK"), 1.0)
-    fill(b("MK", 0, 2048, 16), 0.0, True)
-    for n in ("LW0", "LW1"): fill(b(n, 512, 528), 32.0)
-    for n in ("CM0", "CM1"): fill(b(n, 512, 528), -1.0)
-    fill(b("LB", 48, 64), -1048576.0, True)
-    fill(b("HQ"), -1.0 / 512.0)
-    fill(b("ONB"), 1.0)
-    cp(b("GA", p1=8), b("TD", p1=8))
-    cp(b("LNB", p1=8), b("LN8", p1=8))
-    mm(b("PX"), b("GA", p1=8), b("LNB", p1=8), True, True)
-    mm(b("VV", 0, 192), b("E", p1=16), b("L2T", p1=16), True, True)
-    mm(b("ZP"), b("ID"), b("Z0", 0, K), True, True)
+    fill(b("CS"), 0.0)
+    fill(b("RB", 8192, 8224), 0.0)
+    fill(b("MK", 0, None, 16), 0.0, True)
+    cp(b("RC"), b("UU", 0, 1))
+    fill((T.GE[:, :, :, 0], [("GE0", 0, K)]), 1.0)
+    for s in range(1, max(SIGNS) + 1): fill(b("CS", s, None, 16), 8 * VOTE, True)
+    cp(b("BQ", 15, 144, 16), b("TB", 16, 25), True)
+    for name, scale in (("ID", 1.0), ("ND", -1.0), ("I16", H / 4096.0), ("I32", 32.0), ("I256", 256.0), ("IT", float(TOFF))):
+        ac(b(name), b("TA"), scale=scale)
+    for name, scale in (("BN", -VOTE), ("BV", 1024.0), ("BM", H / 2.0)): ac(b(name), b("BQ"), scale=scale)
+    ac(b("ONB"), b("ONE"), scale=1.0 / 128.0)
+    ac(b("GB"), b("TB", 16, 24))
+    ac(b("GA", p1=8), b("TD", p1=8))
+    ts(b("R16"), b("RC"), 16.0, op.mult)
+    cp(b("SU0", 0, first), b("STK", 0, first))
+    ts(b("KF"), b("KI"), b("RC"), op.add)
+    ts(b("LJ"), b("LI"), b("RC"), op.is_gt)
+    ts(b("CAP"), b("CI"), b("R16"), op.add)
+    ts(b("K16"), b("KF"), 16.0, op.mult)
+    ts(b("KY"), b("KF", 0, 16), 5.0 * H, op.add)
+    fill(b("LT", 0, 32), float(FAR))
+    for t in range(ROUNDS):
+        ts(b("LT", 32 * t + 32, 32 * t + 64), b("LJ"), float(DEAD - (t + 3) * FAR), op.mult, float(FAR), op.add)
+    ts(b("KH"), b("K16", 0, 16), -1.0 - 8 * VOTE, op.add)
+    for n in ("PW0", "PW1"): fill(b(n, K, TOFF), float(FAR))
     cp(b("WF"), b("WI"))
+    cp(b("LNB", p1=8), b("LN8", p1=8))
     ts(b("BW"), b("BQ"), b("WF"), op.mult)
-    cp(b("L2"), b("VV", 0, 192))
-    ts(b("LX"), b("PX"), b("RC"), op.is_gt, float(TOP), op.mult)
+    mm(b("SA"), b("GA", p1=8), b("LNB", p1=8), True, True)
+    fill((T.Y0[:, 16 * H:16 * H + YV], [("Y0f", 1, 2)]), FAR)
+    shifts(0, 0)
+    shifts(0, 1)
 
-    send(b("BA0"), "BA1", 0, K, nxt)
-    send(b("BA0"), "BA2", 0, K, nxt2)
+    def coded():
+        ts(b("LX"), b("SA"), b("RC"), op.is_gt, -float(FAR), op.mult)
+        ts(b("CC"), b("CON"), float(DEAD), op.add)
+        ts(b("BA0"), b("BAS"), float(BASE), op.add)
+        tt(b("PW0", 0, K), b("LX"), b("CC"), op.add)
+        for n in (1, 2): send(b("BA0"), T["BA%d" % n][:, :], "BA%d" % n, ring(n))
 
-    NC = len(CHUNKS)
-    w = lambda n: b("f_" + n)
-    x = lambda n: b("i_" + n)
-    later = [lambda: ac(b("LW0", 0, K), b("PX"), scale=32.0),
-             lambda: tt(b("CM0", 0, K), b("LX"), b("CON"), op.add)]
+    xall = b("X")
+
+    def records(t, ci, on="A"):
+        l0, l1 = CHUNKS[ci]
+        (ac if on == "A" else cp)(b("RB", 16 * l0 + 15, 16 * l1 + 15), ind(xall, b("SU%d" % t, l0, l1)))
+
+    def row(ci, i):
+        a0, a1 = 16 * CHUNKS[ci][0] + 15, 16 * CHUNKS[ci][1] + 15
+        return (T.RB[:, a0 + i:a1:16], [("RB", a0, a1)])
+
+    def slots(ci, s0, s1, r=None):
+        l0, l1 = CHUNKS[ci]
+        ap = T.GE[:, l0 // 16:l1 // 16, :, s0:s1] if r is None else T.GE[:, l0 // 16:l1 // 16, r, s0:s1]
+        return (ap, [("GE%d" % s, l0, l1) for s in range(s0, s1)])
+
+    def differences(t, ci):
+        l0, l1 = CHUNKS[ci]
+        n = SIGNS[ci]
+        for s in range(1, n + 1):
+            mms(b("DD", s - 1, n * (l1 - l0), n), [(b("ID"), row(ci, 16 - s)), (b("ND"), b("Z%d" % t, l0, l1))])
+
+    def signs(ci):
+        l0, l1 = CHUNKS[ci]
+        n = SIGNS[ci]
+        if n: ac(slots(ci, 1, n + 1), b("DD", 0, n * (l1 - l0)), act.Sign, bias=0.5)
+
+    def compare(t, ci, between=None):
+        l0, l1 = CHUNKS[ci]
+        for s in range(SIGNS[ci] + 1, 16):
+            tt((T.GE[:, l0 // 16:l1 // 16, :, s], [("GE%d" % s, l0, l1)]), row(ci, 16 - s), b("Z%d" % t, l0, l1), op.is_ge)
+            yield 1
+        p = l0 // H
+        level = [(b("ND"), b("CS", 0, l1 - l0))] if SIGNS[ci] else []
+        mms(b("VT%d" % p, l0 - p * H, l1 - p * H), level + [(b("BN", 15 - r, 143 - r), slots(ci, 0, 16, r)) for r in range(16)])
+        if between: weave(between)
+        scan(b("PM", 16 * l0, 16 * l1), b("MK", 0, 16 * (l1 - l0)), b("RB", 16 * l0 + 15, 16 * l1 + 15), op.mult, op.max)
+        yield 1
+
+    def handler(t, p):
+        l0, l1 = PARTS[p]
+        scan(b("OA", l0, l1), b("VT%d" % p, 0, H), b("CAP"), op.min, op.max)
+        end = b("OA", l0 + 15, l1, 16)
+        ts(w("ml", p), end, 8 * VOTE, op.add)
+        tt(w("h", p), end, b("KH"), op.subtract)
+
+    def taken(t, p):
+        l0, l1 = PARTS[p]
+        ac(b("ZM%d" % p, H, 2 * H), ind(b("PM", 16 * l0, 16 * l1), w("ml", p)))
+        mms(b("UU", 0, 16), wrap("BW", "ZM%d" % p, H, 2 * H))
+        ac(b("AG", l0, l1), ind(b("RB", 16 * l0 + 16, 16 * l1 + 16), w("ml", p)))
+        mms(b("VV", 0, 16) if p else b("UU", 16, 32), wrap("BV", "AG", l0, l1))
+        mms(b("SA", 0, H), [(b("ID"), b("AG", l0, l1)), (b("ND"), b("Z%d" % t, l0, l1))])
+
+    def changed(t, p):
+        o = 32 * p
+        ts(w("x15", p), b("UI", o, o + 16), 15, op.bitwise_and)
+        yield 1
+        tt(w("xk", p), w("x15", p), b("K16", 16 * p, 16 * p + 16), op.add)
+        yield 1
+        cp(w("xl", p), w("xk", p))
+        yield 1
+
+    def lists(t, p):
+        o, l0, l1 = 32 * p, PARTS[p][0], PARTS[p][1]
+        u, v = b("UM", o, o + 16), b("UM", o + 16, o + 32)
+        ts(w("un", p), w("h", p), 16.0, op.is_ge, 4096.0, op.mult)
+        yield 1
+        if p:
+            cp(b("UI", 48, 64), b("VV", 0, 16))
+            yield 1
+        ts(b("UM", o, o + 32), b("UI", o, o + 32), 4095, op.bitwise_and)
+        yield 1
+        tt(w("pst", p), v, w("un", p), op.is_gt)
+        ts(w("a", p), u, 32.0, op.add)
+        yield 1
+        mms(b("LS", 0, 16), [(b("ID"), b("KF", 0, 16)), (b("I16"), w("un", p))])
+        mms(b("LS", 16, 32), [(b("ID"), w("h", p))] + [(b("I32"), w("pst", p))] * (t + 1))
+        mms(b("LS", 32, 48), [(b("ID"), b("KF", 16 * p, 16 * p + 16)), (b("IT"), w("pst", p))])
+        ts(w("w", p), w("pst", p), -float(NOP), op.mult, b("ACOL") if t else float(NOP), op.add)
+        tt(w("n", p), u, w("a", p), op.mult)
+        yield 1
+        tt(w("n2", p), w("n", p), w("w", p), op.add)
+        yield 1
+        ts(w("j", p), w("n2", p), 5, op.arith_shift_right, 511 + (NOP >> 5), op.bitwise_and)
+        cp(b("L3", 48 * p, 48 * p + 48), b("LS", 0, 48))
+        yield 1
+        ts(w("jl", p), w("j", p), float(K), op.min)
+        yield 1
+
+    def piece(t, p):
+        l0, l1 = PARTS[p]
+        tt(b("PB", l0, l1), ind(b("PW%d" % (t % 2), 0, TOFF), w("jl", p)), b("BA%d" % t, l0, l1), op.min)
+
+    def mark(t, p):
+        l0, l1 = PARTS[p]
+        ac(b("ZM%d" % p, 0, H), b("SA", 0, H), act.Abs)
+        ac(b("ZO%d" % t, l0, l1), ind(b("ZM%d" % p), b("L3", 48 * p, 48 * p + 16)))
+        if t < ROUNDS - 1: send(b("ZO%d" % t, l0, l1), T["Z%d" % (t + 1)][:, l0:l1], "Z%d%d" % (t + 1, p), ring(1))
+        else: dma("S", (T.yz[:, l0:l1], []), b("ZO%d" % t, l0, l1), "out")
+
+    def lengths(t, p):
+        l0, l1 = PARTS[p]
+        ac(b("SG", l0, l1), b("PB", l0, l1), act.Sign)
+        mms(b("LS", 64, 80), [(b("ID"), b("KY")), (b("I256"), w("h", p)), (b("ND"), w("un", p)), (b("I256"), w("pst", p))]
+            + wrap("BM", "SG", l0, l1))
+
+    def stack(t, p):
+        l0, l1 = PARTS[p]
+        sn = b("SN%d" % t, l0, l1)
+        cp(w("yl", p), b("LS", 64, 80))
+        yield 1
+        tt(b("TY", l0, l1), ind(yall(p, 2 * H, 31 * H), w("yl", p)), b("PB", l0, l1), op.min)
+        yield 1
+        ts(sn, b("TY", l0, l1), 8191, op.bitwise_and)
+        yield 1
+        if t < ROUNDS - 1:
+            cp(b("UO%d" % t, l0, l1), sn)
+            send(b("UO%d" % t, l0, l1), T["SU%d" % (t + 1)][:, l0:l1], "SU%d%d" % (t + 1, p), ring(1))
+            send(sn, T["D%d%d" % (t + 1, p)][:, :], "D%d%d" % (t + 1, p), ring(1))
+        else:
+            cp(b("FO", l0, l1), sn)
+            dma("S", (T.ys[:, l0:l1], []), b("FO", l0, l1), "out")
+        yield 1
+
+    def stored(t, p):
+        l0, l1 = PARTS[p]
+        new = b("PW%d" % (t % 2), TOFF + l0, TOFF + l1)
+        tt(new, ind(b("LT"), b("L3", 48 * p + 16, 48 * p + 32)), yall(p, 15 * H, 16 * H), op.add)
+        yield 1
+        tt(b("CC", l0, l1) if t < ROUNDS - 1 else b("CI32", l0, l1), new, b("CC", l0, l1), op.min)
+        yield 1
+        if t == ROUNDS - 1:
+            ts(b("CN", l0, l1), b("CI32", l0, l1), 8191, op.bitwise_and)
+            yield 1
+            cp(b("FC", l0, l1), b("CN", l0, l1))
+            dma("S", (T.yc[:, l0:l1], []), b("FC", l0, l1), "out")
+            yield 1
+
+    def pieces(t, p):
+        l0, l1 = PARTS[p]
+        src = ind(b("PW%d" % (t % 2)), b("L3", 48 * p + 32, 48 * p + 48))
+        if t < ROUNDS - 1: ac(b("PW%d" % ((t + 1) % 2), l0, l1), src)
+        else:
+            ac(b("SF", l0, l1), src, act.Sign)
+            mms(b("SA", H, 2 * H, p1=8), [(b("GB"), b("SF", l0, l1))])
+            ac(b("FN", l0, l1, p1=8), b("SA", H, 2 * H, p1=8), act.Identity, bias=8.0, scale=-0.5)
+            dma("S", (T.yn[:, l0:l1], []), b("FN", l0, l1, p1=8), "out")
+
+    def halves():
+        ac(b("OX"), ind(xall, w("xl", 0)))
+        mms(b("SA", H, 2 * H), [(b("ID"), b("ZM0", H, 2 * H)), (b("ID"), b("OX"))])
+        ac(b("NF"), b("SA", H, 2 * H), act.Identity, bias=WHOLE, scale=0.5 - 1.0 / 2048.0)
+        ac(b("NB"), b("NF"), act.Identity, bias=-WHOLE)
+
+    def table():
+        yield from changed(0, 1)
+        tt(b("XS"), ind(xall, w("xl", 1)), b("ZM1", H, 2 * H), op.add)
+        yield 1
+        ts(b("XH"), b("XS"), 1, op.arith_shift_right)
+        yield 1
+
+    def unhandled():
+        mm(b("SA", 0, 32), b("ONB"), w("un"), True, True)
+        ac(b("AJ"), b("SA", 0, 32), act.Identity, total_in=b("ACOL"), bias=NOP / 32.0)
+
     for t in range(ROUNDS):
         last = t == ROUNDS - 1
-        SU, SE, Z, BA = "SU%d" % t, "SE%d" % t, "Z%d" % t, "BA%d" % t
-        CMc, CMn = "CM%d" % (t % 2), "CM%d" % ((t + 1) % 2)
-        LWc, LWn = "LW%d" % (t % 2), "LW%d" % ((t + 1) % 2)
-        if t: rotations(t)
-        if t: mm(b("ZP"), b("ID"), b(Z, 0, K), True, True)
-
-        def records(ci):
-            l0, l1 = CHUNKS[ci]
-            ac(b("RB", 16 * l0 + 15, 16 * l1 + 15), ind("X", 0, NREC, SU, l0, l1))
-
-        def ge(l0, l1, i):
-            return (T.GE[:, l0 // 16:l1 // 16, i:256:16], [("GE%d" % i, l0, l1)])
-
-        def row(l0, l1, i):
-            a0, a1 = 16 * l0 + 15, 16 * l1 + 15
-            return (T.RB[:, a0 + i:a1:16], [("RB", a0, a1)])
-
-        def compare(ci):
-            l0, l1 = CHUNKS[ci]
-            for i in range(1, 16):
-                tt(ge(l0, l1, i), row(l0, l1, i), b("ZP", l0, l1), op.is_ge)
-            scan(b("PM", 16 * l0, 16 * l1), b("MK", 0, 16 * (l1 - l0)), b("RB", 16 * l0 + 15, 16 * l1 + 15), op.mult, op.max)
-
-        def votes(ci):
-            l0, l1 = CHUNKS[ci]
-            for r in range(16):
-                mm(b("VT%d" % (ci % 2), 0, l1 - l0), b("BQ", 15 - r, 143 - r),
-                   (T.GE[:, l0 // 16:l1 // 16, 16 * r:16 * r + 16], [("GE%d" % i, l0, l1) for i in range(16)]), r == 0, r == 15)
-
-        def handler(ci):
-            l0, l1 = CHUNKS[ci]
-            c0, c1 = l0 // 16, l1 // 16
-            ts(b("T1", l0, l1), b("VT%d" % (ci % 2), 0, l1 - l0), 7.5, op.is_lt, 32768.0, op.mult)
-            scan(b("OA", l0, l1), b("T1", l0, l1), b("D1A", l0, l1), op.min, op.add)
-            cp(b("MLu", c0, c1), b("OA", l0 + 15, l1, 16))
-
-        def taken(ci):
-            l0, l1 = CHUNKS[ci]
-            ac(b("ZM", K + l0, K + l1), ind("PM", 16 * l0, 16 * l1, "MLu", l0 // 16, l1 // 16))
-            ac(b("AG", l0, l1), ind("RB", 16 * l0 + 16, 16 * l1 + 16, "MLu", l0 // 16, l1 // 16))
-
-        def changes(ci):
-            l0, l1 = CHUNKS[ci]
-            mm(b("DF0", l0, l1), b("ID"), b("AG", l0, l1), True, False)
-            mm(b("DF0", l0, l1), b("ND"), b(Z, l0, l1), False, True)
-
-        records(0)
-        records(1)
-        for ci in range(NC):
-            compare(ci)
-            votes(ci)
-            if ci >= 2: changes(ci - 2)
-            if ci + 2 < NC: records(ci + 2)
-            if ci == 0 and t: cp(b("ACOL"), b("VV", 0, 1))
-            if ci == LATER:
-                for f in later: f()
-                later = []
-            if ci:
-                handler(ci - 1)
-                taken(ci - 1)
-        handler(NC - 1)
-        taken(NC - 1)
-        for r in range(16): mm(b("UU", 0, 32), b("BW", 15 - r, 143 - r), b("ZM", K + r, 2 * K, 16), r == 0, r == 15)
-        changes(NC - 2)
-        changes(NC - 1)
-        for r in range(16): mm(b("VV", 0, 32), b("BQ", 15 - r, 143 - r), b("AG", r, K, 16), r == 0, r == 15)
-
-        tt(w("h"), b("OA", 15, K, 16), b("KH"), op.subtract)
-        ts(w("zq"), w("h"), 16.0, op.is_ge, 512.0, op.mult)
-        ts(w("u20"), w("h"), 16.0, op.is_ge, float(NP), op.mult)
-        tt(w("zl"), w("zq"), b("KW"), op.add)
-        ts(w("h5"), w("h"), 512.0, op.mult)
-        cp(b("zlu"), w("zl"))
-        tt(w("h1k"), w("h5"), b("K5"), op.add)
-        ts(w("h528"), w("h"), 528.0, op.add)
-        cp(b("huu"), w("h"))
-        tt(b(CMc, 528, 1040), ind("L2", 64 * t, 64 * t + 64, "huu"), b(SE), op.add)
-        cp(x("ui"), b("UU", 0, 32))
-        ts(x("u"), x("ui"), 4095, op.bitwise_and)
-        tt(x("u2"), x("u"), x("u"), op.mult)
-        cp(x("vi"), b("VV", 0, 32))
-        ts(x("q"), x("u2"), 5, op.arith_shift_right)
-        ts(x("v"), x("vi"), 3, op.bitwise_and)
-        if t: ts(w("w0"), x("u"), b("ACOL"), op.add)
-        ts(w("np0"), x("v"), 0.0, op.is_equal, float(NP), op.mult)
-        if not last: ts(x("x15"), x("u"), 15, op.bitwise_and)
-        tt(w("np"), w("np0"), w("u20"), op.max)
-        if not last: tt(x("xk"), x("x15"), b("K16"), op.add)
-        tt(w("w1"), w("w0") if t else x("u"), w("np"), op.add)
-        ts(w("n32"), w("np"), 1.0 / 32768.0, op.mult)
-        tt(x("j0"), x("q"), w("w1"), op.add)
-        tt(w("hl"), w("n32"), w("h"), op.add)
-        ts(x("j"), x("j0"), NP + 511, op.bitwise_and)
-        cp(b("hlu"), w("hl"))
-        ts(b("jlu"), x("j"), 512.0, op.min)
-        if not last: cp(b("xlu"), x("xk"))
-        ac(b("ZM", 0, K), b("DF0"), act.Abs)
-        ac(b("ZO%d" % t), ind("ZM", 0, 2 * K, "zlu"))
-        ac(b("LG"), ind(LWc, 0, 528, "jlu"))
-        if not last:
-            mm(b("DF1"), b("HQ"), b("ONB"), True, False)
-            mm(b("DF1"), b("HI"), b("ZM", K, 2 * K), False, False)
-        for r in range(16): mm(b("PX", 0, 32), b("BQ", 15 - r, 143 - r), b("LG", r, K, 16), r == 0, r == 15)
-        if not last:
-            ac(b("OX"), ind("X", 0, NREC, "xlu"))
-            mm(b("DF1"), b("HI"), b("OX"), False, True)
-        tt(b("BE"), ind("LB", 0, 64, "hlu"), b(BA), op.add)
-        tt(b("PB"), ind(CMc, 0, 528, "jlu"), b("BE"), op.max)
-
-        def pieces():
-            ts(w("p5"), w("np"), 1.0, op.is_lt, 528.0, op.mult)
-            ts(w("pz"), w("np"), 1.0, op.is_lt)
-            tt(w("cl"), w("p5"), b("KW"), op.add)
-            tt(w("lp"), w("h528"), w("pz"), op.mult)
-            cp(b("clu"), w("cl"))
-            tt(w("ll"), w("lp"), b("KW"), op.max)
-            cp(b("llu"), w("ll"))
-            cf_old = b("CON") if t == 0 else b("CF%d" % ((t + 1) % 2))
-            tt(b("CFI") if last else b("CF%d" % (t % 2)), ind(CMc, 0, 1040, "clu"), cf_old, op.max)
-
-        if last: pieces()
-        tt(x("d"), w("h1k"), b("PX", 0, 32), op.subtract)
-        ts(x("dd"), x("d"), 8191, op.bitwise_and)
-        cp(b("ylu"), x("dd"))
-        if not last: send(b("ZO%d" % t), "Z%d" % (t + 1), 0, K, nxt)
-        if not last:
-            ac(b("NF"), b("DF1"), act.Identity, bias=WHOLE)
-            ac(b("NB"), b("NF"), act.Identity, bias=-WHOLE)
-        for half, (l0, l1) in enumerate(HALVES):
-            yi = ind("Y", 0, 16 * K, "ylu", l0 // 16, l1 // 16)
-            tt(b("TY", l0, l1), (yi[0], yall + yi[1][1:]), b("PB", l0, l1), op.max)
-            ts(b("SN", l0, l1), b("TY", l0, l1), 8191, op.bitwise_and)
-            if not last:
-                cp(b("UO%d" % t, l0, l1), b("SN", l0, l1))
-                send(b("UO%d" % t, l0, l1), "SU%d" % (t + 1), l0, l1, nxt, "ab"[half])
-                if half == 0:
-                    si = ind("X", 0, NREC, "xlu")
-                    cp((si[0], si[1][:1], si[1][1:]), b("NB"))
-        if not last:
-            ts(b("EO%d" % t), b("SN"), b("IC"), op.add)
-            send(b("EO%d" % t), "SE%d" % (t + 1), 0, K, nxt)
-            pieces()
-            later.append(lambda a=LWn, c=LWc: ac(b(a, 0, K), ind(c, 0, 560, "llu")))
-            later.append(lambda a=CMn, c=CMc: ac(b(a, 0, K), ind(c, 0, 1040, "clu")))
-            ts(w("un"), w("h"), 16.0, op.is_ge)
-            run("V", lambda: g.vector.tensor_reduce(T.RED[:, :], w("un")[0], AxisListType.X, op.add), b("RED"), [w("un")])
-            mm(b("VV", 0, 1), b("ONE"), b("RED"), True, True)
+        if t == 0:
+            records(t, 1)
+            records(t, 0, "V")
+            cp(b("SU0", first, K), b("STK", first, K))
         else:
-            cp(b("FO"), b("SN"))
-            dma("S", (T.ys[:, :], []), b("FO"), "oS")
-            dma("S", (T.yz[:, :], []), b("ZO%d" % t), "oZ")
-            ts(b("FI"), b("CFI"), 8191, op.bitwise_and)
-            cp(b("FC"), b("FI"))
-            dma("S", (T.yc[:, :], []), b("FC"), "oC")
-            ac(b(LWn, 0, K), ind(LWc, 0, 560, "llu"))
-            ac(b("FN"), b(LWn, 0, K), scale=1.0 / 32.0)
-            dma("S", (T.yn[:, :], []), (T.FN[0:128:16, :], [("FN", 0, K)]), "oN")
+            records(t, 0)
+            weave(stack(t - 1, 1), stored(t - 1, 1))
+            shifts(t, 0)
+            shifts(t, 1)
+            records(t, 1)
+        records(t, 2)
+        weave(compare(t, 0))
+        if t == 0: coded()
+        else: pieces(t - 1, 1)
+        records(t, 3)
+        weave(compare(t, 1))
+        if t == 0: records(t, 4)
+        weave(compare(t, 2))
+        handler(t, 0)
+        taken(t, 0)
+        if t: records(t, 4)
+        weave(compare(t, 3))
+        cp(b("UI", 0, 32), b("UU", 0, 32))
+        weave(lists(t, 0), *([] if last else [changed(t, 0)]))
+        differences(t, 4)
+        records(t, 5)
+        piece(t, 0)
+        lengths(t, 0)
+        signs(4)
+        differences(t, 5)
+        weave(compare(t, 4))
+        signs(5)
+        weave(stack(t, 0))
+        mark(t, 0)
+        if not last: halves()
+        weave(compare(t, 5))
+        handler(t, 1)
+        taken(t, 1)
+        if not last: cp(scattered(xall, w("xl", 0)), b("NB"))
+        weave(stored(t, 0))
+        pieces(t, 0)
+        cp(b("UI", 32, 48), b("UU", 0, 16))
+        weave(lists(t, 1), *([] if last else [table()]))
+        piece(t, 1)
+        lengths(t, 1)
+        mark(t, 1)
+        if not last:
+            unhandled()
+            cp(scattered(xall, w("xl", 1)), b("XH"))
+        else:
+            weave(stored(t, 1), stack(t, 1))
+            pieces(t, 1)
 
     for s in SEMAPHORES:
         if total[s]: g.wait_ge(T.sem[s], total[s])

@@ -3,9 +3,18 @@ from concourse.mybir import AluOpType, AxisListType, ActivationFunctionType
 ROUNDS, STEP, K, NREC = 3, 3, 512, 8192
 H = 256
 PARTS = [(0, H), (H, K)]
-EDGES = [0, 64, 160, 256, 352, 448, 512]
+EDGES = [0, 64, 160, 256, 384, 448, 512]
 CHUNKS = list(zip(EDGES[:-1], EDGES[1:]))
-SIGNS = [0, 0, 0, 0, 4, 4]
+BATCH = [(4, 1, 9), (5, 1, 9)]
+SIGNS = [max([1] + [s1 for c, s0, s1 in BATCH if c == ci]) - 1 for ci in range(len(CHUNKS))]
+SHARE = 48
+ONV = [False, False]
+EARLY = 12
+AHEAD = 8
+LOW = 2
+FIRST = "r0 c0 r1 c1 r2 C0 v0 v1 m2 c2 v2 r3 m0 j0 B1 Y1 m1 r4 d0 h0+c3 g0 t0 m4 u0 l0+x0+c4 p0 v3 r5 o0 s0 d1 m5 c5 n0 v4 s1 m3 v5 j1 f0 k0 h1 g1 a0 t1"
+ORDER = "z0' w0' u1' e0'+x1'+l1' p1' q0' o1' f1' N0' w1' e1' a1' n1' z1' R1 r0 c0 r1 r2 k1'+c1 m2 v0 q1' c2 v1 m1 m0 v2 h0 B2' r3 g0 c3 t0 u0 r4 l0+x0 v3 d0 r5 d1 c4 p0 c5 m4 n0 o0 m5 s1 s0 m3 v5 a0 f0 v4 k0+h1 g1 t1"
+LAST = "z0' e0' u1' x1'+l1' o1' a1' f1' w0' N0' p1' w1' n1' e1'+k1' z1' r0 r1 R1 c0+c1 r2 v1 m0 r3 c2 r4 v0 m1 m2 v2 d0 h0+c3 g0 m3 t0 q0' q1' r5 u0 l0+c4 p0 m4 v3 d1 m5 c5 n0 s0 v4 a0 k0 s1 z0 v5 h1 e0 g1 t1 q0 u1 a1 l1 p1 e1 z1 n1 q1 k1"
 VOTE = 4096.0
 FAR = 1 << 20
 DEAD = 16384
@@ -27,28 +36,28 @@ SCRATCH = {
     "PW0": ("sbuf", [128, TOFF + K], "float32"), "PW1": ("sbuf", [128, TOFF + K], "float32"),
     "ZM0": ("sbuf", [128, 2 * H], "bfloat16"), "ZM1": ("sbuf", [128, 2 * H], "bfloat16"),
     "AG": ("sbuf", [128, K], "bfloat16"), "OA": ("sbuf", [128, K], "float32"),
-    "OX": ("sbuf", [128, H], "bfloat16"), "NF": ("sbuf", [128, H], "float32"), "NB": ("sbuf", [128, H], "bfloat16"),
-    "XS": ("sbuf", [128, H], "int32"), "XH": ("sbuf", [128, H], "int32"),
+    "OX": ("sbuf", [128, K], "bfloat16"), "NF": ("sbuf", [128, K], "float32"), "NB": ("sbuf", [128, K], "bfloat16"),
+    "XS": ("sbuf", [128, K], "int32"), "XH": ("sbuf", [128, K], "int32"),
     "PB": ("sbuf", [128, K], "float32"), "SG": ("sbuf", [128, K], "bfloat16"), "TY": ("sbuf", [128, K], "int32"),
     "CI32": ("sbuf", [128, K], "int32"), "CN": ("sbuf", [128, K], "int32"), "SF": ("sbuf", [128, K], "bfloat16"),
     "FO": ("sbuf", [128, K], "float32"), "FC": ("sbuf", [128, K], "float32"), "FN": ("sbuf", [128, K], "float32"),
-    "E": ("sbuf", [128, 128], "float32"), "ONE": ("sbuf", [128, 128], "float32"),
-    "KC": ("sbuf", [128, 1], "float32"), "RC": ("sbuf", [128, 1], "float32"), "R16": ("sbuf", [128, 1], "float32"),
-    "TA": ("sbuf", [128, 128], "float32"), "TB": ("sbuf", [128, 32], "float32"), "GB": ("sbuf", [128, 8], "bfloat16"),
-    "TC": ("sbuf", [128, 128], "float32"), "TD": ("sbuf", [128, 128], "float32"),
+    "ONE": ("sbuf", [128, 128], "float32"), "ST1": ("sbuf", [128, K], "int32"), "ST2": ("sbuf", [128, K], "int32"),
+    "KC": ("sbuf", [128, 1], "int32"), "KD": ("sbuf", [128, 1], "int32"), "RC": ("sbuf", [128, 1], "float32"), "R16": ("sbuf", [128, 1], "float32"),
+    "RN": ("sbuf", [128, 1], "float32"), "TN": ("sbuf", [128, 128], "float32"), "TA": ("sbuf", [128, 128], "float32"), "TB": ("sbuf", [128, 32], "float32"), "GB": ("sbuf", [128, 8], "bfloat16"),
     "ID": ("sbuf", [128, 128], "bfloat16"), "ND": ("sbuf", [128, 128], "bfloat16"), "I16": ("sbuf", [128, 128], "bfloat16"),
     "I32": ("sbuf", [128, 128], "bfloat16"), "I256": ("sbuf", [128, 128], "bfloat16"), "IT": ("sbuf", [128, 128], "bfloat16"),
-    "ONB": ("sbuf", [128, 128], "bfloat16"), "CS": ("sbuf", [128, 128], "bfloat16"),
+    "ONB": ("sbuf", [128, 128], "bfloat16"),
     "BQ": ("sbuf", [128, 144], "bfloat16"), "BN": ("sbuf", [128, 144], "bfloat16"), "BV": ("sbuf", [128, 144], "bfloat16"),
     "BM": ("sbuf", [128, 144], "bfloat16"), "BW": ("sbuf", [128, 144], "float16"),
-    "GA": ("sbuf", [128, 128], "bfloat16"), "MK": ("sbuf", [128, 16 * 96], "bfloat16"),
+    "GA": ("sbuf", [128, 128], "bfloat16"), "MK": ("sbuf", [128, 16 * max(c[1] - c[0] for c in CHUNKS)], "bfloat16"),
     "CI": ("sbuf", [128, H], "float32"), "CAP": ("sbuf", [128, H], "float32"),
     "LI": ("sbuf", [128, 32], "float32"), "LJ": ("sbuf", [128, 32], "float32"), "LT": ("sbuf", [128, 128], "float32"),
     "KI": ("sbuf", [128, 32], "float32"), "K16": ("sbuf", [128, 32], "float32"), "KH": ("sbuf", [128, 16], "float32"),
     "KF": ("sbuf", [128, 32], "float16"), "KY": ("sbuf", [128, 16], "float16"),
     "ACOL": ("sbuf", [128, 1], "float32"), "AJ": ("sbuf", [128, 32], "float32"),
 }
-BANKS = ["VT0", "VT1", "UU", "VV", "LS", "SA", "CC", "DD"]
+for _n in set(SIGNS) - {0}: SCRATCH["CS%d" % _n] = ("sbuf", [128, 8, 16], "bfloat16")
+BANKS = ["VT0", "VT1", "UU", "LS", "SA", "CC", "DD0", "DD1"]
 for _n in BANKS:
     SCRATCH[_n] = ("psum", [128, K], "float32")
 for _t in range(3):
@@ -69,7 +78,7 @@ SCRATCH["UI"] = ("sbuf", [128, 64], "int32")
 SCRATCH["UM"] = ("sbuf", [128, 64], "int32")
 SCRATCH["L3"] = ("sbuf", [128, 96], "uint16")
 
-LOADS = ["STKa", "STKb", "X", "Z0", "WI", "LN8", "BAS", "CON", "D00", "D01"]
+LOADS = ["STKa", "STKb", "X", "Z0", "WI", "LN8", "BAS", "CON", "D00", "D01", "ST10", "ST11", "ST20", "ST21"]
 ARR = ["%s%d%d" % (n, t, p) for n in ("SU", "D", "Z") for t in (1, 2) for p in (0, 1)] + ["BA1", "BA2"]
 SEMAPHORES = (["sV", "sA", "sP", "sG", "local", "dY0", "dY1", "out"]
               + ["ld" + n for n in LOADS] + ["ar" + n for n in ARR])
@@ -123,7 +132,7 @@ def rank_program(g, core, T, topo):
         reads = [x for i in ins for x in i[1]]
         writes = list(out[1])
         for x in out[2:]: reads += x
-        await_deps(q, reads, writes, own_waw)
+        await_deps(q, reads, writes, q != "P")
         sem = "s" + q
         total[sem] += 1
         fn().then_inc(T.sem[sem], 1)
@@ -162,8 +171,8 @@ def rank_program(g, core, T, topo):
         else:
             run("V", lambda: g.vector.tensor_scalar(out[0], a[0], v1, v2, o1, o2), out, ins, waw)
 
-    def cp(out, a, waw=False):
-        run("V", lambda: g.vector.tensor_copy(out[0], a[0]), out, [a], waw)
+    def cp(out, a):
+        run("V", lambda: g.vector.tensor_copy(out[0], a[0]), out, [a], True)
 
     def scan(out, a, c, o1, o2):
         run("V", lambda: g.vector.tensor_tensor_scan(out[0], a[0], c[0], 0.0, o1, o2), out, [a, c])
@@ -218,58 +227,63 @@ def rank_program(g, core, T, topo):
         arrives("BA%d" % t, 0, K, ring(-t), "BA%d" % t)
 
     first = EDGES[2]
+    dma("A", b("LN8", p1=8), (T.ln[:, :], []), "ldLN8")
+    dma("A", b("WI"), (T.w[:, :], []), "ldWI")
     dma("S", b("STK", 0, first), (T.stk[:, 0:first], []), "ldSTKa")
     dma("S", b("X"), (T.xt[:, :], []), "ldX")
     dma("S", b("STK", first, K), (T.stk[:, first:K], []), "ldSTKb")
     dma("S", b("Z0", 0, K), (T.z[:, :], []), "ldZ0")
-    dma("A", b("LN8", p1=8), (T.ln[:, :], []), "ldLN8")
-    dma("A", b("WI"), (T.w[:, :], []), "ldWI")
+    for p, (l0, l1) in enumerate(PARTS): dma("S", (T["D0%d" % p][:, :], [("D0%d" % p, 0, H)]), (T.stk[:, l0:l1], []), "ldD0%d" % p)
     dma("S", b("CON"), (T.con[:, :], []), "ldCON")
     dma("S", b("BAS"), (T.bas[:, :], []), "ldBAS")
-    for p, (l0, l1) in enumerate(PARTS): dma("S", (T["D0%d" % p][:, :], [("D0%d" % p, 0, H)]), (T.stk[:, l0:l1], []), "ldD0%d" % p)
 
     def yall(p, lo, hi):
         return (T["Y%d" % p][:, lo:hi], [("Y%d" % p, 0, 64)])
 
-    def shifts(t, p):
+    def shifts(t, p, rows=range(16)):
         Y, D = "Y%d" % p, "D%d%d" % (t, p)
-        if t: await_deps("S", [("D%d1" % t, 0, H)], [], False)
-        for q in range(16):
-            dma("S", (T[Y][q::16, (15 - q) * H:(31 - q) * H], [(Y, 4 * q, 4 * q + 1)]), (T[D][:, :], [(D, 0, H), (Y + "f", 0, 2)]), "d" + Y)
-        if t == 0:
-            for q in range(13):
-                dma("S", (T[Y][q::16, 2 * H:(15 - q) * H], [(Y, 4 * q + 2, 4 * q + 3)]), (T[D][0:8 * (13 - q), :], [(D, 0, H)]), "d" + Y)
+        if rows.start:
+            await_deps("S", [("D%d1" % t if t else "D10", 0, H)], [], False)
+        elif t: dma("S", b("ST%d" % t, *PARTS[p]), (T[D][:, :], [(D, 0, H)]), "ldST%d%d" % (t, p))
+        for q in rows:
+            dma("S", (T[Y][q::16, (15 - q) * H:(31 - q) * H], [(Y, 4 * q, 4 * q + 1)]), (T[D][:, :], [(D, 0, H), (Y + "f", 0, 3)]), "d" + Y)
+        if t == 0 and p == 1 and rows.start == 0:
+            for q in range(15 - LOW):
+                dma("S", (T[Y][q::16, LOW * H:(15 - q) * H], [(Y, 4 * q + 2, 4 * q + 3)]), (T[D][0:8 * (15 - LOW - q), :], [(D, 0, H)]), "d" + Y)
 
     fill(b("ONE"), 1.0)
-    iota(b("KC", p1=16), [[0, 1]], 0, 1)
-    select(b("E", p1=16), b("ONE", p1=16), [[0, 8], [-1, 16]], op.is_equal, 0.0, 0, 1)
-    mm(b("UU", 0, 1), b("E", p1=16), b("KC", p1=16), True, True)
+    iota(b("KC"), [[0, 1]], 0, 1, False)
     select(b("TA"), b("ONE"), [[-1, 128]], op.is_equal, 0.0, 0, 1)
     select(b("TB", 0, 9), b("ONE", 0, 9), [[-16, 9]], op.is_ge, 0.0, 0, 1)
     select(b("TB", 16, 25), b("TB", 0, 9), [[16, 9]], op.is_ge, 0.0, 15, -1)
     iota(b("KI"), [[16, 32]], 0, 0)
     iota(b("LI"), [[1, 32]], 0, 0)
     iota(b("CI"), [[256, 16], [-1, 16]], 15 - 8 * int(VOTE), 0)
-    select(b("TC", p1=8), b("ONE", p1=8), [[1, 128]], op.is_ge, 0.0, 0, -16)
-    select(b("TD", p1=8), b("TC", p1=8), [[-1, 128]], op.is_ge, 0.0, 15, 16)
-    iota((T.Y0[:, 16 * H + YV:31 * H], [("Y0f", 0, 1)]), [[0, 15 * H - YV]], FAR, 0, False)
-    iota((T.Y1[:, 16 * H:31 * H], [("Y1f", 0, 1)]), [[0, 15 * H]], FAR, 0, False)
+    def far(p, i, lo, hi):
+        if hi > lo: iota((T["Y%d" % p][:, lo:hi], [("Y%df" % p, i, i + 1)]), [[0, hi - lo]], FAR, 0, False)
+
+    far(0, 0, 16 * H + YV, 31 * H)
+    far(0, 1, 2 * H, 15 * H)
+    far(1, 0, 16 * H, 31 * H)
+    ts(b("KD"), b("KC"), 15, op.bitwise_and)
     fill(b("BQ"), 0.0)
     fill(b("MK"), 1.0)
-    fill(b("CS"), 0.0)
+    for n in set(SIGNS) - {0}: fill((T["CS%d" % n][:, :, :], [("CS%d" % n, 0, 1)]), 0.0)
     fill(b("RB", 8192, 8224), 0.0)
     fill(b("MK", 0, None, 16), 0.0, True)
-    cp(b("RC"), b("UU", 0, 1))
+    cp(b("RC"), b("KD"))
     fill((T.GE[:, :, :, 0], [("GE0", 0, K)]), 1.0)
-    for s in range(1, max(SIGNS) + 1): fill(b("CS", s, None, 16), 8 * VOTE, True)
-    cp(b("BQ", 15, 144, 16), b("TB", 16, 25), True)
-    for name, scale in (("ID", 1.0), ("ND", -1.0), ("I16", H / 4096.0), ("I32", 32.0), ("I256", 256.0), ("IT", float(TOFF))):
+    for n in set(SIGNS) - {0}: fill((T["CS%d" % n][:, :, 1:n + 1], [("CS%d" % n, 0, 1)]), 8 * VOTE, True)
+    cp(b("BQ", 15, 144, 16), b("TB", 16, 25))
+    for name, scale in (("ID", 1.0), ("ND", -1.0), ("TN", -1.0), ("I16", H / 4096.0), ("I32", 32.0), ("I256", 256.0), ("IT", float(TOFF))):
         ac(b(name), b("TA"), scale=scale)
     for name, scale in (("BN", -VOTE), ("BV", 1024.0), ("BM", H / 2.0)): ac(b(name), b("BQ"), scale=scale)
     ac(b("ONB"), b("ONE"), scale=1.0 / 128.0)
     ac(b("GB"), b("TB", 16, 24))
-    ac(b("GA", p1=8), b("TD", p1=8))
+    mm(b("UU", 0, 128, p1=8), b("GB"), b("ID"), True, True)
+    ac(b("GA", p1=8), b("UU", 0, 128, p1=8))
     ts(b("R16"), b("RC"), 16.0, op.mult)
+    ts(b("RN"), b("RC"), -1.0, op.mult, -0.5, op.add)
     cp(b("SU0", 0, first), b("STK", 0, first))
     ts(b("KF"), b("KI"), b("RC"), op.add)
     ts(b("LJ"), b("LI"), b("RC"), op.is_gt)
@@ -281,25 +295,32 @@ def rank_program(g, core, T, topo):
         ts(b("LT", 32 * t + 32, 32 * t + 64), b("LJ"), float(DEAD - (t + 3) * FAR), op.mult, float(FAR), op.add)
     ts(b("KH"), b("K16", 0, 16), -1.0 - 8 * VOTE, op.add)
     for n in ("PW0", "PW1"): fill(b(n, K, TOFF), float(FAR))
-    cp(b("WF"), b("WI"))
     cp(b("LNB", p1=8), b("LN8", p1=8))
-    ts(b("BW"), b("BQ"), b("WF"), op.mult)
     mm(b("SA"), b("GA", p1=8), b("LNB", p1=8), True, True)
-    fill((T.Y0[:, 16 * H:16 * H + YV], [("Y0f", 1, 2)]), FAR)
+    run("A", lambda: g.scalar.activation(T.SG[:, :], T.SA[:, :], act.Sign, bias=T.RN[:, :]), b("SG"), [b("SA"), b("RN")])
+    for n in ("DD0", "LX"): ac(b(n), b("SG"), act.Identity, scale=-FAR / 2.0, bias=DEAD - FAR / 2.0)
+    fill((T.Y0[:, 16 * H:16 * H + YV], [("Y0f", 2, 3)]), FAR)
     shifts(0, 0)
-    shifts(0, 1)
+
+    def second(t, p):
+        far(1, 1, 2 * H, LOW * H)
+        shifts(0, 1, range(EARLY))
 
     def coded():
-        ts(b("LX"), b("SA"), b("RC"), op.is_gt, -float(FAR), op.mult)
-        ts(b("CC"), b("CON"), float(DEAD), op.add)
+        cp(b("WF"), b("WI"))
+        tt(b("PW0", 0, K), b("CON"), b("DD0"), op.add)
+        ts(b("BW"), b("BQ"), b("WF"), op.mult)
         ts(b("BA0"), b("BAS"), float(BASE), op.add)
-        tt(b("PW0", 0, K), b("LX"), b("CC"), op.add)
-        for n in (1, 2): send(b("BA0"), T["BA%d" % n][:, :], "BA%d" % n, ring(n))
+
+    def names(t, p):
+        mms(b("CC", *PARTS[p]), [(b("TA"), b("PW0", *PARTS[p])), (b("TN"), b("LX", *PARTS[p]))])
+
+    def bases(t, n):
+        send(b("BA0"), T["BA%d" % n][:, :], "BA%d" % n, ring(n))
 
     xall = b("X")
 
-    def records(t, ci, on="A"):
-        l0, l1 = CHUNKS[ci]
+    def records(t, l0, l1, on="A"):
         (ac if on == "A" else cp)(b("RB", 16 * l0 + 15, 16 * l1 + 15), ind(xall, b("SU%d" % t, l0, l1)))
 
     def row(ci, i):
@@ -311,43 +332,55 @@ def rank_program(g, core, T, topo):
         ap = T.GE[:, l0 // 16:l1 // 16, :, s0:s1] if r is None else T.GE[:, l0 // 16:l1 // 16, r, s0:s1]
         return (ap, [("GE%d" % s, l0, l1) for s in range(s0, s1)])
 
-    def differences(t, ci):
+    def differences(t, i):
+        ci, s0, s1 = BATCH[i]
         l0, l1 = CHUNKS[ci]
-        n = SIGNS[ci]
-        for s in range(1, n + 1):
-            mms(b("DD", s - 1, n * (l1 - l0), n), [(b("ID"), row(ci, 16 - s)), (b("ND"), b("Z%d" % t, l0, l1))])
+        for s in range(s0, s1):
+            mms(b("DD%d" % (i % 2), s - s0, (s1 - s0) * (l1 - l0), s1 - s0), [(b("ID"), row(ci, 16 - s)), (b("ND"), b("Z%d" % t, l0, l1))])
 
-    def signs(ci):
+    def signs(t, i):
+        ci, s0, s1 = BATCH[i]
         l0, l1 = CHUNKS[ci]
-        n = SIGNS[ci]
-        if n: ac(slots(ci, 1, n + 1), b("DD", 0, n * (l1 - l0)), act.Sign, bias=0.5)
+        ac(slots(ci, s0, s1), b("DD%d" % (i % 2), 0, (s1 - s0) * (l1 - l0)), act.Sign, bias=0.5)
 
-    def compare(t, ci, between=None):
+    def compare(t, ci):
         l0, l1 = CHUNKS[ci]
         for s in range(SIGNS[ci] + 1, 16):
             tt((T.GE[:, l0 // 16:l1 // 16, :, s], [("GE%d" % s, l0, l1)]), row(ci, 16 - s), b("Z%d" % t, l0, l1), op.is_ge)
             yield 1
-        p = l0 // H
-        level = [(b("ND"), b("CS", 0, l1 - l0))] if SIGNS[ci] else []
+
+    def votes(t, ci):
+        l0, l1 = CHUNKS[ci]
+        p, n = l0 // H, SIGNS[ci]
+        level = [(b("ND"), (T["CS%d" % n][:, 0:(l1 - l0) // 16, :], [("CS%d" % n, 0, 1)]))] if n else []
         mms(b("VT%d" % p, l0 - p * H, l1 - p * H), level + [(b("BN", 15 - r, 143 - r), slots(ci, 0, 16, r)) for r in range(16)])
-        if between: weave(between)
+
+    def maxima(t, ci):
+        l0, l1 = CHUNKS[ci]
         scan(b("PM", 16 * l0, 16 * l1), b("MK", 0, 16 * (l1 - l0)), b("RB", 16 * l0 + 15, 16 * l1 + 15), op.mult, op.max)
-        yield 1
 
     def handler(t, p):
         l0, l1 = PARTS[p]
         scan(b("OA", l0, l1), b("VT%d" % p, 0, H), b("CAP"), op.min, op.max)
+        yield 1
         end = b("OA", l0 + 15, l1, 16)
         ts(w("ml", p), end, 8 * VOTE, op.add)
         tt(w("h", p), end, b("KH"), op.subtract)
+        yield 1
 
-    def taken(t, p):
+    def greatest(t, p):
         l0, l1 = PARTS[p]
         ac(b("ZM%d" % p, H, 2 * H), ind(b("PM", 16 * l0, 16 * l1), w("ml", p)))
         mms(b("UU", 0, 16), wrap("BW", "ZM%d" % p, H, 2 * H))
+
+    def taken(t, p):
+        l0, l1 = PARTS[p]
         ac(b("AG", l0, l1), ind(b("RB", 16 * l0 + 16, 16 * l1 + 16), w("ml", p)))
-        mms(b("VV", 0, 16) if p else b("UU", 16, 32), wrap("BV", "AG", l0, l1))
+        mms(b("LS", 128, 144) if p else b("UU", 16, 32), wrap("BV", "AG", l0, l1))
         mms(b("SA", 0, H), [(b("ID"), b("AG", l0, l1)), (b("ND"), b("Z%d" % t, l0, l1))])
+
+    def sums(t, p):
+        cp(b("UI", 32 * p, 48 if p else 32), b("UU", 0, 16 if p else 32))
 
     def changed(t, p):
         o = 32 * p
@@ -364,7 +397,7 @@ def rank_program(g, core, T, topo):
         ts(w("un", p), w("h", p), 16.0, op.is_ge, 4096.0, op.mult)
         yield 1
         if p:
-            cp(b("UI", 48, 64), b("VV", 0, 16))
+            cp(b("UI", 48, 64), b("LS", 128, 144))
             yield 1
         ts(b("UM", o, o + 32), b("UI", o, o + 32), 4095, op.bitwise_and)
         yield 1
@@ -389,9 +422,11 @@ def rank_program(g, core, T, topo):
         l0, l1 = PARTS[p]
         tt(b("PB", l0, l1), ind(b("PW%d" % (t % 2), 0, TOFF), w("jl", p)), b("BA%d" % t, l0, l1), op.min)
 
+    def distance(t, p):
+        ac(b("ZM%d" % p, 0, H), b("SA", 0, H), act.Abs)
+
     def mark(t, p):
         l0, l1 = PARTS[p]
-        ac(b("ZM%d" % p, 0, H), b("SA", 0, H), act.Abs)
         ac(b("ZO%d" % t, l0, l1), ind(b("ZM%d" % p), b("L3", 48 * p, 48 * p + 16)))
         if t < ROUNDS - 1: send(b("ZO%d" % t, l0, l1), T["Z%d" % (t + 1)][:, l0:l1], "Z%d%d" % (t + 1, p), ring(1))
         else: dma("S", (T.yz[:, l0:l1], []), b("ZO%d" % t, l0, l1), "out")
@@ -415,6 +450,12 @@ def rank_program(g, core, T, topo):
             cp(b("UO%d" % t, l0, l1), sn)
             send(b("UO%d" % t, l0, l1), T["SU%d" % (t + 1)][:, l0:l1], "SU%d%d" % (t + 1, p), ring(1))
             send(sn, T["D%d%d" % (t + 1, p)][:, :], "D%d%d" % (t + 1, p), ring(1))
+            if p == 0:
+                if t == 0 and EARLY < 16: shifts(0, 1, range(EARLY, 16))
+                shifts(t + 1, 0, range(AHEAD))
+            else:
+                shifts(t + 1, 0, range(AHEAD, 16))
+                shifts(t + 1, 1)
         else:
             cp(b("FO", l0, l1), sn)
             dma("S", (T.ys[:, l0:l1], []), b("FO", l0, l1), "out")
@@ -423,7 +464,7 @@ def rank_program(g, core, T, topo):
     def stored(t, p):
         l0, l1 = PARTS[p]
         new = b("PW%d" % (t % 2), TOFF + l0, TOFF + l1)
-        tt(new, ind(b("LT"), b("L3", 48 * p + 16, 48 * p + 32)), yall(p, 15 * H, 16 * H), op.add)
+        tt(new, ind(b("LT"), b("L3", 48 * p + 16, 48 * p + 32)), b("ST%d" % t if t else "STK", l0, l1), op.add)
         yield 1
         tt(b("CC", l0, l1) if t < ROUNDS - 1 else b("CI32", l0, l1), new, b("CC", l0, l1), op.min)
         yield 1
@@ -444,77 +485,56 @@ def rank_program(g, core, T, topo):
             ac(b("FN", l0, l1, p1=8), b("SA", H, 2 * H, p1=8), act.Identity, bias=8.0, scale=-0.5)
             dma("S", (T.yn[:, l0:l1], []), b("FN", l0, l1, p1=8), "out")
 
-    def halves():
-        ac(b("OX"), ind(xall, w("xl", 0)))
-        mms(b("SA", H, 2 * H), [(b("ID"), b("ZM0", H, 2 * H)), (b("ID"), b("OX"))])
-        ac(b("NF"), b("SA", H, 2 * H), act.Identity, bias=WHOLE, scale=0.5 - 1.0 / 2048.0)
-        ac(b("NB"), b("NF"), act.Identity, bias=-WHOLE)
+    def old(t, p):
+        if ONV[p]: return
+        ac(b("OX", *PARTS[p]), ind(xall, w("xl", p)))
+        mms(b("SA", H, 2 * H), [(b("ID"), b("ZM%d" % p, H, 2 * H)), (b("ID"), b("OX", *PARTS[p]))])
 
-    def table():
-        yield from changed(0, 1)
-        tt(b("XS"), ind(xall, w("xl", 1)), b("ZM1", H, 2 * H), op.add)
+    def halves(t, p):
+        if ONV[p]: return
+        ac(b("NF", *PARTS[p]), b("SA", H, 2 * H), act.Identity, bias=WHOLE, scale=0.5 - 1.0 / 2048.0)
+        ac(b("NB", *PARTS[p]), b("NF", *PARTS[p]), act.Identity, bias=-WHOLE)
+
+    def table(t, p):
+        yield from changed(t, p)
+        if not ONV[p]: return
+        tt(b("XS", *PARTS[p]), ind(xall, w("xl", p)), b("ZM%d" % p, H, 2 * H), op.add)
         yield 1
-        ts(b("XH"), b("XS"), 1, op.arith_shift_right)
+        ts(b("XH", *PARTS[p]), b("XS", *PARTS[p]), 1, op.arith_shift_right)
         yield 1
 
     def unhandled():
-        mm(b("SA", 0, 32), b("ONB"), w("un"), True, True)
-        ac(b("AJ"), b("SA", 0, 32), act.Identity, total_in=b("ACOL"), bias=NOP / 32.0)
+        mm(b("LS", 96, 128), b("ONB"), w("un"), True, True)
+        ac(b("AJ"), b("LS", 96, 128), act.Identity, total_in=b("ACOL"), bias=NOP / 32.0)
 
-    for t in range(ROUNDS):
-        last = t == ROUNDS - 1
-        if t == 0:
-            records(t, 1)
-            records(t, 0, "V")
+    def gather(t, ci):
+        l0, l1 = CHUNKS[ci]
+        if t or ci > 1: records(t, l0 + (SHARE if ci == 1 else 0), l1)
+        elif ci == 0:
+            records(t, *CHUNKS[1])
+            records(t, l0, l1, "V")
             cp(b("SU0", first, K), b("STK", first, K))
-        else:
-            records(t, 0)
-            weave(stack(t - 1, 1), stored(t - 1, 1))
-            shifts(t, 0)
-            shifts(t, 1)
-            records(t, 1)
-        records(t, 2)
-        weave(compare(t, 0))
-        if t == 0: coded()
-        else: pieces(t - 1, 1)
-        records(t, 3)
-        weave(compare(t, 1))
-        if t == 0: records(t, 4)
-        weave(compare(t, 2))
-        handler(t, 0)
-        taken(t, 0)
-        if t: records(t, 4)
-        weave(compare(t, 3))
-        cp(b("UI", 0, 32), b("UU", 0, 32))
-        weave(lists(t, 0), *([] if last else [changed(t, 0)]))
-        differences(t, 4)
-        records(t, 5)
-        piece(t, 0)
-        lengths(t, 0)
-        signs(4)
-        differences(t, 5)
-        weave(compare(t, 4))
-        signs(5)
-        weave(stack(t, 0))
-        mark(t, 0)
-        if not last: halves()
-        weave(compare(t, 5))
-        handler(t, 1)
-        taken(t, 1)
-        if not last: cp(scattered(xall, w("xl", 0)), b("NB"))
-        weave(stored(t, 0))
-        pieces(t, 0)
-        cp(b("UI", 32, 48), b("UU", 0, 16))
-        weave(lists(t, 1), *([] if last else [table()]))
-        piece(t, 1)
-        lengths(t, 1)
-        mark(t, 1)
-        if not last:
-            unhandled()
-            cp(scattered(xall, w("xl", 1)), b("XH"))
-        else:
-            weave(stored(t, 1), stack(t, 1))
-            pieces(t, 1)
+
+    def share(t, ci):
+        if t and SHARE: records(t, EDGES[1], EDGES[1] + SHARE, "V")
+
+    steps = {"r": gather, "R": share, "c": compare, "v": votes, "m": maxima, "d": differences, "s": signs,
+             "h": handler, "g": greatest, "t": taken, "u": sums, "l": lists, "p": piece, "n": lengths, "a": distance, "z": mark,
+             "k": stack, "e": stored, "q": pieces}
+    inner = {"x": table, "o": old, "f": halves, "N": lambda t, p: unhandled(),
+             "w": lambda t, p: cp(scattered(xall, w("xl", p)), b("XH" if ONV[p] else "NB", *PARTS[p]))}
+
+    once = {"C": lambda t, p: coded(), "j": names, "B": bases, "Y": second}
+
+    def issue(order, t):
+        for group in order.split():
+            todo = []
+            for name in group.split("+"):
+                tt_ = t - name.count("'")
+                todo.append({**steps, **inner, **once}[name[0]](tt_, int(name[1])))
+            weave(*[s for s in todo if s])
+
+    for t in range(ROUNDS): issue((FIRST, ORDER, LAST)[t], t)
 
     for s in SEMAPHORES:
         if total[s]: g.wait_ge(T.sem[s], total[s])

@@ -3,18 +3,23 @@ from concourse.mybir import AluOpType, AxisListType, ActivationFunctionType
 ROUNDS, STEP, K, NREC = 3, 3, 512, 8192
 H = 256
 PARTS = [(0, H), (H, K)]
-EDGES = [0, 64, 160, 256, 384, 448, 512]
+EDGES = [0, 64, 160, 256, 352, 448, 512]
 CHUNKS = list(zip(EDGES[:-1], EDGES[1:]))
-BATCH = [(4, 1, 9), (5, 1, 9)]
-SIGNS = [max([1] + [s1 for c, s0, s1 in BATCH if c == ci]) - 1 for ci in range(len(CHUNKS))]
-SHARE = 48
-ONV = [False, False]
-EARLY = 12
-AHEAD = 8
-LOW = 2
-FIRST = "r0 c0 r1 c1 r2 C0 v0 v1 m2 c2 v2 r3 m0 j0 B1 Y1 m1 r4 d0 h0+c3 g0 t0 m4 u0 l0+x0+c4 p0 v3 r5 o0 s0 d1 m5 c5 n0 v4 s1 m3 v5 j1 f0 k0 h1 g1 a0 t1"
-ORDER = "z0' w0' u1' e0'+x1'+l1' p1' q0' o1' f1' N0' w1' e1' a1' n1' z1' R1 r0 c0 r1 r2 k1'+c1 m2 v0 q1' c2 v1 m1 m0 v2 h0 B2' r3 g0 c3 t0 u0 r4 l0+x0 v3 d0 r5 d1 c4 p0 c5 m4 n0 o0 m5 s1 s0 m3 v5 a0 f0 v4 k0+h1 g1 t1"
-LAST = "z0' e0' u1' x1'+l1' o1' a1' f1' w0' N0' p1' w1' n1' e1'+k1' z1' r0 r1 R1 c0+c1 r2 v1 m0 r3 c2 r4 v0 m1 m2 v2 d0 h0+c3 g0 m3 t0 q0' q1' r5 u0 l0+c4 p0 m4 v3 d1 m5 c5 n0 s0 v4 a0 k0 s1 z0 v5 h1 e0 g1 t1 q0 u1 a1 l1 p1 e1 z1 n1 q1 k1"
+BATCH = [(4, 1, 6), (5, 1, 9)]
+USED = [2, 2, 2]
+SIGNS = [max([1] + [s1 for c, s0, s1 in BATCH[:n] if c == ci]) - 1 for ci in range(len(CHUNKS)) for n in USED]
+SHARE = [(1, 64, 96), (1, 64, 112), (1, 64, 96)]
+DIRECT = True
+GCP = False
+FINE = 32
+SECTIONS = [[(0, 256), (256, 512)], [(0, 256), (256, 512)], [(0, 256), (256, 512)]]
+ONV = [2]
+ONA = [[1], [1], [1]]
+NOST = True
+LOW = 6
+FIRST = "S0 V0. G0 V0.34 Y1 A0.10 P0. A0. V0 U0 P0 A0 R0 C0. i1 i0 r0 y0 m0 c0 m1. C0.2 r2 c2.10 i2 m2. r1 c1 c2 r3 c3.5 j0 m1 m3 i3 v0 v1 v2 r5 i7 d1 h0. c3.3 h0 t0 i5 r4 d0 i4 l0. c5.5 m2 c5 m5. c4.5 g0 c3.4 m4. s1 i6 u0 c3. l0. c3 l0.3 x0. c4.2 v5 s0 l0.4 c4 l0. m5 l0 v3 v4 x0. n0 C0 x0 m4 z0 h1 p0 o0 k0. l1. k0. g1 e0. k0. t1.3 u1 k0 x1. f0 l1. x1. l1. x1 l1.8 i3.3^ i0.3^ w0 l1 q0 o1 t1 f1 w1 N0. z1. n1 B1 z1 p1"
+ORDER = "R0 k1.3' y0. r2 c2. k1' m1. c2 i3 r0 c0 m0 i1 r1 c1 y0 m2 r3 m1 c3.6 j1' i2 i0 v2 v0 v1 B2' i6 m3. e0' i5 i7 h0. c3.2 h0 c3 t0. e1.' l0. r4 c4.8 d0 m4. g0 t0 u0 r5 c5.4 l0. m5. l0.3 v3 d1 c5 c4 N0' l0.4 q1' i4 m4. l0. s0 v4 s1 v5 m3 l0 x0. n0 m5 x0. m4 x0 e1' z0 o0 h1 g1 p0 k0. e0. k0. t1.3 u1 k0. x1. k0 l1.2 x1. f0 q0 l1. x1 l1.8 o1 t1 N0. i3.2^ i2^ w0 f1 l1 z1 n1 w1 p1"
+LAST = "r0 R0 k1.' m1. k1.' c0.3 k1.' e0' k1' i1 r1 c0 c1 r2 m0. m1 v1 c2 m2. i0 v0 r5 v2 c5.6 i3 m0 m2. e1.' y0. h0. i4 m2 h0 y0 t0. i7 r3 c3.9 i6 m3.2 i5 e1' g0. d1 t0 g0 l0. u0 m3 l0. r4 c3.2 l0.5 c3 c5 N0' c4 l0.2 m5 l0. d0 v3 s1 m4. l0 v5 s0 q1' v4 e0. m4. n0 z0 e0. h1.2 t1.2 m4 p0 e0. g1 h1 e0 q0 k0. l1.2 t1 k0. u1 l1 e1. n1 z1 q1 p1 e1. k0. e1. k1. e1 k1. k0 k1"
 VOTE = 4096.0
 FAR = 1 << 20
 DEAD = 16384
@@ -22,11 +27,11 @@ BASE = 8192
 NOP = 1 << 26
 TOFF = 528
 WHOLE = 12582912.0
-YV = 3072
+YV = 3840
 
 SCRATCH = {
     "X": ("sbuf", [128, NREC], "bfloat16"),
-    "RB": ("sbuf", [128, NREC + 32], "bfloat16"),
+    "RB": ("sbuf", [128, NREC + 64], "bfloat16"),
     "PM": ("sbuf", [128, NREC], "bfloat16"),
     "GE": ("sbuf", [128, 32, 16, 16], "bfloat16"),
     "Y0": ("sbuf", [128, 31 * H], "int32"), "Y1": ("sbuf", [128, 31 * H], "int32"),
@@ -35,9 +40,9 @@ SCRATCH = {
     "WI": ("sbuf", [128, 1], "int32"), "WF": ("sbuf", [128, 1], "float32"),
     "PW0": ("sbuf", [128, TOFF + K], "float32"), "PW1": ("sbuf", [128, TOFF + K], "float32"),
     "ZM0": ("sbuf", [128, 2 * H], "bfloat16"), "ZM1": ("sbuf", [128, 2 * H], "bfloat16"),
-    "AG": ("sbuf", [128, K], "bfloat16"), "OA": ("sbuf", [128, K], "float32"),
-    "OX": ("sbuf", [128, K], "bfloat16"), "NF": ("sbuf", [128, K], "float32"), "NB": ("sbuf", [128, K], "bfloat16"),
-    "XS": ("sbuf", [128, K], "int32"), "XH": ("sbuf", [128, K], "int32"),
+    "OA": ("sbuf", [128, K], "float32"), "AG": ("sbuf", [128, H], "bfloat16"),
+    "OX": ("sbuf", [128, K], "bfloat16"), "NB": ("sbuf", [128, K], "bfloat16"),
+    "IH": ("sbuf", [128, 128], "float16"), "IR": ("sbuf", [128, 128], "bfloat16"), "ONH": ("sbuf", [128, H], "bfloat16"),
     "PB": ("sbuf", [128, K], "float32"), "SG": ("sbuf", [128, K], "bfloat16"), "TY": ("sbuf", [128, K], "int32"),
     "CI32": ("sbuf", [128, K], "int32"), "CN": ("sbuf", [128, K], "int32"), "SF": ("sbuf", [128, K], "bfloat16"),
     "FO": ("sbuf", [128, K], "float32"), "FC": ("sbuf", [128, K], "float32"), "FN": ("sbuf", [128, K], "float32"),
@@ -49,13 +54,14 @@ SCRATCH = {
     "ONB": ("sbuf", [128, 128], "bfloat16"),
     "BQ": ("sbuf", [128, 144], "bfloat16"), "BN": ("sbuf", [128, 144], "bfloat16"), "BV": ("sbuf", [128, 144], "bfloat16"),
     "BM": ("sbuf", [128, 144], "bfloat16"), "BW": ("sbuf", [128, 144], "float16"),
-    "GA": ("sbuf", [128, 128], "bfloat16"), "MK": ("sbuf", [128, 16 * max(c[1] - c[0] for c in CHUNKS)], "bfloat16"),
+    "GA": ("sbuf", [128, 128], "bfloat16"), "MK": ("sbuf", [128, 16 * FINE], "bfloat16"),
     "CI": ("sbuf", [128, H], "float32"), "CAP": ("sbuf", [128, H], "float32"),
     "LI": ("sbuf", [128, 32], "float32"), "LJ": ("sbuf", [128, 32], "float32"), "LT": ("sbuf", [128, 128], "float32"),
     "KI": ("sbuf", [128, 32], "float32"), "K16": ("sbuf", [128, 32], "float32"), "KH": ("sbuf", [128, 16], "float32"),
     "KF": ("sbuf", [128, 32], "float16"), "KY": ("sbuf", [128, 16], "float16"),
     "ACOL": ("sbuf", [128, 1], "float32"), "AJ": ("sbuf", [128, 32], "float32"),
 }
+for _n in ("XS", "XH"): SCRATCH[_n] = ("sbuf", [128, H], "int32")
 for _n in set(SIGNS) - {0}: SCRATCH["CS%d" % _n] = ("sbuf", [128, 8, 16], "bfloat16")
 BANKS = ["VT0", "VT1", "UU", "LS", "SA", "CC", "DD0", "DD1"]
 for _n in BANKS:
@@ -68,7 +74,7 @@ for _t in range(3):
     SCRATCH["SN%d" % _t] = ("sbuf", [128, K], "int32")
     if _t < 2: SCRATCH["UO%d" % _t] = ("sbuf", [128, K], "uint16")
     for _p in range(2): SCRATCH["D%d%d" % (_t, _p)] = ("dram", [128, H], "int32")
-TILES = {"FW": ("float32", ["xk", "a", "w"]), "IW": ("int32", ["x15", "n", "n2", "j"]), "BT": ("bfloat16", ["h", "un", "pst"]),
+TILES = {"FW": ("float32", ["xk", "a", "w", "zs"]), "IW": ("int32", ["x15", "n", "n2", "j"]), "BT": ("bfloat16", ["h", "un", "pst"]),
          "LU": ("uint16", ["ml", "xl", "jl", "yl"])}
 TILE = {}
 for _b, (_d, _names) in TILES.items():
@@ -128,7 +134,12 @@ def rank_program(g, core, T, topo):
             old = [e for e in hist.get(name, []) if not (not e[2] and e[3] == oq and lo <= e[0] and e[1] <= hi)]
             hist[name] = old + [(lo, hi, False, oq, sem, cnt)]
 
-    def run(q, fn, out, ins, own_waw=False):
+    calls, step = {}, [None]
+
+    def later(q, fn):
+        calls.setdefault(step[0] or (q, 0, 0), []).append(fn)
+
+    def now(q, fn, out, ins):
         reads = [x for i in ins for x in i[1]]
         writes = list(out[1])
         for x in out[2:]: reads += x
@@ -138,11 +149,17 @@ def rank_program(g, core, T, topo):
         fn().then_inc(T.sem[sem], 1)
         note(q, q, reads, writes, sem, total[sem])
 
-    def dma(q, out, in_, sem):
-        await_deps(q, in_[1], out[1], True)
-        total[sem] += 16
-        queue[q].dma_start(out[0], in_[0]).then_inc(T.sem[sem], 16)
-        note("dma" + sem, q, in_[1], out[1], sem, total[sem])
+    def run(q, fn, out, ins, own_waw=False):
+        later(q, lambda: now(q, fn, out, ins))
+
+    def dma(q, out, in_, sem, paced=False):
+        def issue():
+            if paced: pace(q)
+            await_deps(q, in_[1], out[1], True)
+            total[sem] += 16
+            queue[q].dma_start(out[0], in_[0]).then_inc(T.sem[sem], 16)
+            note("dma" + sem, q, in_[1], out[1], sem, total[sem])
+        later(q, issue)
 
     def b(name, lo=0, hi=None, step=1, p0=0, p1=128):
         hi = SCRATCH[name][1][-1] if hi is None else hi
@@ -186,11 +203,14 @@ def rank_program(g, core, T, topo):
             out = (out[0], out[1] + total_in[1])
         run("A", lambda: g.scalar.activation(out[0], a[0], func, **kw), out, [a])
 
-    def mm(out, l, r, start, stop):
-        run("P", lambda: g.tensor.matmul(out[0], l[0], r[0], start, stop), out, [l, r])
-
     def mms(out, terms):
-        for i, (l, r) in enumerate(terms): mm(out, l, r, i == 0, i == len(terms) - 1)
+        def issue():
+            for i, (l, r) in enumerate(terms):
+                now("P", lambda: g.tensor.matmul(out[0], l[0], r[0], i == 0, i == len(terms) - 1), out, [l, r])
+        later("P", issue)
+
+    def mm(out, l, r, start, stop):
+        mms(out, [(l, r)])
 
     def wrap(sel, name, lo, hi):
         return [(b(sel, 15 - r, 143 - r), b(name, lo + r, hi, 16)) for r in range(16)]
@@ -202,21 +222,18 @@ def rank_program(g, core, T, topo):
     def select(out, a, pattern, cmp, fillv, base, cm):
         run("G", lambda: g.affine_select(out[0], a[0], pattern, cmp, fillv, base, cm), out, [a])
 
-    def send(src, dst_ap, sem, dst):
-        await_deps("G", src[1], [], False)
-        rid, pid, _se = topo.addr(dst)
-        g.remote_dma(dst_ap, src[0], T.sem["ar" + sem], T.sem["local"], pid, rid, topo.mask(core, dst))
-        total["local"] += len(topo.engines(core, dst))
+    def send(src, to, sem, dst):
+        def issue():
+            await_deps("G", src[1], [], False)
+            rid, pid, _se = topo.addr(dst)
+            g.remote_dma(to[0], src[0], T.sem["ar" + sem], T.sem["local"], pid, rid, topo.mask(core, dst))
+            total["local"] += len(topo.engines(core, dst))
+        later("G", issue)
 
     def arrives(name, lo, hi, src, sem):
         n = len(topo.engines(src, core))
         total["ar" + sem] += n
         note("remote", None, [], [(name, lo, hi)], "ar" + sem, n)
-
-    def weave(*steps):
-        steps = list(steps)
-        while steps:
-            steps = [s for s in steps if next(s, None) is not None]
 
     ring = lambda n: T.cores[(rank + n * STEP) % len(T.cores)]
     for t in (1, 2):
@@ -226,30 +243,33 @@ def rank_program(g, core, T, topo):
             arrives("D%d%d" % (t, p), 0, H, ring(-1), "D%d%d" % (t, p))
         arrives("BA%d" % t, 0, K, ring(-t), "BA%d" % t)
 
-    first = EDGES[2]
+    first = EDGES[1]
     dma("A", b("LN8", p1=8), (T.ln[:, :], []), "ldLN8")
-    dma("A", b("WI"), (T.w[:, :], []), "ldWI")
     dma("S", b("STK", 0, first), (T.stk[:, 0:first], []), "ldSTKa")
     dma("S", b("X"), (T.xt[:, :], []), "ldX")
     dma("S", b("STK", first, K), (T.stk[:, first:K], []), "ldSTKb")
     dma("S", b("Z0", 0, K), (T.z[:, :], []), "ldZ0")
+    dma("S", b("WI"), (T.w[:, :], []), "ldWI")
     for p, (l0, l1) in enumerate(PARTS): dma("S", (T["D0%d" % p][:, :], [("D0%d" % p, 0, H)]), (T.stk[:, l0:l1], []), "ldD0%d" % p)
     dma("S", b("CON"), (T.con[:, :], []), "ldCON")
     dma("S", b("BAS"), (T.bas[:, :], []), "ldBAS")
 
+    rb = lambda k: 16 * k + 32 * (k // H) + 15
+
     def yall(p, lo, hi):
         return (T["Y%d" % p][:, lo:hi], [("Y%d" % p, 0, 64)])
 
-    def shifts(t, p, rows=range(16)):
+    def pace(q):
+        if seen[q].get("sV", 0) < total["sV"]:
+            queue[q].wait_ge(T.sem.sV, total["sV"])
+            learn(q, "sV", total["sV"])
+
+    def shifts(t, n):
+        p = n // 4
         Y, D = "Y%d" % p, "D%d%d" % (t, p)
-        if rows.start:
-            await_deps("S", [("D%d1" % t if t else "D10", 0, H)], [], False)
-        elif t: dma("S", b("ST%d" % t, *PARTS[p]), (T[D][:, :], [(D, 0, H)]), "ldST%d%d" % (t, p))
-        for q in rows:
-            dma("S", (T[Y][q::16, (15 - q) * H:(31 - q) * H], [(Y, 4 * q, 4 * q + 1)]), (T[D][:, :], [(D, 0, H), (Y + "f", 0, 3)]), "d" + Y)
-        if t == 0 and p == 1 and rows.start == 0:
-            for q in range(15 - LOW):
-                dma("S", (T[Y][q::16, LOW * H:(15 - q) * H], [(Y, 4 * q + 2, 4 * q + 3)]), (T[D][0:8 * (15 - LOW - q), :], [(D, 0, H)]), "d" + Y)
+        if t and n % 4 == 3 and not NOST: dma("S", b("ST%d" % t, *PARTS[p]), (T[D][:, :], [(D, 0, H)]), "ldST%d%d" % (t, p))
+        for q in range(n % 4, 16, 4):
+            dma("S", (T[Y][q::16, (15 - q) * H:(31 - q) * H], [(Y, 4 * q, 4 * q + 1)]), (T[D][:, :], [(D, 0, H), (Y + "f", 0, 3)]), "d" + Y, True)
 
     fill(b("ONE"), 1.0)
     iota(b("KC"), [[0, 1]], 0, 1, False)
@@ -268,15 +288,17 @@ def rank_program(g, core, T, topo):
     ts(b("KD"), b("KC"), 15, op.bitwise_and)
     fill(b("BQ"), 0.0)
     fill(b("MK"), 1.0)
+    fill(b("ONH"), 1.0)
     for n in set(SIGNS) - {0}: fill((T["CS%d" % n][:, :, :], [("CS%d" % n, 0, 1)]), 0.0)
-    fill(b("RB", 8192, 8224), 0.0)
+    for p, (l0, l1) in enumerate(PARTS): fill(b("RB", rb(l0) + 16 * H, rb(l0) + 16 * H + 1), 0.0)
     fill(b("MK", 0, None, 16), 0.0, True)
     cp(b("RC"), b("KD"))
     fill((T.GE[:, :, :, 0], [("GE0", 0, K)]), 1.0)
+    ts(b("IH"), b("TA"), 0.5 - 1.0 / 2048.0, op.mult)
     for n in set(SIGNS) - {0}: fill((T["CS%d" % n][:, :, 1:n + 1], [("CS%d" % n, 0, 1)]), 8 * VOTE, True)
     cp(b("BQ", 15, 144, 16), b("TB", 16, 25))
-    for name, scale in (("ID", 1.0), ("ND", -1.0), ("TN", -1.0), ("I16", H / 4096.0), ("I32", 32.0), ("I256", 256.0), ("IT", float(TOFF))):
-        ac(b(name), b("TA"), scale=scale)
+    for name, scale in (("ID", 1.0), ("ND", -1.0), ("I256", 256.0), ("IR", WHOLE)): ac(b(name), b("TA"), scale=scale)
+    for name, scale in (("TN", -1.0), ("I16", H / 4096.0), ("I32", 32.0), ("IT", float(TOFF))): ts(b(name), b("TA"), scale, op.mult)
     for name, scale in (("BN", -VOTE), ("BV", 1024.0), ("BM", H / 2.0)): ac(b(name), b("BQ"), scale=scale)
     ac(b("ONB"), b("ONE"), scale=1.0 / 128.0)
     ac(b("GB"), b("TB", 16, 24))
@@ -298,17 +320,17 @@ def rank_program(g, core, T, topo):
     cp(b("LNB", p1=8), b("LN8", p1=8))
     mm(b("SA"), b("GA", p1=8), b("LNB", p1=8), True, True)
     run("A", lambda: g.scalar.activation(T.SG[:, :], T.SA[:, :], act.Sign, bias=T.RN[:, :]), b("SG"), [b("SA"), b("RN")])
-    for n in ("DD0", "LX"): ac(b(n), b("SG"), act.Identity, scale=-FAR / 2.0, bias=DEAD - FAR / 2.0)
+    for n in ("VT1", "LX"): ac(b(n), b("SG"), act.Identity, scale=-FAR / 2.0, bias=DEAD - FAR / 2.0)
     fill((T.Y0[:, 16 * H:16 * H + YV], [("Y0f", 2, 3)]), FAR)
-    shifts(0, 0)
 
     def second(t, p):
         far(1, 1, 2 * H, LOW * H)
-        shifts(0, 1, range(EARLY))
+        for q in range(15 - LOW):
+            dma("S", (T.Y1[q::16, LOW * H:(15 - q) * H], [("Y1", 4 * q + 2, 4 * q + 3)]), (T.D01[0:8 * (15 - LOW - q), :], [("D01", 0, H)]), "dY1", True)
 
     def coded():
         cp(b("WF"), b("WI"))
-        tt(b("PW0", 0, K), b("CON"), b("DD0"), op.add)
+        tt(b("PW0", 0, K), b("CON"), b("VT1"), op.add)
         ts(b("BW"), b("BQ"), b("WF"), op.mult)
         ts(b("BA0"), b("BAS"), float(BASE), op.add)
 
@@ -316,15 +338,16 @@ def rank_program(g, core, T, topo):
         mms(b("CC", *PARTS[p]), [(b("TA"), b("PW0", *PARTS[p])), (b("TN"), b("LX", *PARTS[p]))])
 
     def bases(t, n):
-        send(b("BA0"), T["BA%d" % n][:, :], "BA%d" % n, ring(n))
+        send(b("BA0"), b("BA%d" % n), "BA%d" % n, ring(n))
 
     xall = b("X")
 
     def records(t, l0, l1, on="A"):
-        (ac if on == "A" else cp)(b("RB", 16 * l0 + 15, 16 * l1 + 15), ind(xall, b("SU%d" % t, l0, l1)))
+        (ac if on == "A" else cp)(b("RB", rb(l0), rb(l0) + 16 * (l1 - l0)), ind(xall, b("SU%d" % t, l0, l1)))
 
     def row(ci, i):
-        a0, a1 = 16 * CHUNKS[ci][0] + 15, 16 * CHUNKS[ci][1] + 15
+        a0 = rb(CHUNKS[ci][0])
+        a1 = a0 + 16 * (CHUNKS[ci][1] - CHUNKS[ci][0])
         return (T.RB[:, a0 + i:a1:16], [("RB", a0, a1)])
 
     def slots(ci, s0, s1, r=None):
@@ -332,63 +355,91 @@ def rank_program(g, core, T, topo):
         ap = T.GE[:, l0 // 16:l1 // 16, :, s0:s1] if r is None else T.GE[:, l0 // 16:l1 // 16, r, s0:s1]
         return (ap, [("GE%d" % s, l0, l1) for s in range(s0, s1)])
 
+    signed = lambda t, ci: max([1] + [s1 for c, s0, s1 in BATCH[:USED[t]] if c == ci]) - 1
+
     def differences(t, i):
+        if i >= USED[t]: return
         ci, s0, s1 = BATCH[i]
         l0, l1 = CHUNKS[ci]
         for s in range(s0, s1):
             mms(b("DD%d" % (i % 2), s - s0, (s1 - s0) * (l1 - l0), s1 - s0), [(b("ID"), row(ci, 16 - s)), (b("ND"), b("Z%d" % t, l0, l1))])
 
     def signs(t, i):
+        if i >= USED[t]: return
         ci, s0, s1 = BATCH[i]
         l0, l1 = CHUNKS[ci]
         ac(slots(ci, s0, s1), b("DD%d" % (i % 2), 0, (s1 - s0) * (l1 - l0)), act.Sign, bias=0.5)
 
     def compare(t, ci):
         l0, l1 = CHUNKS[ci]
-        for s in range(SIGNS[ci] + 1, 16):
+        for s in range(signed(t, ci) + 1, 16):
             tt((T.GE[:, l0 // 16:l1 // 16, :, s], [("GE%d" % s, l0, l1)]), row(ci, 16 - s), b("Z%d" % t, l0, l1), op.is_ge)
             yield 1
 
     def votes(t, ci):
         l0, l1 = CHUNKS[ci]
-        p, n = l0 // H, SIGNS[ci]
+        p, n = l0 // H, signed(t, ci)
         level = [(b("ND"), (T["CS%d" % n][:, 0:(l1 - l0) // 16, :], [("CS%d" % n, 0, 1)]))] if n else []
         mms(b("VT%d" % p, l0 - p * H, l1 - p * H), level + [(b("BN", 15 - r, 143 - r), slots(ci, 0, 16, r)) for r in range(16)])
 
     def maxima(t, ci):
         l0, l1 = CHUNKS[ci]
-        scan(b("PM", 16 * l0, 16 * l1), b("MK", 0, 16 * (l1 - l0)), b("RB", 16 * l0 + 15, 16 * l1 + 15), op.mult, op.max)
+        for k in range(l0, l1, FINE):
+            scan(b("PM", 16 * k, 16 * (k + FINE)), b("MK"), b("RB", rb(k), rb(k) + 16 * FINE), op.mult, op.max)
+            yield 1
 
-    def handler(t, p):
-        l0, l1 = PARTS[p]
-        scan(b("OA", l0, l1), b("VT%d" % p, 0, H), b("CAP"), op.min, op.max)
+    def sub(t, s):
+        l0, l1 = SECTIONS[t][s] if s < len(SECTIONS[t]) else (K, K)
+        p = min(l0 // H, 1)
+        return l0, l1, p, l0 - p * H, l1 - p * H
+
+    def ws(name, l0, l1):
+        return b(TILE[name][0], TILE[name][1] + l0 // 16, TILE[name][1] + l1 // 16)
+
+    def handler(t, s):
+        l0, l1, p, a0, a1 = sub(t, s)
+        if l0 == l1: return
+        scan(b("OA", l0, l1), b("VT%d" % p, a0, a1), b("CAP", a0, a1), op.min, op.max)
         yield 1
         end = b("OA", l0 + 15, l1, 16)
-        ts(w("ml", p), end, 8 * VOTE, op.add)
-        tt(w("h", p), end, b("KH"), op.subtract)
+        ts(ws("ml", l0, l1), end, 8 * VOTE, op.add)
+        tt(ws("h", l0, l1), end, b("KH", a0 // 16, a1 // 16), op.subtract)
         yield 1
 
-    def greatest(t, p):
-        l0, l1 = PARTS[p]
-        ac(b("ZM%d" % p, H, 2 * H), ind(b("PM", 16 * l0, 16 * l1), w("ml", p)))
-        mms(b("UU", 0, 16), wrap("BW", "ZM%d" % p, H, 2 * H))
+    def greatest(t, s):
+        l0, l1, p, a0, a1 = sub(t, s)
+        if l0 == l1: return
+        (cp if s in ONV else ac)(b("ZM%d" % p, H + a0, H + a1), ind(b("PM", 16 * H * p, 16 * l1), ws("ml", l0, l1)))
+        mms(b("UU", a0 // 16, a1 // 16), wrap("BW", "ZM%d" % p, H + a0, H + a1))
 
     def taken(t, p):
         l0, l1 = PARTS[p]
-        ac(b("AG", l0, l1), ind(b("RB", 16 * l0 + 16, 16 * l1 + 16), w("ml", p)))
-        mms(b("LS", 128, 144) if p else b("UU", 16, 32), wrap("BV", "AG", l0, l1))
-        mms(b("SA", 0, H), [(b("ID"), b("AG", l0, l1)), (b("ND"), b("Z%d" % t, l0, l1))])
+        src = ind(b("RB", rb(l0) + 1, rb(l0) + 16 * H + 1), w("ml", p))
+        if p in ONA[t]:
+            ac(b("AG"), src)
+            mms(b("LS", 128, 144) if p else b("UU", 16, 32), wrap("BV", "AG", 0, H))
+            mms(b("VT0", H, K), [(b("ID"), b("AG")), (b("ND"), b("Z%d" % t, l0, l1))])
+            return ac(b("ZM%d" % p, 0, H), b("VT0", H, K))
+        tt(b("ZM%d" % p, 0, H), src, b("Z%d" % t, l0, l1), op.subtract)
+        mms(b("LS", 128, 144) if p else b("UU", 16, 32), [(b("TA"), w("zs", p))] + wrap("BV", "ZM%d" % p, 0, H))
 
-    def sums(t, p):
-        cp(b("UI", 32 * p, 48 if p else 32), b("UU", 0, 16 if p else 32))
+    def level(t, p):
+        if p in ONA[t]: return
+        mms(b("UU", 32 + 16 * p, 48 + 16 * p), wrap("BV", "Z%d" % t, *PARTS[p]))
+        cp(w("zs", p), b("UU", 32 + 16 * p, 48 + 16 * p))
 
-    def changed(t, p):
-        o = 32 * p
-        ts(w("x15", p), b("UI", o, o + 16), 15, op.bitwise_and)
+    def sums(t, s):
+        l0, l1, p, a0, a1 = sub(t, s)
+        if l1 > l0: cp(b("UI", 32 * p + a0 // 16, 32 * p + a1 // 16 if p else 32), b("UU", a0 // 16, a1 // 16 if p else 32))
+
+    def changed(t, s):
+        l0, l1, p, a0, a1 = sub(t, s)
+        if l0 == l1: return
+        ts(ws("x15", l0, l1), b("UI", 32 * p + a0 // 16, 32 * p + a1 // 16), 15, op.bitwise_and)
         yield 1
-        tt(w("xk", p), w("x15", p), b("K16", 16 * p, 16 * p + 16), op.add)
+        tt(ws("xk", l0, l1), ws("x15", l0, l1), b("K16", 0, (l1 - l0) // 16), op.add)
         yield 1
-        cp(w("xl", p), w("xk", p))
+        cp(ws("xl", l0, l1), ws("xk", l0, l1))
         yield 1
 
     def lists(t, p):
@@ -422,18 +473,15 @@ def rank_program(g, core, T, topo):
         l0, l1 = PARTS[p]
         tt(b("PB", l0, l1), ind(b("PW%d" % (t % 2), 0, TOFF), w("jl", p)), b("BA%d" % t, l0, l1), op.min)
 
-    def distance(t, p):
-        ac(b("ZM%d" % p, 0, H), b("SA", 0, H), act.Abs)
-
     def mark(t, p):
         l0, l1 = PARTS[p]
-        ac(b("ZO%d" % t, l0, l1), ind(b("ZM%d" % p), b("L3", 48 * p, 48 * p + 16)))
-        if t < ROUNDS - 1: send(b("ZO%d" % t, l0, l1), T["Z%d" % (t + 1)][:, l0:l1], "Z%d%d" % (t + 1, p), ring(1))
+        ac(b("ZO%d" % t, l0, l1), ind(b("ZM%d" % p), b("L3", 48 * p, 48 * p + 16)), act.Abs)
+        if t < ROUNDS - 1: send(b("ZO%d" % t, l0, l1), b("Z%d" % (t + 1), l0, l1), "Z%d%d" % (t + 1, p), ring(1))
         else: dma("S", (T.yz[:, l0:l1], []), b("ZO%d" % t, l0, l1), "out")
 
     def lengths(t, p):
         l0, l1 = PARTS[p]
-        ac(b("SG", l0, l1), b("PB", l0, l1), act.Sign)
+        ac(b("SG", l0, l1), ind(b("PW%d" % (t % 2), 0, TOFF), w("jl", p)) if DIRECT else b("PB", l0, l1), act.Sign)
         mms(b("LS", 64, 80), [(b("ID"), b("KY")), (b("I256"), w("h", p)), (b("ND"), w("un", p)), (b("I256"), w("pst", p))]
             + wrap("BM", "SG", l0, l1))
 
@@ -447,15 +495,10 @@ def rank_program(g, core, T, topo):
         ts(sn, b("TY", l0, l1), 8191, op.bitwise_and)
         yield 1
         if t < ROUNDS - 1:
-            cp(b("UO%d" % t, l0, l1), sn)
-            send(b("UO%d" % t, l0, l1), T["SU%d" % (t + 1)][:, l0:l1], "SU%d%d" % (t + 1, p), ring(1))
-            send(sn, T["D%d%d" % (t + 1, p)][:, :], "D%d%d" % (t + 1, p), ring(1))
-            if p == 0:
-                if t == 0 and EARLY < 16: shifts(0, 1, range(EARLY, 16))
-                shifts(t + 1, 0, range(AHEAD))
-            else:
-                shifts(t + 1, 0, range(AHEAD, 16))
-                shifts(t + 1, 1)
+            if GCP: select(b("UO%d" % t, l0, l1), sn, [[0, H]], op.is_ge, 0.0, 0, 0)
+            else: cp(b("UO%d" % t, l0, l1), sn)
+            send(b("UO%d" % t, l0, l1), b("SU%d" % (t + 1), l0, l1), "SU%d%d" % (t + 1, p), ring(1))
+            send(sn, b("D%d%d" % (t + 1, p)), "D%d%d" % (t + 1, p), ring(1))
         else:
             cp(b("FO", l0, l1), sn)
             dma("S", (T.ys[:, l0:l1], []), b("FO", l0, l1), "out")
@@ -464,7 +507,7 @@ def rank_program(g, core, T, topo):
     def stored(t, p):
         l0, l1 = PARTS[p]
         new = b("PW%d" % (t % 2), TOFF + l0, TOFF + l1)
-        tt(new, ind(b("LT"), b("L3", 48 * p + 16, 48 * p + 32)), b("ST%d" % t if t else "STK", l0, l1), op.add)
+        tt(new, ind(b("LT"), b("L3", 48 * p + 16, 48 * p + 32)), yall(p, 15 * H, 16 * H) if t and NOST else b("ST%d" % t if t else "STK", l0, l1), op.add)
         yield 1
         tt(b("CC", l0, l1) if t < ROUNDS - 1 else b("CI32", l0, l1), new, b("CC", l0, l1), op.min)
         yield 1
@@ -485,23 +528,23 @@ def rank_program(g, core, T, topo):
             ac(b("FN", l0, l1, p1=8), b("SA", H, 2 * H, p1=8), act.Identity, bias=8.0, scale=-0.5)
             dma("S", (T.yn[:, l0:l1], []), b("FN", l0, l1, p1=8), "out")
 
-    def old(t, p):
-        if ONV[p]: return
-        ac(b("OX", *PARTS[p]), ind(xall, w("xl", p)))
-        mms(b("SA", H, 2 * H), [(b("ID"), b("ZM%d" % p, H, 2 * H)), (b("ID"), b("OX", *PARTS[p]))])
+    def old(t, s):
+        l0, l1, p, a0, a1 = sub(t, s)
+        if l0 == l1: return
+        src, m = ind(b("X", 16 * l0, 16 * l1), ws("xl", l0, l1)), b("ZM%d" % p, H + a0, H + a1)
+        if s in ONV: return tt(b("XS", 0, l1 - l0), src, m, op.add)
+        ac(b("OX", l0, l1), src)
+        mms(b("SA", l0, l1), [(b("IH"), m), (b("IH"), b("OX", l0, l1)), (b("IR"), b("ONH", 0, l1 - l0))])
 
-    def halves(t, p):
-        if ONV[p]: return
-        ac(b("NF", *PARTS[p]), b("SA", H, 2 * H), act.Identity, bias=WHOLE, scale=0.5 - 1.0 / 2048.0)
-        ac(b("NB", *PARTS[p]), b("NF", *PARTS[p]), act.Identity, bias=-WHOLE)
+    def halves(t, s):
+        l0, l1, p, a0, a1 = sub(t, s)
+        if l0 == l1: return
+        if s in ONV: ts(b("XH", 0, l1 - l0), b("XS", 0, l1 - l0), 1, op.arith_shift_right)
+        else: ac(b("NB", l0, l1), b("SA", l0, l1), act.Identity, bias=-WHOLE)
 
-    def table(t, p):
-        yield from changed(t, p)
-        if not ONV[p]: return
-        tt(b("XS", *PARTS[p]), ind(xall, w("xl", p)), b("ZM%d" % p, H, 2 * H), op.add)
-        yield 1
-        ts(b("XH", *PARTS[p]), b("XS", *PARTS[p]), 1, op.arith_shift_right)
-        yield 1
+    def written(t, s):
+        l0, l1, p, a0, a1 = sub(t, s)
+        if l1 > l0: cp(scattered(b("X", 16 * l0, 16 * l1), ws("xl", l0, l1)), b("XH", 0, l1 - l0) if s in ONV else b("NB", l0, l1))
 
     def unhandled():
         mm(b("LS", 96, 128), b("ONB"), w("un"), True, True)
@@ -509,32 +552,32 @@ def rank_program(g, core, T, topo):
 
     def gather(t, ci):
         l0, l1 = CHUNKS[ci]
-        if t or ci > 1: records(t, l0 + (SHARE if ci == 1 else 0), l1)
-        elif ci == 0:
-            records(t, *CHUNKS[1])
-            records(t, l0, l1, "V")
-            cp(b("SU0", first, K), b("STK", first, K))
+        c, s0, s1 = SHARE[t]
+        for a0, a1 in ((l0, s0), (s1, l1)) if ci == c else ((l0, l1),):
+            if a1 > a0: records(t, a0, a1)
 
     def share(t, ci):
-        if t and SHARE: records(t, EDGES[1], EDGES[1] + SHARE, "V")
+        if SHARE[t][2] > SHARE[t][1]: records(t, *SHARE[t][1:], "V")
 
-    steps = {"r": gather, "R": share, "c": compare, "v": votes, "m": maxima, "d": differences, "s": signs,
-             "h": handler, "g": greatest, "t": taken, "u": sums, "l": lists, "p": piece, "n": lengths, "a": distance, "z": mark,
+    steps = {"r": gather, "R": share, "i": shifts, "y": level, "d": differences, "s": signs, "c": compare, "v": votes, "m": maxima,
+             "h": handler, "g": greatest, "t": taken, "u": sums, "l": lists, "p": piece, "n": lengths, "z": mark,
              "k": stack, "e": stored, "q": pieces}
-    inner = {"x": table, "o": old, "f": halves, "N": lambda t, p: unhandled(),
-             "w": lambda t, p: cp(scattered(xall, w("xl", p)), b("XH" if ONV[p] else "NB", *PARTS[p]))}
+    inner = {"x": changed, "o": old, "f": halves, "N": lambda t, p: unhandled(),
+             "w": written}
 
-    once = {"C": lambda t, p: coded(), "j": names, "B": bases, "Y": second}
+    once = {"C": lambda t, p: coded(), "j": names, "B": bases, "Y": second, "U": lambda t, p: cp(b("SU0", first, K), b("STK", first, K))}
 
-    def issue(order, t):
-        for group in order.split():
-            todo = []
-            for name in group.split("+"):
-                tt_ = t - name.count("'")
-                todo.append({**steps, **inner, **once}[name[0]](tt_, int(name[1])))
-            weave(*[s for s in todo if s])
-
-    for t in range(ROUNDS): issue((FIRST, ORDER, LAST)[t], t)
+    table = {**steps, **inner, **once}
+    for t, order in enumerate((FIRST, ORDER, LAST)):
+        for word in order.split():
+            key = (word[0], t - word.count("'") + word.count("^"), int(word[1]))
+            if key not in calls:
+                step[0] = key
+                calls[key] = []
+                for _ in table[key[0]](*key[1:]) or (): pass
+            n = word[2:].strip("'^")
+            for _ in range(int(n[1:]) if n[1:] else 1 if n else len(calls[key])): calls[key].pop(0)()
+    assert not any(calls.values())
 
     for s in SEMAPHORES:
         if total[s]: g.wait_ge(T.sem[s], total[s])

from concourse.mybir import AluOpType, AxisListType, ActivationFunctionType

ROUNDS, STEP, K, NREC = 3, 3, 512, 8192
H = 256
PARTS = [(0, H), (H, K)]
EDGES = [0, 64, 160, 256, 352, 448, 512]
CHUNKS = list(zip(EDGES[:-1], EDGES[1:]))
BATCH = [(4, 1, 6), (5, 1, 9)]
USED = [2, 2, 2]
SIGNS = [max([1] + [s1 for c, s0, s1 in BATCH[:n] if c == ci]) - 1 for ci in range(len(CHUNKS)) for n in USED]
SHARE = [(1, 64, 96), (1, 64, 112), (1, 64, 96)]
DIRECT = True
GCP = False
FINE = 32
SECTIONS = [[(0, 256), (256, 512)], [(0, 256), (256, 512)], [(0, 256), (256, 512)]]
ONV = [2]
ONA = [[1], [1], [1]]
NOST = True
LOW = 6
FIRST = "S0 V0. G0 V0.34 Y1 A0.10 P0. A0. V0 U0 P0 A0 R0 C0. i1 i0 r0 y0 m0 c0 m1. C0.2 r2 c2.10 i2 m2. r1 c1 c2 r3 c3.5 j0 m1 m3 i3 v0 v1 v2 r5 i7 d1 h0. c3.3 h0 t0 i5 r4 d0 i4 l0. c5.5 m2 c5 m5. c4.5 g0 c3.4 m4. s1 i6 u0 c3. l0. c3 l0.3 x0. c4.2 v5 s0 l0.4 c4 l0. m5 l0 v3 v4 x0. n0 C0 x0 m4 z0 h1 p0 o0 k0. l1. k0. g1 e0. k0. t1.3 u1 k0 x1. f0 l1. x1. l1. x1 l1.8 i3.3^ i0.3^ w0 l1 q0 o1 t1 f1 w1 N0. z1. n1 B1 z1 p1"
ORDER = "R0 k1.3' y0. r2 c2. k1' m1. c2 i3 r0 c0 m0 i1 r1 c1 y0 m2 r3 m1 c3.6 j1' i2 i0 v2 v0 v1 B2' i6 m3. e0' i5 i7 h0. c3.2 h0 c3 t0. e1.' l0. r4 c4.8 d0 m4. g0 t0 u0 r5 c5.4 l0. m5. l0.3 v3 d1 c5 c4 N0' l0.4 q1' i4 m4. l0. s0 v4 s1 v5 m3 l0 x0. n0 m5 x0. m4 x0 e1' z0 o0 h1 g1 p0 k0. e0. k0. t1.3 u1 k0. x1. k0 l1.2 x1. f0 q0 l1. x1 l1.8 o1 t1 N0. i3.2^ i2^ w0 f1 l1 z1 n1 w1 p1"
LAST = "r0 R0 k1.' m1. k1.' c0.3 k1.' e0' k1' i1 r1 c0 c1 r2 m0. m1 v1 c2 m2. i0 v0 r5 v2 c5.6 i3 m0 m2. e1.' y0. h0. i4 m2 h0 y0 t0. i7 r3 c3.9 i6 m3.2 i5 e1' g0. d1 t0 g0 l0. u0 m3 l0. r4 c3.2 l0.5 c3 c5 N0' c4 l0.2 m5 l0. d0 v3 s1 m4. l0 v5 s0 q1' v4 e0. m4. n0 z0 e0. h1.2 t1.2 m4 p0 e0. g1 h1 e0 q0 k0. l1.2 t1 k0. u1 l1 e1. n1 z1 q1 p1 e1. k0. e1. k1. e1 k1. k0 k1"
VOTE = 4096.0
FAR = 1 << 20
DEAD = 16384
BASE = 8192
NOP = 1 << 26
TOFF = 528
WHOLE = 12582912.0
YV = 3840

SCRATCH = {
    "X": ("sbuf", [128, NREC], "bfloat16"),
    "RB": ("sbuf", [128, NREC + 64], "bfloat16"),
    "PM": ("sbuf", [128, NREC], "bfloat16"),
    "GE": ("sbuf", [128, 32, 16, 16], "bfloat16"),
    "Y0": ("sbuf", [128, 31 * H], "int32"), "Y1": ("sbuf", [128, 31 * H], "int32"),
    "STK": ("sbuf", [128, K], "int32"), "CON": ("sbuf", [128, K], "int32"), "BAS": ("sbuf", [128, K], "int32"),
    "LN8": ("sbuf", [128, K], "int32"), "LNB": ("sbuf", [128, K], "bfloat16"), "LX": ("sbuf", [128, K], "float32"),
    "WI": ("sbuf", [128, 1], "int32"), "WF": ("sbuf", [128, 1], "float32"),
    "PW0": ("sbuf", [128, TOFF + K], "float32"), "PW1": ("sbuf", [128, TOFF + K], "float32"),
    "ZM0": ("sbuf", [128, 2 * H], "bfloat16"), "ZM1": ("sbuf", [128, 2 * H], "bfloat16"),
    "OA": ("sbuf", [128, K], "float32"), "AG": ("sbuf", [128, H], "bfloat16"),
    "OX": ("sbuf", [128, K], "bfloat16"), "NB": ("sbuf", [128, K], "bfloat16"),
    "IH": ("sbuf", [128, 128], "float16"), "IR": ("sbuf", [128, 128], "bfloat16"), "ONH": ("sbuf", [128, H], "bfloat16"),
    "PB": ("sbuf", [128, K], "float32"), "SG": ("sbuf", [128, K], "bfloat16"), "TY": ("sbuf", [128, K], "int32"),
    "CI32": ("sbuf", [128, K], "int32"), "CN": ("sbuf", [128, K], "int32"), "SF": ("sbuf", [128, K], "bfloat16"),
    "FO": ("sbuf", [128, K], "float32"), "FC": ("sbuf", [128, K], "float32"), "FN": ("sbuf", [128, K], "float32"),
    "ONE": ("sbuf", [128, 128], "float32"), "ST1": ("sbuf", [128, K], "int32"), "ST2": ("sbuf", [128, K], "int32"),
    "KC": ("sbuf", [128, 1], "int32"), "KD": ("sbuf", [128, 1], "int32"), "RC": ("sbuf", [128, 1], "float32"), "R16": ("sbuf", [128, 1], "float32"),
    "RN": ("sbuf", [128, 1], "float32"), "TN": ("sbuf", [128, 128], "float32"), "TA": ("sbuf", [128, 128], "float32"), "TB": ("sbuf", [128, 32], "float32"), "GB": ("sbuf", [128, 8], "bfloat16"),
    "ID": ("sbuf", [128, 128], "bfloat16"), "ND": ("sbuf", [128, 128], "bfloat16"), "I16": ("sbuf", [128, 128], "bfloat16"),
    "I32": ("sbuf", [128, 128], "bfloat16"), "I256": ("sbuf", [128, 128], "bfloat16"), "IT": ("sbuf", [128, 128], "bfloat16"),
    "ONB": ("sbuf", [128, 128], "bfloat16"),
    "BQ": ("sbuf", [128, 144], "bfloat16"), "BN": ("sbuf", [128, 144], "bfloat16"), "BV": ("sbuf", [128, 144], "bfloat16"),
    "BM": ("sbuf", [128, 144], "bfloat16"), "BW": ("sbuf", [128, 144], "float16"),
    "GA": ("sbuf", [128, 128], "bfloat16"), "MK": ("sbuf", [128, 16 * FINE], "bfloat16"),
    "CI": ("sbuf", [128, H], "float32"), "CAP": ("sbuf", [128, H], "float32"),
    "LI": ("sbuf", [128, 32], "float32"), "LJ": ("sbuf", [128, 32], "float32"), "LT": ("sbuf", [128, 128], "float32"),
    "KI": ("sbuf", [128, 32], "float32"), "K16": ("sbuf", [128, 32], "float32"), "KH": ("sbuf", [128, 16], "float32"),
    "KF": ("sbuf", [128, 32], "float16"), "KY": ("sbuf", [128, 16], "float16"),
    "ACOL": ("sbuf", [128, 1], "float32"), "AJ": ("sbuf", [128, 32], "float32"),
}
for _n in ("XS", "XH"): SCRATCH[_n] = ("sbuf", [128, H], "int32")
for _n in set(SIGNS) - {0}: SCRATCH["CS%d" % _n] = ("sbuf", [128, 8, 16], "bfloat16")
BANKS = ["VT0", "VT1", "UU", "LS", "SA", "CC", "DD0", "DD1"]
for _n in BANKS:
    SCRATCH[_n] = ("psum", [128, K], "float32")
for _t in range(3):
    SCRATCH["SU%d" % _t] = ("sbuf", [128, K], "uint16")
    SCRATCH["Z%d" % _t] = ("sbuf", [128, K], "bfloat16")
    SCRATCH["BA%d" % _t] = ("sbuf", [128, K], "int32")
    SCRATCH["ZO%d" % _t] = ("sbuf", [128, K], "bfloat16")
    SCRATCH["SN%d" % _t] = ("sbuf", [128, K], "int32")
    if _t < 2: SCRATCH["UO%d" % _t] = ("sbuf", [128, K], "uint16")
    for _p in range(2): SCRATCH["D%d%d" % (_t, _p)] = ("dram", [128, H], "int32")
TILES = {"FW": ("float32", ["xk", "a", "w", "zs"]), "IW": ("int32", ["x15", "n", "n2", "j"]), "BT": ("bfloat16", ["h", "un", "pst"]),
         "LU": ("uint16", ["ml", "xl", "jl", "yl"])}
TILE = {}
for _b, (_d, _names) in TILES.items():
    SCRATCH[_b] = ("sbuf", [128, 32 * len(_names)], _d)
    for _i, _n in enumerate(_names): TILE[_n] = (_b, 32 * _i)
SCRATCH["UI"] = ("sbuf", [128, 64], "int32")
SCRATCH["UM"] = ("sbuf", [128, 64], "int32")
SCRATCH["L3"] = ("sbuf", [128, 96], "uint16")

LOADS = ["STKa", "STKb", "X", "Z0", "WI", "LN8", "BAS", "CON", "D00", "D01", "ST10", "ST11", "ST20", "ST21"]
ARR = ["%s%d%d" % (n, t, p) for n in ("SU", "D", "Z") for t in (1, 2) for p in (0, 1)] + ["BA1", "BA2"]
SEMAPHORES = (["sV", "sA", "sP", "sG", "local", "dY0", "dY1", "out"]
              + ["ld" + n for n in LOADS] + ["ar" + n for n in ARR])


def rank_program(g, core, T, topo):
    rank = T.rank_of(core)
    if rank is None:
        return
    op = AluOpType
    act = ActivationFunctionType
    queue = {"V": g.vector, "A": g.scalar, "P": g.tensor, "G": g, "S": g.sync}
    total = {s: 0 for s in SEMAPHORES}
    seen = {q: {} for q in queue}
    snap = {}
    hist = {}

    def learn(q, sem, cnt):
        if seen[q].get(sem, 0) < cnt: seen[q][sem] = cnt
        for s, n in snap.get((sem, cnt), {}).items():
            if seen[q].get(s, 0) < n: seen[q][s] = n

    def await_deps(q, reads, writes, own_waw):
        need = {}
        for lst, isw in ((reads, False), (writes, True)):
            for name, lo, hi in lst:
                ps = name in BANKS
                for l, h, w, oq, sem, cnt in hist.get(name, []):
                    if (oq == q or not ps) and (h <= lo or hi <= l): continue
                    if oq == q:
                        if not (w and (not isw or own_waw)): continue
                    elif not (isw or w or ps): continue
                    if seen[q].get(sem, 0) >= cnt: continue
                    if sem[0] in "ldo": cnt = total[sem]
                    if need.get(sem, 0) < cnt: need[sem] = cnt
        for sem in sorted(need, key=lambda s: -need[s]):
            if seen[q].get(sem, 0) < need[sem]:
                queue[q].wait_ge(T.sem[sem], need[sem])
                learn(q, sem, need[sem])

    def note(oq, q, reads, writes, sem, cnt):
        snap[(sem, cnt)] = dict(seen[q]) if q else {}
        for name, lo, hi in writes:
            old = [e for e in hist.get(name, []) if not (lo <= e[0] and e[1] <= hi)]
            hist[name] = old + [(lo, hi, True, oq, sem, cnt)]
        for name, lo, hi in reads:
            old = [e for e in hist.get(name, []) if not (not e[2] and e[3] == oq and lo <= e[0] and e[1] <= hi)]
            hist[name] = old + [(lo, hi, False, oq, sem, cnt)]

    calls, step = {}, [None]

    def later(q, fn):
        calls.setdefault(step[0] or (q, 0, 0), []).append(fn)

    def now(q, fn, out, ins):
        reads = [x for i in ins for x in i[1]]
        writes = list(out[1])
        for x in out[2:]: reads += x
        await_deps(q, reads, writes, q != "P")
        sem = "s" + q
        total[sem] += 1
        fn().then_inc(T.sem[sem], 1)
        note(q, q, reads, writes, sem, total[sem])

    def run(q, fn, out, ins, own_waw=False):
        later(q, lambda: now(q, fn, out, ins))

    def dma(q, out, in_, sem, paced=False):
        def issue():
            if paced: pace(q)
            await_deps(q, in_[1], out[1], True)
            total[sem] += 16
            queue[q].dma_start(out[0], in_[0]).then_inc(T.sem[sem], 16)
            note("dma" + sem, q, in_[1], out[1], sem, total[sem])
        later(q, issue)

    def b(name, lo=0, hi=None, step=1, p0=0, p1=128):
        hi = SCRATCH[name][1][-1] if hi is None else hi
        ap = T[name][p0:p1, lo:hi] if step == 1 else T[name][p0:p1, lo:hi:step]
        return (ap, [(name, lo, hi)])

    def w(name, p=None):
        buf, o = TILE[name]
        return b(buf, o, o + 32) if p is None else b(buf, o + 16 * p, o + 16 * p + 16)

    def ind(win, lst):
        return (win[0].indirect(lst[0]), win[1] + lst[1])

    def scattered(win, lst):
        return (win[0].indirect(lst[0]), win[1], lst[1])

    def tt(out, a, c, o):
        run("V", lambda: g.vector.tensor_tensor(out[0], a[0], c[0], o), out, [a, c])

    def ts(out, a, s1, o1, s2=None, o2=None, waw=False):
        ins = [a] + [s for s in (s1, s2) if isinstance(s, tuple)]
        v1 = s1[0] if isinstance(s1, tuple) else s1
        v2 = s2[0] if isinstance(s2, tuple) else s2
        if o2 is None:
            run("V", lambda: g.vector.tensor_scalar(out[0], a[0], v1, None, o1), out, ins, waw)
        else:
            run("V", lambda: g.vector.tensor_scalar(out[0], a[0], v1, v2, o1, o2), out, ins, waw)

    def cp(out, a):
        run("V", lambda: g.vector.tensor_copy(out[0], a[0]), out, [a], True)

    def scan(out, a, c, o1, o2):
        run("V", lambda: g.vector.tensor_tensor_scan(out[0], a[0], c[0], 0.0, o1, o2), out, [a, c])

    def fill(out, v, waw=False):
        run("V", lambda: g.vector.memset(out[0], v), out, [], waw)

    def ac(out, a, func=act.Copy, total_in=None, **kw):
        if total_in:
            kw["accum_out"] = total_in[0]
            out = (out[0], out[1] + total_in[1])
        run("A", lambda: g.scalar.activation(out[0], a[0], func, **kw), out, [a])

    def mms(out, terms):
        def issue():
            for i, (l, r) in enumerate(terms):
                now("P", lambda: g.tensor.matmul(out[0], l[0], r[0], i == 0, i == len(terms) - 1), out, [l, r])
        later("P", issue)

    def mm(out, l, r, start, stop):
        mms(out, [(l, r)])

    def wrap(sel, name, lo, hi):
        return [(b(sel, 15 - r, 143 - r), b(name, lo + r, hi, 16)) for r in range(16)]

    def iota(out, pattern, base, cm, small=True):
        if small: run("G", lambda: g.iota(out[0], pattern, base, cm, allow_small_or_imprecise_dtypes=True), out, [])
        else: run("G", lambda: g.iota(out[0], pattern, base, cm), out, [])

    def select(out, a, pattern, cmp, fillv, base, cm):
        run("G", lambda: g.affine_select(out[0], a[0], pattern, cmp, fillv, base, cm), out, [a])

    def send(src, to, sem, dst):
        def issue():
            await_deps("G", src[1], [], False)
            rid, pid, _se = topo.addr(dst)
            g.remote_dma(to[0], src[0], T.sem["ar" + sem], T.sem["local"], pid, rid, topo.mask(core, dst))
            total["local"] += len(topo.engines(core, dst))
        later("G", issue)

    def arrives(name, lo, hi, src, sem):
        n = len(topo.engines(src, core))
        total["ar" + sem] += n
        note("remote", None, [], [(name, lo, hi)], "ar" + sem, n)

    ring = lambda n: T.cores[(rank + n * STEP) % len(T.cores)]
    for t in (1, 2):
        for p, (l0, l1) in enumerate(PARTS):
            arrives("SU%d" % t, l0, l1, ring(-1), "SU%d%d" % (t, p))
            arrives("Z%d" % t, l0, l1, ring(-1), "Z%d%d" % (t, p))
            arrives("D%d%d" % (t, p), 0, H, ring(-1), "D%d%d" % (t, p))
        arrives("BA%d" % t, 0, K, ring(-t), "BA%d" % t)

    first = EDGES[1]
    dma("A", b("LN8", p1=8), (T.ln[:, :], []), "ldLN8")
    dma("S", b("STK", 0, first), (T.stk[:, 0:first], []), "ldSTKa")
    dma("S", b("X"), (T.xt[:, :], []), "ldX")
    dma("S", b("STK", first, K), (T.stk[:, first:K], []), "ldSTKb")
    dma("S", b("Z0", 0, K), (T.z[:, :], []), "ldZ0")
    dma("S", b("WI"), (T.w[:, :], []), "ldWI")
    for p, (l0, l1) in enumerate(PARTS): dma("S", (T["D0%d" % p][:, :], [("D0%d" % p, 0, H)]), (T.stk[:, l0:l1], []), "ldD0%d" % p)
    dma("S", b("CON"), (T.con[:, :], []), "ldCON")
    dma("S", b("BAS"), (T.bas[:, :], []), "ldBAS")

    rb = lambda k: 16 * k + 32 * (k // H) + 15

    def yall(p, lo, hi):
        return (T["Y%d" % p][:, lo:hi], [("Y%d" % p, 0, 64)])

    def pace(q):
        if seen[q].get("sV", 0) < total["sV"]:
            queue[q].wait_ge(T.sem.sV, total["sV"])
            learn(q, "sV", total["sV"])

    def shifts(t, n):
        p = n // 4
        Y, D = "Y%d" % p, "D%d%d" % (t, p)
        if t and n % 4 == 3 and not NOST: dma("S", b("ST%d" % t, *PARTS[p]), (T[D][:, :], [(D, 0, H)]), "ldST%d%d" % (t, p))
        for q in range(n % 4, 16, 4):
            dma("S", (T[Y][q::16, (15 - q) * H:(31 - q) * H], [(Y, 4 * q, 4 * q + 1)]), (T[D][:, :], [(D, 0, H), (Y + "f", 0, 3)]), "d" + Y, True)

    fill(b("ONE"), 1.0)
    iota(b("KC"), [[0, 1]], 0, 1, False)
    select(b("TA"), b("ONE"), [[-1, 128]], op.is_equal, 0.0, 0, 1)
    select(b("TB", 0, 9), b("ONE", 0, 9), [[-16, 9]], op.is_ge, 0.0, 0, 1)
    select(b("TB", 16, 25), b("TB", 0, 9), [[16, 9]], op.is_ge, 0.0, 15, -1)
    iota(b("KI"), [[16, 32]], 0, 0)
    iota(b("LI"), [[1, 32]], 0, 0)
    iota(b("CI"), [[256, 16], [-1, 16]], 15 - 8 * int(VOTE), 0)
    def far(p, i, lo, hi):
        if hi > lo: iota((T["Y%d" % p][:, lo:hi], [("Y%df" % p, i, i + 1)]), [[0, hi - lo]], FAR, 0, False)

    far(0, 0, 16 * H + YV, 31 * H)
    far(0, 1, 2 * H, 15 * H)
    far(1, 0, 16 * H, 31 * H)
    ts(b("KD"), b("KC"), 15, op.bitwise_and)
    fill(b("BQ"), 0.0)
    fill(b("MK"), 1.0)
    fill(b("ONH"), 1.0)
    for n in set(SIGNS) - {0}: fill((T["CS%d" % n][:, :, :], [("CS%d" % n, 0, 1)]), 0.0)
    for p, (l0, l1) in enumerate(PARTS): fill(b("RB", rb(l0) + 16 * H, rb(l0) + 16 * H + 1), 0.0)
    fill(b("MK", 0, None, 16), 0.0, True)
    cp(b("RC"), b("KD"))
    fill((T.GE[:, :, :, 0], [("GE0", 0, K)]), 1.0)
    ts(b("IH"), b("TA"), 0.5 - 1.0 / 2048.0, op.mult)
    for n in set(SIGNS) - {0}: fill((T["CS%d" % n][:, :, 1:n + 1], [("CS%d" % n, 0, 1)]), 8 * VOTE, True)
    cp(b("BQ", 15, 144, 16), b("TB", 16, 25))
    for name, scale in (("ID", 1.0), ("ND", -1.0), ("I256", 256.0), ("IR", WHOLE)): ac(b(name), b("TA"), scale=scale)
    for name, scale in (("TN", -1.0), ("I16", H / 4096.0), ("I32", 32.0), ("IT", float(TOFF))): ts(b(name), b("TA"), scale, op.mult)
    for name, scale in (("BN", -VOTE), ("BV", 1024.0), ("BM", H / 2.0)): ac(b(name), b("BQ"), scale=scale)
    ac(b("ONB"), b("ONE"), scale=1.0 / 128.0)
    ac(b("GB"), b("TB", 16, 24))
    mm(b("UU", 0, 128, p1=8), b("GB"), b("ID"), True, True)
    ac(b("GA", p1=8), b("UU", 0, 128, p1=8))
    ts(b("R16"), b("RC"), 16.0, op.mult)
    ts(b("RN"), b("RC"), -1.0, op.mult, -0.5, op.add)
    cp(b("SU0", 0, first), b("STK", 0, first))
    ts(b("KF"), b("KI"), b("RC"), op.add)
    ts(b("LJ"), b("LI"), b("RC"), op.is_gt)
    ts(b("CAP"), b("CI"), b("R16"), op.add)
    ts(b("K16"), b("KF"), 16.0, op.mult)
    ts(b("KY"), b("KF", 0, 16), 5.0 * H, op.add)
    fill(b("LT", 0, 32), float(FAR))
    for t in range(ROUNDS):
        ts(b("LT", 32 * t + 32, 32 * t + 64), b("LJ"), float(DEAD - (t + 3) * FAR), op.mult, float(FAR), op.add)
    ts(b("KH"), b("K16", 0, 16), -1.0 - 8 * VOTE, op.add)
    for n in ("PW0", "PW1"): fill(b(n, K, TOFF), float(FAR))
    cp(b("LNB", p1=8), b("LN8", p1=8))
    mm(b("SA"), b("GA", p1=8), b("LNB", p1=8), True, True)
    run("A", lambda: g.scalar.activation(T.SG[:, :], T.SA[:, :], act.Sign, bias=T.RN[:, :]), b("SG"), [b("SA"), b("RN")])
    for n in ("VT1", "LX"): ac(b(n), b("SG"), act.Identity, scale=-FAR / 2.0, bias=DEAD - FAR / 2.0)
    fill((T.Y0[:, 16 * H:16 * H + YV], [("Y0f", 2, 3)]), FAR)

    def second(t, p):
        far(1, 1, 2 * H, LOW * H)
        for q in range(15 - LOW):
            dma("S", (T.Y1[q::16, LOW * H:(15 - q) * H], [("Y1", 4 * q + 2, 4 * q + 3)]), (T.D01[0:8 * (15 - LOW - q), :], [("D01", 0, H)]), "dY1", True)

    def coded():
        cp(b("WF"), b("WI"))
        tt(b("PW0", 0, K), b("CON"), b("VT1"), op.add)
        ts(b("BW"), b("BQ"), b("WF"), op.mult)
        ts(b("BA0"), b("BAS"), float(BASE), op.add)

    def names(t, p):
        mms(b("CC", *PARTS[p]), [(b("TA"), b("PW0", *PARTS[p])), (b("TN"), b("LX", *PARTS[p]))])

    def bases(t, n):
        send(b("BA0"), b("BA%d" % n), "BA%d" % n, ring(n))

    xall = b("X")

    def records(t, l0, l1, on="A"):
        (ac if on == "A" else cp)(b("RB", rb(l0), rb(l0) + 16 * (l1 - l0)), ind(xall, b("SU%d" % t, l0, l1)))

    def row(ci, i):
        a0 = rb(CHUNKS[ci][0])
        a1 = a0 + 16 * (CHUNKS[ci][1] - CHUNKS[ci][0])
        return (T.RB[:, a0 + i:a1:16], [("RB", a0, a1)])

    def slots(ci, s0, s1, r=None):
        l0, l1 = CHUNKS[ci]
        ap = T.GE[:, l0 // 16:l1 // 16, :, s0:s1] if r is None else T.GE[:, l0 // 16:l1 // 16, r, s0:s1]
        return (ap, [("GE%d" % s, l0, l1) for s in range(s0, s1)])

    signed = lambda t, ci: max([1] + [s1 for c, s0, s1 in BATCH[:USED[t]] if c == ci]) - 1

    def differences(t, i):
        if i >= USED[t]: return
        ci, s0, s1 = BATCH[i]
        l0, l1 = CHUNKS[ci]
        for s in range(s0, s1):
            mms(b("DD%d" % (i % 2), s - s0, (s1 - s0) * (l1 - l0), s1 - s0), [(b("ID"), row(ci, 16 - s)), (b("ND"), b("Z%d" % t, l0, l1))])

    def signs(t, i):
        if i >= USED[t]: return
        ci, s0, s1 = BATCH[i]
        l0, l1 = CHUNKS[ci]
        ac(slots(ci, s0, s1), b("DD%d" % (i % 2), 0, (s1 - s0) * (l1 - l0)), act.Sign, bias=0.5)

    def compare(t, ci):
        l0, l1 = CHUNKS[ci]
        for s in range(signed(t, ci) + 1, 16):
            tt((T.GE[:, l0 // 16:l1 // 16, :, s], [("GE%d" % s, l0, l1)]), row(ci, 16 - s), b("Z%d" % t, l0, l1), op.is_ge)
            yield 1

    def votes(t, ci):
        l0, l1 = CHUNKS[ci]
        p, n = l0 // H, signed(t, ci)
        level = [(b("ND"), (T["CS%d" % n][:, 0:(l1 - l0) // 16, :], [("CS%d" % n, 0, 1)]))] if n else []
        mms(b("VT%d" % p, l0 - p * H, l1 - p * H), level + [(b("BN", 15 - r, 143 - r), slots(ci, 0, 16, r)) for r in range(16)])

    def maxima(t, ci):
        l0, l1 = CHUNKS[ci]
        for k in range(l0, l1, FINE):
            scan(b("PM", 16 * k, 16 * (k + FINE)), b("MK"), b("RB", rb(k), rb(k) + 16 * FINE), op.mult, op.max)
            yield 1

    def sub(t, s):
        l0, l1 = SECTIONS[t][s] if s < len(SECTIONS[t]) else (K, K)
        p = min(l0 // H, 1)
        return l0, l1, p, l0 - p * H, l1 - p * H

    def ws(name, l0, l1):
        return b(TILE[name][0], TILE[name][1] + l0 // 16, TILE[name][1] + l1 // 16)

    def handler(t, s):
        l0, l1, p, a0, a1 = sub(t, s)
        if l0 == l1: return
        scan(b("OA", l0, l1), b("VT%d" % p, a0, a1), b("CAP", a0, a1), op.min, op.max)
        yield 1
        end = b("OA", l0 + 15, l1, 16)
        ts(ws("ml", l0, l1), end, 8 * VOTE, op.add)
        tt(ws("h", l0, l1), end, b("KH", a0 // 16, a1 // 16), op.subtract)
        yield 1

    def greatest(t, s):
        l0, l1, p, a0, a1 = sub(t, s)
        if l0 == l1: return
        (cp if s in ONV else ac)(b("ZM%d" % p, H + a0, H + a1), ind(b("PM", 16 * H * p, 16 * l1), ws("ml", l0, l1)))
        mms(b("UU", a0 // 16, a1 // 16), wrap("BW", "ZM%d" % p, H + a0, H + a1))

    def taken(t, p):
        l0, l1 = PARTS[p]
        src = ind(b("RB", rb(l0) + 1, rb(l0) + 16 * H + 1), w("ml", p))
        if p in ONA[t]:
            ac(b("AG"), src)
            mms(b("LS", 128, 144) if p else b("UU", 16, 32), wrap("BV", "AG", 0, H))
            mms(b("VT0", H, K), [(b("ID"), b("AG")), (b("ND"), b("Z%d" % t, l0, l1))])
            return ac(b("ZM%d" % p, 0, H), b("VT0", H, K))
        tt(b("ZM%d" % p, 0, H), src, b("Z%d" % t, l0, l1), op.subtract)
        mms(b("LS", 128, 144) if p else b("UU", 16, 32), [(b("TA"), w("zs", p))] + wrap("BV", "ZM%d" % p, 0, H))

    def level(t, p):
        if p in ONA[t]: return
        mms(b("UU", 32 + 16 * p, 48 + 16 * p), wrap("BV", "Z%d" % t, *PARTS[p]))
        cp(w("zs", p), b("UU", 32 + 16 * p, 48 + 16 * p))

    def sums(t, s):
        l0, l1, p, a0, a1 = sub(t, s)
        if l1 > l0: cp(b("UI", 32 * p + a0 // 16, 32 * p + a1 // 16 if p else 32), b("UU", a0 // 16, a1 // 16 if p else 32))

    def changed(t, s):
        l0, l1, p, a0, a1 = sub(t, s)
        if l0 == l1: return
        ts(ws("x15", l0, l1), b("UI", 32 * p + a0 // 16, 32 * p + a1 // 16), 15, op.bitwise_and)
        yield 1
        tt(ws("xk", l0, l1), ws("x15", l0, l1), b("K16", 0, (l1 - l0) // 16), op.add)
        yield 1
        cp(ws("xl", l0, l1), ws("xk", l0, l1))
        yield 1

    def lists(t, p):
        o, l0, l1 = 32 * p, PARTS[p][0], PARTS[p][1]
        u, v = b("UM", o, o + 16), b("UM", o + 16, o + 32)
        ts(w("un", p), w("h", p), 16.0, op.is_ge, 4096.0, op.mult)
        yield 1
        if p:
            cp(b("UI", 48, 64), b("LS", 128, 144))
            yield 1
        ts(b("UM", o, o + 32), b("UI", o, o + 32), 4095, op.bitwise_and)
        yield 1
        tt(w("pst", p), v, w("un", p), op.is_gt)
        ts(w("a", p), u, 32.0, op.add)
        yield 1
        mms(b("LS", 0, 16), [(b("ID"), b("KF", 0, 16)), (b("I16"), w("un", p))])
        mms(b("LS", 16, 32), [(b("ID"), w("h", p))] + [(b("I32"), w("pst", p))] * (t + 1))
        mms(b("LS", 32, 48), [(b("ID"), b("KF", 16 * p, 16 * p + 16)), (b("IT"), w("pst", p))])
        ts(w("w", p), w("pst", p), -float(NOP), op.mult, b("ACOL") if t else float(NOP), op.add)
        tt(w("n", p), u, w("a", p), op.mult)
        yield 1
        tt(w("n2", p), w("n", p), w("w", p), op.add)
        yield 1
        ts(w("j", p), w("n2", p), 5, op.arith_shift_right, 511 + (NOP >> 5), op.bitwise_and)
        cp(b("L3", 48 * p, 48 * p + 48), b("LS", 0, 48))
        yield 1
        ts(w("jl", p), w("j", p), float(K), op.min)
        yield 1

    def piece(t, p):
        l0, l1 = PARTS[p]
        tt(b("PB", l0, l1), ind(b("PW%d" % (t % 2), 0, TOFF), w("jl", p)), b("BA%d" % t, l0, l1), op.min)

    def mark(t, p):
        l0, l1 = PARTS[p]
        ac(b("ZO%d" % t, l0, l1), ind(b("ZM%d" % p), b("L3", 48 * p, 48 * p + 16)), act.Abs)
        if t < ROUNDS - 1: send(b("ZO%d" % t, l0, l1), b("Z%d" % (t + 1), l0, l1), "Z%d%d" % (t + 1, p), ring(1))
        else: dma("S", (T.yz[:, l0:l1], []), b("ZO%d" % t, l0, l1), "out")

    def lengths(t, p):
        l0, l1 = PARTS[p]
        ac(b("SG", l0, l1), ind(b("PW%d" % (t % 2), 0, TOFF), w("jl", p)) if DIRECT else b("PB", l0, l1), act.Sign)
        mms(b("LS", 64, 80), [(b("ID"), b("KY")), (b("I256"), w("h", p)), (b("ND"), w("un", p)), (b("I256"), w("pst", p))]
            + wrap("BM", "SG", l0, l1))

    def stack(t, p):
        l0, l1 = PARTS[p]
        sn = b("SN%d" % t, l0, l1)
        cp(w("yl", p), b("LS", 64, 80))
        yield 1
        tt(b("TY", l0, l1), ind(yall(p, 2 * H, 31 * H), w("yl", p)), b("PB", l0, l1), op.min)
        yield 1
        ts(sn, b("TY", l0, l1), 8191, op.bitwise_and)
        yield 1
        if t < ROUNDS - 1:
            if GCP: select(b("UO%d" % t, l0, l1), sn, [[0, H]], op.is_ge, 0.0, 0, 0)
            else: cp(b("UO%d" % t, l0, l1), sn)
            send(b("UO%d" % t, l0, l1), b("SU%d" % (t + 1), l0, l1), "SU%d%d" % (t + 1, p), ring(1))
            send(sn, b("D%d%d" % (t + 1, p)), "D%d%d" % (t + 1, p), ring(1))
        else:
            cp(b("FO", l0, l1), sn)
            dma("S", (T.ys[:, l0:l1], []), b("FO", l0, l1), "out")
        yield 1

    def stored(t, p):
        l0, l1 = PARTS[p]
        new = b("PW%d" % (t % 2), TOFF + l0, TOFF + l1)
        tt(new, ind(b("LT"), b("L3", 48 * p + 16, 48 * p + 32)), yall(p, 15 * H, 16 * H) if t and NOST else b("ST%d" % t if t else "STK", l0, l1), op.add)
        yield 1
        tt(b("CC", l0, l1) if t < ROUNDS - 1 else b("CI32", l0, l1), new, b("CC", l0, l1), op.min)
        yield 1
        if t == ROUNDS - 1:
            ts(b("CN", l0, l1), b("CI32", l0, l1), 8191, op.bitwise_and)
            yield 1
            cp(b("FC", l0, l1), b("CN", l0, l1))
            dma("S", (T.yc[:, l0:l1], []), b("FC", l0, l1), "out")
            yield 1

    def pieces(t, p):
        l0, l1 = PARTS[p]
        src = ind(b("PW%d" % (t % 2)), b("L3", 48 * p + 32, 48 * p + 48))
        if t < ROUNDS - 1: ac(b("PW%d" % ((t + 1) % 2), l0, l1), src)
        else:
            ac(b("SF", l0, l1), src, act.Sign)
            mms(b("SA", H, 2 * H, p1=8), [(b("GB"), b("SF", l0, l1))])
            ac(b("FN", l0, l1, p1=8), b("SA", H, 2 * H, p1=8), act.Identity, bias=8.0, scale=-0.5)
            dma("S", (T.yn[:, l0:l1], []), b("FN", l0, l1, p1=8), "out")

    def old(t, s):
        l0, l1, p, a0, a1 = sub(t, s)
        if l0 == l1: return
        src, m = ind(b("X", 16 * l0, 16 * l1), ws("xl", l0, l1)), b("ZM%d" % p, H + a0, H + a1)
        if s in ONV: return tt(b("XS", 0, l1 - l0), src, m, op.add)
        ac(b("OX", l0, l1), src)
        mms(b("SA", l0, l1), [(b("IH"), m), (b("IH"), b("OX", l0, l1)), (b("IR"), b("ONH", 0, l1 - l0))])

    def halves(t, s):
        l0, l1, p, a0, a1 = sub(t, s)
        if l0 == l1: return
        if s in ONV: ts(b("XH", 0, l1 - l0), b("XS", 0, l1 - l0), 1, op.arith_shift_right)
        else: ac(b("NB", l0, l1), b("SA", l0, l1), act.Identity, bias=-WHOLE)

    def written(t, s):
        l0, l1, p, a0, a1 = sub(t, s)
        if l1 > l0: cp(scattered(b("X", 16 * l0, 16 * l1), ws("xl", l0, l1)), b("XH", 0, l1 - l0) if s in ONV else b("NB", l0, l1))

    def unhandled():
        mm(b("LS", 96, 128), b("ONB"), w("un"), True, True)
        ac(b("AJ"), b("LS", 96, 128), act.Identity, total_in=b("ACOL"), bias=NOP / 32.0)

    def gather(t, ci):
        l0, l1 = CHUNKS[ci]
        c, s0, s1 = SHARE[t]
        for a0, a1 in ((l0, s0), (s1, l1)) if ci == c else ((l0, l1),):
            if a1 > a0: records(t, a0, a1)

    def share(t, ci):
        if SHARE[t][2] > SHARE[t][1]: records(t, *SHARE[t][1:], "V")

    steps = {"r": gather, "R": share, "i": shifts, "y": level, "d": differences, "s": signs, "c": compare, "v": votes, "m": maxima,
             "h": handler, "g": greatest, "t": taken, "u": sums, "l": lists, "p": piece, "n": lengths, "z": mark,
             "k": stack, "e": stored, "q": pieces}
    inner = {"x": changed, "o": old, "f": halves, "N": lambda t, p: unhandled(),
             "w": written}

    once = {"C": lambda t, p: coded(), "j": names, "B": bases, "Y": second, "U": lambda t, p: cp(b("SU0", first, K), b("STK", first, K))}

    table = {**steps, **inner, **once}
    for t, order in enumerate((FIRST, ORDER, LAST)):
        for word in order.split():
            key = (word[0], t - word.count("'") + word.count("^"), int(word[1]))
            if key not in calls:
                step[0] = key
                calls[key] = []
                for _ in table[key[0]](*key[1:]) or (): pass
            n = word[2:].strip("'^")
            for _ in range(int(n[1:]) if n[1:] else 1 if n else len(calls[key])): calls[key].pop(0)()
    assert not any(calls.values())

    for s in SEMAPHORES:
        if total[s]: g.wait_ge(T.sem[s], total[s])
